import numpy as np
import ml_dtypes


def mxq(x, axis, fmt="e4m3"):
    dtype, down = {"e4m3": (ml_dtypes.float8_e4m3fn, 7), "e5m2": (ml_dtypes.float8_e5m2, 14)}[fmt]
    v = np.moveaxis(np.asarray(x, np.float32).astype(ml_dtypes.bfloat16).astype(np.float64), axis, -1)
    blocks = v.reshape(v.shape[:-1] + (-1, 32))
    amax = np.abs(blocks).max(-1, keepdims=True)
    byte = np.maximum(np.where(amax > 0, np.frexp(amax)[1] - 1 + 127, 0) - down, 1)
    scale = np.exp2(byte - 127.0)
    codes = (blocks / scale).astype(np.float32).astype(dtype).astype(np.float64)
    return np.moveaxis((codes * scale).reshape(v.shape), -1, axis)


WIDE = False


def mx_kscale(k):
    if not WIDE:
        return np.ones(k)
    levels = np.array([10, -10, 5, -5, 0])
    if k % 512:
        return np.exp2(np.random.permutation(np.resize(levels, k // 32))).repeat(32)
    a = np.empty((k // 512, 16))
    for p in range(k // 512):
        a[p, :8] = np.random.permutation(np.resize(levels, 8))
        for g in range(8):
            far = levels[np.abs(levels - a[p, g]) >= 10]
            a[p, g + 8] = far[np.random.randint(len(far))]
    return np.exp2(a.ravel()).repeat(32)


def f64(x):
    return np.asarray(x).astype(np.float64)


def striped(idx):
    return np.tile(idx.reshape(-1, 16).T, (8, 1)).astype(np.uint16)


def unstriped(offs):
    return offs[:16].T.reshape(-1).astype(np.int64)


E2M1 = np.array([0.0, 0.5, 1.0, 1.5, 2.0, 3.0, 4.0, 6.0, -0.0, -0.5, -1.0, -1.5, -2.0, -3.0, -4.0, -6.0])


def pack_weight(w, fmt):
    k, n = w.shape
    w = f64(np.asarray(w, np.float32).astype(ml_dtypes.bfloat16)).reshape(k // 32, 32, n)
    amax = np.abs(w).max(1)
    if fmt == "e4m3":
        byte = np.frexp(amax)[1] - 1 + 127 - 7
    else:
        mant, ex = np.frexp(amax / 6.0)
        byte = np.where(mant > 0.5, ex, ex - 1) + 127
    byte = np.clip(np.where(amax > 0, byte, 1), 1, 254)
    scaled = (w * np.exp2(127.0 - byte)[:, None, :]).reshape(k, n).astype(np.float32)
    by_word = np.ascontiguousarray(scaled.reshape(k // 512, 128, 4, n).transpose(0, 1, 3, 2))
    if fmt == "e4m3":
        words = by_word.astype(ml_dtypes.float8_e4m3fn).view(np.uint8)
    else:
        c = by_word.astype(ml_dtypes.float4_e2m1fn).view(np.uint8) & 0xF
        words = (c[..., 0::2] | (c[..., 1::2] << 4)).reshape(k // 512, 128, 2 * n)
    return np.ascontiguousarray(words), np.ascontiguousarray(byte.astype(np.uint8).reshape(k // 512, 16, n))


def unpack_weight(words, scales, fmt):
    g, _, n = scales.shape
    words = np.ascontiguousarray(words).reshape(g, 128, n, -1)
    if fmt == "e4m3":
        vals = words.view(ml_dtypes.float8_e4m3fn).astype(np.float64)
    else:
        nib = np.empty((g, 128, n, 4), np.uint8)
        nib[..., 0::2] = words & 0xF
        nib[..., 1::2] = words >> 4
        vals = E2M1[nib]
    vals = vals * np.repeat(np.exp2(scales.astype(np.float64) - 127.0), 8, axis=1)[..., None]
    return vals.transpose(0, 1, 3, 2).reshape(g * 512, n)


def gelu(v):
    return 0.5 * v * (1.0 + np.tanh(np.sqrt(2.0 / np.pi) * (v + 0.044715 * v**3)))


K, T, S, P, H, N = 1024, 4096, 1024, 512, 1536, 256

def setup_inputs():
    n = np.random.standard_normal
    s = mx_kscale(K)[:, None]
    u = mx_kscale(H)[:, None]
    tab_words, tab_scales = pack_weight(n((K, T)) * s, "e4m3")
    w1_words, w1_scales = pack_weight(n((K, H)) / np.sqrt(K) / s * u.T, "e2m1")
    return {
        "tab_words": tab_words, "tab_scales": tab_scales,
        "offs": striped(np.random.permutation(T)[:S]),
        "w1_words": w1_words, "w1_scales": w1_scales,
        "pos1": striped(np.random.permutation(S)[:P]),
        "pos2": striped(np.random.permutation(S)[:P]),
        "w2": (n((H, N)) / np.sqrt(H) / u).astype(np.float32),
        "rew": (0.5 * n((N, P))).astype(np.float32),
    }

def reference(tab_words, tab_scales, offs, w1_words, w1_scales, pos1, pos2, w2, rew):
    v = unpack_weight(tab_words, tab_scales, "e4m3")[:, unstriped(offs)]
    w1 = unpack_weight(w1_words, w1_scales, "e2m1")
    h = np.maximum(w1.T @ v, 0.0)
    a = h[:, unstriped(pos1)]
    b = h[:, unstriped(pos2)]
    z = a - 0.99 * b
    d = mxq(w2, 0, "e4m3").T @ mxq(z, 0, "e4m3")
    return np.tanh(f64(rew) - d)

@@ -1,0 +1,240 @@
+from contextlib import ExitStack
+
+import concourse.mybir as mybir
+
+K, T, S, PAIRS, H, N = 1024, 4096, 1024, 512, 1536, 256
+FLOPS = 2 * K * H * S + 2 * H * N * PAIRS
+
+F32 = mybir.dt.float32
+BF16 = mybir.dt.bfloat16
+I32 = mybir.dt.int32
+U32 = mybir.dt.uint32
+U16 = mybir.dt.uint16
+U8 = mybir.dt.uint8
+FP8X4 = mybir.dt.float8_e4m3fn_x4
+FP4X4 = mybir.dt.float4_e2m1fn_x4
+ACT = mybir.ActivationFunctionType
+ALU = mybir.AluOpType
+
+P = 128
+PASSES = K // 512
+GROUPS = H // 512
+BANK = 512
+DISCOUNT = 0.99
+
+
+def interleaved(dst, src):
+    return (
+        dst.rearrange("p (c i) t -> p c t i", i=2),
+        src.rearrange("p t (c i) -> p c t i", i=2),
+    )
+
+
+def tile_list_replay_td_errors_kernel(
+    tc, tab_words, tab_scales, offs, w1_words, w1_scales, pos1, pos2, w2, rew, out
+):
+    nc = tc.nc
+    with ExitStack() as ctx:
+        lists = ctx.enter_context(tc.tile_pool(name="lists", bufs=1))
+        keep = ctx.enter_context(tc.tile_pool(name="keep", bufs=1))
+        shared = ctx.enter_context(tc.tile_pool(name="shared", bufs=1))
+        ring = ctx.enter_context(tc.tile_pool(name="ring", bufs=2))
+        psum = ctx.enter_context(tc.psum_pool(name="psum", bufs=8))
+
+        idx = lists.tile([P, S // 16], U16, name="idx")
+        p1 = lists.tile([P, PAIRS // 16], U16, name="p1")
+        p2 = lists.tile([P, PAIRS // 16], U16, name="p2")
+
+        seed_in = keep.tile([P, 16], F32, name="seed_in", tag="seed_table", align_bytes=64)
+        nc.vector.memset(seed_in[:], 1.0)
+        seed = keep.tile([P, 16], F32, name="seed")
+        nc.scalar.activation(out=seed[:], in_=seed_in[:], func=ACT.Relu, scale=DISCOUNT)
+
+        nc.sync.dma_start(idx[:], offs)
+        nc.sync.dma_start(p1[:], pos1)
+        nc.sync.dma_start(p2[:], pos2)
+        w1w_hbm = w1_words.rearrange("a p c -> p a c").bitcast(I32)
+        w1w_first = keep.tile([P, PASSES, 256], I32, name="w1w_first", align_bytes=64)
+        nc.sync.dma_start(out=w1w_first[:], in_=w1w_hbm[:, :, 0:256])
+        table0 = keep.tile([P, T], I32, name="table0", align_bytes=64)
+        nc.sync.dma_start(out=table0[:], in_=tab_words[0].rearrange("p t i -> p (t i)").bitcast(I32))
+
+        w1s_raw = keep.tile([P, PASSES, H // 4], I32, name="w1s_raw", align_bytes=64)
+        nc.vector.memset(w1s_raw[:], 0)
+        w1s_hbm = w1_scales.rearrange("a q c -> q a c").bitcast(I32)
+        for quad in range(4):
+            nc.sync.dma_start(
+                out=w1s_raw[32 * quad : 32 * quad + 4, :, :], in_=w1s_hbm[4 * quad : 4 * quad + 4, :, :]
+            )
+        ts_win = shared.tile([P, PASSES, T // 4], I32, name="ts_win", offset=15 * 1024)
+        nc.vector.memset(ts_win[:], 0)
+        nc.scalar.dma_start(
+            out=ts_win[4:P:8, :, :], in_=tab_scales.rearrange("a q t -> q a t").bitcast(I32)
+        )
+        table1 = keep.tile([P, T], I32, name="table1", tag="seed_table", align_bytes=64)
+        nc.sync.dma_start(out=table1[:], in_=tab_words[1].rearrange("p t i -> p (t i)").bitcast(I32))
+        table = [table0, table1]
+
+        v_scales = keep.tile([P, PASSES, S // 4], I32, name="v_scales", align_bytes=64)
+        nc.vector.memset(v_scales[:], 0)
+        discount = keep.tile([P, PAIRS], F32, name="discount")
+        nc.vector.tensor_copy(
+            out=discount[:].rearrange("p (x s) -> p x s", s=16),
+            in_=seed[:].unsqueeze(1).to_broadcast([P, PAIRS // 16, 16]),
+        )
+
+        ts_picked = keep.tile([P, PASSES, S], U8, name="ts_picked", align_bytes=64)
+        for a in range(PASSES):
+            nc.vector.tensor_copy(ts_picked[:, a, :], ts_win[:, a, :].bitcast(U8).indirect(idx[:]))
+        for quad in range(4):
+            nc.scalar.dma_start(
+                out=v_scales[32 * quad : 32 * quad + 4, :, :],
+                in_=ts_picked[32 * quad + 4 : 32 * quad + 32 : 8, :, :].bitcast(I32),
+            )
+
+        w1w_rest = shared.tile([P, PASSES, 512], I32, name="w1w_rest", offset=16 * 1024)
+        nc.sync.dma_start(out=w1w_rest[:], in_=w1w_hbm[:, :, 256:768])
+        late = shared.tile([P, 16, N], F32, name="late", offset=0)
+        for c in range(GROUPS):
+            rows = w2[512 * c : 512 * (c + 1), :].rearrange("(b t u) n -> t b u n", t=4, u=8)
+            for t in range(4):
+                nc.sync.dma_start(out=late[:, 4 * c + t, :], in_=rows[t])
+        rew_sb = late[:, 12:16, :].rearrange("p (m x) n -> p m (x n)", m=2)
+        nc.sync.dma_start(out=rew_sb, in_=rew.rearrange("(m p) j -> p m j", p=P))
+
+        w1w = keep.tile([P, GROUPS, PASSES, 256], I32, name="w1w", align_bytes=64)
+        w1s = keep.tile([P, GROUPS, PASSES, 128], I32, name="w1s", align_bytes=64)
+
+        def permute_w1(c):
+            for a in range(PASSES):
+                src = w1w_first[:, a, :] if c == 0 else w1w_rest[:, a, 256 * (c - 1) : 256 * c]
+                nc.vector.tensor_copy(
+                    out=w1w[:, c, a, :].rearrange("p (t b w) -> p t b w", t=4, w=4),
+                    in_=src.rearrange("p (b t w) -> p t b w", t=4, w=4),
+                )
+                nc.vector.tensor_copy(
+                    out=w1s[:, c, a, :].rearrange("p (t b w) -> p t b w", t=4, w=2),
+                    in_=w1s_raw[:, a, 128 * c : 128 * (c + 1)].rearrange("p (b t w) -> p t b w", t=4, w=2),
+                )
+
+        permute_w1(0)
+        v_words = shared.tile([P, PASSES, S], U32, name="v_words", offset=20 * 1024, align_bytes=64)
+        nc.vector.tensor_copy(v_words[:, 0, :], table[0][:].bitcast(U32).indirect(idx[:]))
+        for half in range(2):
+            nc.vector.tensor_copy(
+                v_words[:, 1, BANK * half : BANK * (half + 1)],
+                table[1][:].bitcast(U32).indirect(idx[:, 32 * half : 32 * (half + 1)]),
+            )
+        permute_w1(1)
+        permute_w1(2)
+
+        def hidden_tile(c, t):
+            h = keep.tile([P, S], F32, name="h%d_%d" % (c, t))
+            for half in range(2):
+                cols = slice(BANK * half, BANK * (half + 1))
+                acc = psum.tile([P, BANK], F32, name="acc", tag="bank")
+                for a in range(PASSES):
+                    nc.tensor.matmul_mx(
+                        out=acc[:],
+                        lhsT=w1w[:, c, a, 64 * t : 64 * (t + 1)].bitcast(U8).bitcast(FP4X4),
+                        lhsT_scale=w1s[:, c, a, 32 * t : 32 * (t + 1)].bitcast(U8),
+                        rhs=v_words[:, a, cols].bitcast(FP8X4),
+                        rhs_scale=v_scales[:, a, :].bitcast(U8)[:, cols],
+                        start=(a == 0),
+                        stop=(a == PASSES - 1),
+                    )
+                nc.scalar.activation(out=h[:, cols], in_=acc[:], func=ACT.Relu)
+            return h
+
+        w2_codes = keep.tile([P, GROUPS, N], U32, name="w2_codes", align_bytes=64)
+        w2_scales = keep.tile([P, GROUPS, N], U8, name="w2_scales", align_bytes=64)
+        w2_bf = keep.tile([P, GROUPS, N, 4], BF16, name="w2_bf", align_bytes=64)
+
+        def round_w2(c):
+            dst, src = interleaved(w2_bf[:, c, :, :], late[:, 4 * c : 4 * (c + 1), :])
+            nc.scalar.activation(out=dst, in_=src, func=ACT.Copy)
+
+        def quantize_w2(c):
+            nc.vector.quantize_mx(
+                out=w2_codes[:, c, :].bitcast(FP8X4),
+                scales=w2_scales[:, c, :],
+                in_=w2_bf[:, c, :, :].rearrange("p n t -> p (n t)"),
+            )
+
+        hs = []
+        for c in range(GROUPS):
+            for t in range(4):
+                hs.append(hidden_tile(c, t))
+            round_w2(c)
+
+        z_codes = keep.tile([P, GROUPS, PAIRS], U32, name="z_codes", align_bytes=64)
+        z_scales = keep.tile([P, GROUPS, PAIRS], U8, name="z_scales", align_bytes=64)
+
+        def pick(c, j0, j1):
+            state = ring.tile([P, 4, j1 - j0], F32, name="state")
+            succ = ring.tile([P, 4, j1 - j0], F32, name="succ")
+            for t in range(4):
+                h = hs[4 * c + t]
+                nc.vector.tensor_copy(state[:, t, :], h[:].indirect(p1[:, j0 // 16 : j1 // 16]))
+                nc.vector.tensor_tensor(
+                    succ[:, t, :], h[:].indirect(p2[:, j0 // 16 : j1 // 16]), discount[:, j0:j1], ALU.mult
+                )
+            return state, succ
+
+        def difference(state, succ, width):
+            z = ring.tile([P, width, 4], BF16, name="z", align_bytes=64)
+            dst, in0 = interleaved(z[:], state[:])
+            dst, in1 = interleaved(z[:], succ[:])
+            nc.vector.tensor_tensor(out=dst, in0=in0, in1=in1, op=ALU.subtract)
+            return z
+
+        def quantize_z(c, z, z0, j0, j1):
+            nc.vector.quantize_mx(
+                out=z_codes[:, c, j0:j1].bitcast(FP8X4),
+                scales=z_scales[:, c, j0:j1],
+                in_=z[:, j0 - z0 : j1 - z0, :].rearrange("p j t -> p (j t)"),
+            )
+
+        out_v = out.rearrange("(m p) j -> p m j", p=P)
+
+        def heads(j0, j1):
+            width = j1 - j0
+            err = ring.tile([P, 2, width], F32, name="err", bufs=3)
+            res = ring.tile([P, 2, width], F32, name="res", bufs=3)
+            for m in range(2):
+                acc = psum.tile([P, width], F32, name="acc_d", tag="bank")
+                for c in range(GROUPS):
+                    nc.tensor.matmul_mx(
+                        out=acc[:],
+                        lhsT=w2_codes[:, c, P * m : P * (m + 1)].bitcast(FP8X4),
+                        lhsT_scale=w2_scales[:, c, P * m : P * (m + 1)],
+                        rhs=z_codes[:, c, j0:j1].bitcast(FP8X4),
+                        rhs_scale=z_scales[:, c, j0:j1],
+                        start=(c == 0),
+                        stop=(c == GROUPS - 1),
+                    )
+                nc.vector.tensor_tensor(out=err[:, m, :], in0=rew_sb[:, m, j0:j1], in1=acc[:], op=ALU.subtract)
+            nc.scalar.activation(out=res[:], in_=err[:], func=ACT.Tanh)
+            nc.sync.dma_start(out=out_v[:, :, j0:j1], in_=res[:])
+
+        zs = None
+        for c in range(GROUPS - 1):
+            state, succ = pick(c, 0, PAIRS)
+            if zs is not None:
+                quantize_z(*zs)
+            z = difference(state, succ, PAIRS)
+            quantize_w2(c)
+            zs = (c, z, 0, 0, PAIRS)
+        last = GROUPS - 1
+        state, succ = pick(last, 0, 384)
+        quantize_z(*zs)
+        z = difference(state, succ, 384)
+        quantize_w2(last)
+        quantize_z(last, z, 0, 0, 256)
+        quantize_z(last, z, 0, 256, 384)
+        state, succ = pick(last, 384, PAIRS)
+        heads(0, 256)
+        heads(256, 384)
+        z = difference(state, succ, 128)
+        quantize_z(last, z, 384, 384, PAIRS)
+        heads(384, PAIRS)

@@ -45,10 +45,10 @@ def tile_list_replay_td_errors_kernel(
         p1 = lists.tile([P, PAIRS // 16], U16, name="p1")
         p2 = lists.tile([P, PAIRS // 16], U16, name="p2")
 
-        seed_in = keep.tile([P, 16], F32, name="seed_in", tag="seed_table", align_bytes=64)
+        seed_in = keep.tile([P, 1], F32, name="seed_in", tag="seed_table", align_bytes=64)
         nc.vector.memset(seed_in[:], 1.0)
-        seed = keep.tile([P, 16], F32, name="seed")
-        nc.scalar.activation(out=seed[:], in_=seed_in[:], func=ACT.Relu, scale=DISCOUNT)
+        discount = keep.tile([P, 1], F32, name="discount")
+        nc.scalar.activation(out=discount[:], in_=seed_in[:], func=ACT.Relu, scale=DISCOUNT)
 
         nc.sync.dma_start(idx[:], offs)
         nc.sync.dma_start(p1[:], pos1)
@@ -59,14 +59,14 @@ def tile_list_replay_td_errors_kernel(
         table0 = keep.tile([P, T], I32, name="table0", align_bytes=64)
         nc.sync.dma_start(out=table0[:], in_=tab_words[0].rearrange("p t i -> p (t i)").bitcast(I32))
 
-        w1s_raw = keep.tile([P, PASSES, H // 4], I32, name="w1s_raw", align_bytes=64)
-        nc.vector.memset(w1s_raw[:], 0)
         w1s_hbm = w1_scales.rearrange("a q c -> q a c").bitcast(I32)
+        w1s_first = keep.tile([P, PASSES, 128], I32, name="w1s_first", align_bytes=64)
+        nc.vector.memset(w1s_first[:], 0)
         for quad in range(4):
             nc.sync.dma_start(
-                out=w1s_raw[32 * quad : 32 * quad + 4, :, :], in_=w1s_hbm[4 * quad : 4 * quad + 4, :, :]
+                out=w1s_first[32 * quad : 32 * quad + 4, :, :], in_=w1s_hbm[4 * quad : 4 * quad + 4, :, 0:128]
             )
-        ts_win = shared.tile([P, PASSES, T // 4], I32, name="ts_win", offset=15 * 1024)
+        ts_win = keep.tile([P, PASSES, T // 4], I32, name="ts_win", tag="win_words", align_bytes=64)
         nc.vector.memset(ts_win[:], 0)
         nc.scalar.dma_start(
             out=ts_win[4:P:8, :, :], in_=tab_scales.rearrange("a q t -> q a t").bitcast(I32)
@@ -77,13 +77,8 @@ def tile_list_replay_td_errors_kernel(
 
         v_scales = keep.tile([P, PASSES, S // 4], I32, name="v_scales", align_bytes=64)
         nc.vector.memset(v_scales[:], 0)
-        discount = keep.tile([P, PAIRS], F32, name="discount")
-        nc.vector.tensor_copy(
-            out=discount[:].rearrange("p (x s) -> p x s", s=16),
-            in_=seed[:].unsqueeze(1).to_broadcast([P, PAIRS // 16, 16]),
-        )
 
-        ts_picked = keep.tile([P, PASSES, S], U8, name="ts_picked", align_bytes=64)
+        ts_picked = shared.tile([P, PASSES, S], U8, name="ts_picked", offset=15 * 1024)
         for a in range(PASSES):
             nc.vector.tensor_copy(ts_picked[:, a, :], ts_win[:, a, :].bitcast(U8).indirect(idx[:]))
         for quad in range(4):
@@ -92,8 +87,15 @@ def tile_list_replay_td_errors_kernel(
                 in_=ts_picked[32 * quad + 4 : 32 * quad + 32 : 8, :, :].bitcast(I32),
             )
 
-        w1w_rest = shared.tile([P, PASSES, 512], I32, name="w1w_rest", offset=16 * 1024)
-        nc.sync.dma_start(out=w1w_rest[:], in_=w1w_hbm[:, :, 256:768])
+        w1_rest = shared.tile([P, PASSES, 768], I32, name="w1_rest", offset=16 * 1024)
+        w1w_rest = w1_rest[:, :, 0:512]
+        w1s_rest = w1_rest[:, :, 512:768]
+        nc.gpsimd.memset(w1s_rest, 0)
+        nc.sync.dma_start(out=w1w_rest, in_=w1w_hbm[:, :, 256:768])
+        for quad in range(4):
+            nc.sync.dma_start(
+                out=w1s_rest[32 * quad : 32 * quad + 4, :, :], in_=w1s_hbm[4 * quad : 4 * quad + 4, :, 128:384]
+            )
         late = shared.tile([P, 16, N], F32, name="late", offset=0)
         for c in range(GROUPS):
             rows = w2[512 * c : 512 * (c + 1), :].rearrange("(b t u) n -> t b u n", t=4, u=8)
@@ -112,13 +114,14 @@ def tile_list_replay_td_errors_kernel(
                     out=w1w[:, c, a, :].rearrange("p (t b w) -> p t b w", t=4, w=4),
                     in_=src.rearrange("p (b t w) -> p t b w", t=4, w=4),
                 )
+                src = w1s_first[:, a, :] if c == 0 else w1s_rest[:, a, 128 * (c - 1) : 128 * c]
                 nc.vector.tensor_copy(
                     out=w1s[:, c, a, :].rearrange("p (t b w) -> p t b w", t=4, w=2),
-                    in_=w1s_raw[:, a, 128 * c : 128 * (c + 1)].rearrange("p (b t w) -> p t b w", t=4, w=2),
+                    in_=src.rearrange("p (b t w) -> p t b w", t=4, w=2),
                 )
 
         permute_w1(0)
-        v_words = shared.tile([P, PASSES, S], U32, name="v_words", offset=20 * 1024, align_bytes=64)
+        v_words = keep.tile([P, PASSES, S], U32, name="v_words", tag="win_words", align_bytes=64)
         nc.vector.tensor_copy(v_words[:, 0, :], table[0][:].bitcast(U32).indirect(idx[:]))
         for half in range(2):
             nc.vector.tensor_copy(
@@ -161,31 +164,43 @@ def tile_list_replay_td_errors_kernel(
                 in_=w2_bf[:, c, :, :].rearrange("p n t -> p (n t)"),
             )
 
-        hs = []
-        for c in range(GROUPS):
+        hs = {}
+
+        def hidden_group(c):
             for t in range(4):
-                hs.append(hidden_tile(c, t))
-            round_w2(c)
+                hs[c, t] = hidden_tile(c, t)
 
         z_codes = keep.tile([P, GROUPS, PAIRS], U32, name="z_codes", align_bytes=64)
         z_scales = keep.tile([P, GROUPS, PAIRS], U8, name="z_scales", align_bytes=64)
 
-        def pick(c, j0, j1):
-            state = ring.tile([P, 4, j1 - j0], F32, name="state")
-            succ = ring.tile([P, 4, j1 - j0], F32, name="succ")
-            for t in range(4):
-                h = hs[4 * c + t]
-                nc.vector.tensor_copy(state[:, t, :], h[:].indirect(p1[:, j0 // 16 : j1 // 16]))
-                nc.vector.tensor_tensor(
-                    succ[:, t, :], h[:].indirect(p2[:, j0 // 16 : j1 // 16]), discount[:, j0:j1], ALU.mult
-                )
-            return state, succ
+        def pick_tiles(c, j0, j1):
+            state = ring.tile([P, 4, j1 - j0], F32, name="state", bufs=3)
+            succ = ring.tile([P, 4, j1 - j0], F32, name="succ", bufs=3)
+            return c, j0, j1, state, succ
 
-        def difference(state, succ, width):
-            z = ring.tile([P, width, 4], BF16, name="z", align_bytes=64)
-            dst, in0 = interleaved(z[:], state[:])
-            dst, in1 = interleaved(z[:], succ[:])
-            nc.vector.tensor_tensor(out=dst, in0=in0, in1=in1, op=ALU.subtract)
+        def pick_succ(part, t):
+            c, j0, j1, state, succ = part
+            nc.vector.tensor_copy(succ[:, t, :], hs[c, t][:].indirect(p2[:, j0 // 16 : j1 // 16]))
+            nc.scalar.activation(out=succ[:, t, :], in_=succ[:, t, :], func=ACT.Copy, scale=discount[:])
+
+        def pick_state(part, t):
+            c, j0, j1, state, succ = part
+            nc.vector.tensor_copy(state[:, t, :], hs[c, t][:].indirect(p1[:, j0 // 16 : j1 // 16]))
+
+        def difference(part, on_gpsimd):
+            c, j0, j1, state, succ = part
+            z = ring.tile([P, j1 - j0, 4], BF16, name="z", align_bytes=64)
+            if on_gpsimd:
+                nc.gpsimd.tensor_tensor(
+                    out=z[:],
+                    in0=state[:].rearrange("p t j -> p j t"),
+                    in1=succ[:].rearrange("p t j -> p j t"),
+                    op=ALU.subtract,
+                )
+            else:
+                dst, in0 = interleaved(z[:], state[:])
+                dst, in1 = interleaved(z[:], succ[:])
+                nc.vector.tensor_tensor(out=dst, in0=in0, in1=in1, op=ALU.subtract)
             return z
 
         def quantize_z(c, z, z0, j0, j1):
@@ -217,24 +232,45 @@ def tile_list_replay_td_errors_kernel(
             nc.scalar.activation(out=res[:], in_=err[:], func=ACT.Tanh)
             nc.sync.dma_start(out=out_v[:, :, j0:j1], in_=res[:])
 
-        zs = None
-        for c in range(GROUPS - 1):
-            state, succ = pick(c, 0, PAIRS)
-            if zs is not None:
-                quantize_z(*zs)
-            z = difference(state, succ, PAIRS)
-            quantize_w2(c)
-            zs = (c, z, 0, 0, PAIRS)
+        hidden_group(0)
+        hidden_group(1)
+        part0 = pick_tiles(0, 0, PAIRS)
+        for t in range(4):
+            pick_succ(part0, t)
+            pick_state(part0, t)
+        z0 = difference(part0, True)
+        hidden_group(2)
+        for c in range(GROUPS):
+            round_w2(c)
+
+        part1 = pick_tiles(1, 0, PAIRS)
+        for t in range(4):
+            if t == 3:
+                quantize_z(0, z0, 0, 0, PAIRS)
+                for c in range(GROUPS):
+                    quantize_w2(c)
+            pick_succ(part1, t)
+            pick_state(part1, t)
+        z1 = difference(part1, True)
+
         last = GROUPS - 1
-        state, succ = pick(last, 0, 384)
-        quantize_z(*zs)
-        z = difference(state, succ, 384)
-        quantize_w2(last)
+        part2 = pick_tiles(last, 0, 384)
+        for t in range(4):
+            pick_succ(part2, t)
+        for t in range(4):
+            pick_state(part2, t)
+        quantize_z(1, z1, 0, 0, PAIRS)
+        z = difference(part2, False)
+        part3 = pick_tiles(last, 384, PAIRS)
+        pick_succ(part3, 0)
         quantize_z(last, z, 0, 0, 256)
         quantize_z(last, z, 0, 256, 384)
-        state, succ = pick(last, 384, PAIRS)
+        for t in range(1, 4):
+            pick_succ(part3, t)
+        for t in range(4):
+            pick_state(part3, t)
         heads(0, 256)
         heads(256, 384)
-        z = difference(state, succ, 128)
+        z = difference(part3, False)
         quantize_z(last, z, 384, 384, PAIRS)
         heads(384, PAIRS)

@@ -45,11 +45,10 @@ def tile_list_replay_td_errors_kernel(
         p1 = lists.tile([P, PAIRS // 16], U16, name="p1")
         p2 = lists.tile([P, PAIRS // 16], U16, name="p2")
 
-        seed_in = keep.tile([P, 1], F32, name="seed_in", tag="seed_table", align_bytes=64)
-        nc.vector.memset(seed_in[:], 1.0)
-        discount = keep.tile([P, 1], F32, name="discount")
-        nc.scalar.activation(out=discount[:], in_=seed_in[:], func=ACT.Relu, scale=DISCOUNT)
-
+        ts_win = keep.tile([P, T // 4], I32, name="ts_win", tag="win_table", align_bytes=64)
+        nc.sync.dma_start(
+            out=ts_win[96:P, :], in_=tab_scales.rearrange("a q t -> (a q) t").bitcast(I32)
+        )
         nc.sync.dma_start(idx[:], offs)
         nc.sync.dma_start(p1[:], pos1)
         nc.sync.dma_start(p2[:], pos2)
@@ -59,43 +58,40 @@ def tile_list_replay_td_errors_kernel(
         table0 = keep.tile([P, T], I32, name="table0", align_bytes=64)
         nc.sync.dma_start(out=table0[:], in_=tab_words[0].rearrange("p t i -> p (t i)").bitcast(I32))
 
-        w1s_hbm = w1_scales.rearrange("a q c -> q a c").bitcast(I32)
-        w1s_first = keep.tile([P, PASSES, 128], I32, name="w1s_first", align_bytes=64)
-        nc.vector.memset(w1s_first[:], 0)
-        for quad in range(4):
-            nc.sync.dma_start(
-                out=w1s_first[32 * quad : 32 * quad + 4, :, :], in_=w1s_hbm[4 * quad : 4 * quad + 4, :, 0:128]
-            )
-        ts_win = keep.tile([P, PASSES, T // 4], I32, name="ts_win", tag="win_words", align_bytes=64)
-        nc.vector.memset(ts_win[:], 0)
-        nc.scalar.dma_start(
-            out=ts_win[4:P:8, :, :], in_=tab_scales.rearrange("a q t -> q a t").bitcast(I32)
-        )
-        table1 = keep.tile([P, T], I32, name="table1", tag="seed_table", align_bytes=64)
-        nc.sync.dma_start(out=table1[:], in_=tab_words[1].rearrange("p t i -> p (t i)").bitcast(I32))
-        table = [table0, table1]
+        one = keep.tile([P, 1], F32, name="one")
+        nc.vector.memset(one[:], 1.0)
+        discount = keep.tile([P, 1], F32, name="discount")
+        nc.scalar.activation(out=discount[:], in_=one[:], func=ACT.Relu, scale=DISCOUNT)
 
+        w1s_hbm = w1_scales.rearrange("a q c -> q a c").bitcast(I32)
+        w1s_raw = keep.tile([P, PASSES, H // 4], I32, name="w1s_raw", align_bytes=64)
+        nc.vector.memset(w1s_raw[:], 0)
+        for quad in range(4):
+            nc.scalar.dma_start(
+                out=w1s_raw[32 * quad : 32 * quad + 4, :, :], in_=w1s_hbm[4 * quad : 4 * quad + 4, :, :]
+            )
+        nc.vector.memset(ts_win[0:96, :], 0)
         v_scales = keep.tile([P, PASSES, S // 4], I32, name="v_scales", align_bytes=64)
         nc.vector.memset(v_scales[:], 0)
 
-        ts_picked = shared.tile([P, PASSES, S], U8, name="ts_picked", offset=15 * 1024)
-        for a in range(PASSES):
-            nc.vector.tensor_copy(ts_picked[:, a, :], ts_win[:, a, :].bitcast(U8).indirect(idx[:]))
-        for quad in range(4):
-            nc.scalar.dma_start(
-                out=v_scales[32 * quad : 32 * quad + 4, :, :],
-                in_=ts_picked[32 * quad + 4 : 32 * quad + 32 : 8, :, :].bitcast(I32),
+        ts_picked = shared.tile([P, S], U8, name="ts_picked", offset=15 * 1024 + 512)
+        nc.vector.tensor_copy(ts_picked[:], ts_win[:].bitcast(U8).indirect(idx[:]))
+
+        def move_scales(queue, a, quad):
+            first = 96 + 16 * a + 4 * quad
+            queue.dma_start(
+                out=v_scales[32 * quad : 32 * quad + 4, a, :], in_=ts_picked[first : first + 4, :].bitcast(I32)
             )
 
-        w1_rest = shared.tile([P, PASSES, 768], I32, name="w1_rest", offset=16 * 1024)
-        w1w_rest = w1_rest[:, :, 0:512]
-        w1s_rest = w1_rest[:, :, 512:768]
-        nc.gpsimd.memset(w1s_rest, 0)
-        nc.sync.dma_start(out=w1w_rest, in_=w1w_hbm[:, :, 256:768])
-        for quad in range(4):
-            nc.sync.dma_start(
-                out=w1s_rest[32 * quad : 32 * quad + 4, :, :], in_=w1s_hbm[4 * quad : 4 * quad + 4, :, 128:384]
-            )
+        move_scales(nc.sync, 0, 0)
+        table1 = keep.tile([P, T], I32, name="table1", tag="win_table", align_bytes=64)
+        nc.sync.dma_start(out=table1[:], in_=tab_words[1].rearrange("p t i -> p (t i)").bitcast(I32))
+        table = [table0, table1]
+        for n in range(1, 4 * PASSES):
+            move_scales(nc.scalar, n // 4, n % 4)
+
+        w1w_rest = shared.tile([P, PASSES, 512], I32, name="w1w_rest", offset=16 * 1024)
+        nc.sync.dma_start(out=w1w_rest[:], in_=w1w_hbm[:, :, 256:768])
         late = shared.tile([P, 16, N], F32, name="late", offset=0)
         for c in range(GROUPS):
             rows = w2[512 * c : 512 * (c + 1), :].rearrange("(b t u) n -> t b u n", t=4, u=8)
@@ -107,29 +103,34 @@ def tile_list_replay_td_errors_kernel(
         w1w = keep.tile([P, GROUPS, PASSES, 256], I32, name="w1w", align_bytes=64)
         w1s = keep.tile([P, GROUPS, PASSES, 128], I32, name="w1s", align_bytes=64)
 
-        def permute_w1(c):
+        def permute_words(c):
             for a in range(PASSES):
                 src = w1w_first[:, a, :] if c == 0 else w1w_rest[:, a, 256 * (c - 1) : 256 * c]
                 nc.vector.tensor_copy(
                     out=w1w[:, c, a, :].rearrange("p (t b w) -> p t b w", t=4, w=4),
                     in_=src.rearrange("p (b t w) -> p t b w", t=4, w=4),
                 )
-                src = w1s_first[:, a, :] if c == 0 else w1s_rest[:, a, 128 * (c - 1) : 128 * c]
+
+        def permute_scales(c):
+            for a in range(PASSES):
                 nc.vector.tensor_copy(
                     out=w1s[:, c, a, :].rearrange("p (t b w) -> p t b w", t=4, w=2),
-                    in_=src.rearrange("p (b t w) -> p t b w", t=4, w=2),
+                    in_=w1s_raw[:, a, 128 * c : 128 * (c + 1)].rearrange("p (b t w) -> p t b w", t=4, w=2),
                 )
 
-        permute_w1(0)
-        v_words = keep.tile([P, PASSES, S], U32, name="v_words", tag="win_words", align_bytes=64)
+        permute_words(0)
+        permute_scales(0)
+        v_words = keep.tile([P, PASSES, S], U32, name="v_words", align_bytes=64)
         nc.vector.tensor_copy(v_words[:, 0, :], table[0][:].bitcast(U32).indirect(idx[:]))
+        permute_scales(1)
+        permute_scales(2)
         for half in range(2):
             nc.vector.tensor_copy(
                 v_words[:, 1, BANK * half : BANK * (half + 1)],
                 table[1][:].bitcast(U32).indirect(idx[:, 32 * half : 32 * (half + 1)]),
             )
-        permute_w1(1)
-        permute_w1(2)
+        permute_words(1)
+        permute_words(2)
 
         def hidden_tile(c, t):
             h = keep.tile([P, S], F32, name="h%d_%d" % (c, t))
@@ -187,20 +188,23 @@ def tile_list_replay_td_errors_kernel(
             c, j0, j1, state, succ = part
             nc.vector.tensor_copy(state[:, t, :], hs[c, t][:].indirect(p1[:, j0 // 16 : j1 // 16]))
 
-        def difference(part, on_gpsimd):
+        def subtract_tile(part, t):
             c, j0, j1, state, succ = part
-            z = ring.tile([P, j1 - j0, 4], BF16, name="z", align_bytes=64)
-            if on_gpsimd:
-                nc.gpsimd.tensor_tensor(
-                    out=z[:],
-                    in0=state[:].rearrange("p t j -> p j t"),
-                    in1=succ[:].rearrange("p t j -> p j t"),
-                    op=ALU.subtract,
-                )
-            else:
-                dst, in0 = interleaved(z[:], state[:])
-                dst, in1 = interleaved(z[:], succ[:])
-                nc.vector.tensor_tensor(out=dst, in0=in0, in1=in1, op=ALU.subtract)
+            nc.gpsimd.tensor_tensor(out=state[:, t, :], in0=state[:, t, :], in1=succ[:, t, :], op=ALU.subtract)
+
+        def round_z(part, x0, x1):
+            c, j0, j1, state, succ = part
+            z = ring.tile([P, x1 - x0, 4], BF16, name="z", align_bytes=64, bufs=3)
+            dst, src = interleaved(z[:], state[:, :, x0 - j0 : x1 - j0])
+            nc.scalar.activation(out=dst, in_=src, func=ACT.Copy)
+            return z
+
+        def difference(part):
+            c, j0, j1, state, succ = part
+            z = ring.tile([P, j1 - j0, 4], BF16, name="z", align_bytes=64, bufs=3)
+            dst, in0 = interleaved(z[:], state[:])
+            dst, in1 = interleaved(z[:], succ[:])
+            nc.vector.tensor_tensor(out=dst, in0=in0, in1=in1, op=ALU.subtract)
             return z
 
         def quantize_z(c, z, z0, j0, j1):
@@ -232,45 +236,46 @@ def tile_list_replay_td_errors_kernel(
             nc.scalar.activation(out=res[:], in_=err[:], func=ACT.Tanh)
             nc.sync.dma_start(out=out_v[:, :, j0:j1], in_=res[:])
 
+        def pick_tile(part, t):
+            pick_succ(part, t)
+            pick_state(part, t)
+            subtract_tile(part, t)
+
         hidden_group(0)
-        hidden_group(1)
         part0 = pick_tiles(0, 0, PAIRS)
         for t in range(4):
-            pick_succ(part0, t)
-            pick_state(part0, t)
-        z0 = difference(part0, True)
-        hidden_group(2)
-        for c in range(GROUPS):
-            round_w2(c)
+            pick_tile(part0, t)
+            hs[1, t] = hidden_tile(1, t)
+        z0 = round_z(part0, 0, PAIRS)
 
         part1 = pick_tiles(1, 0, PAIRS)
         for t in range(4):
             if t == 3:
                 quantize_z(0, z0, 0, 0, PAIRS)
-                for c in range(GROUPS):
-                    quantize_w2(c)
-            pick_succ(part1, t)
-            pick_state(part1, t)
-        z1 = difference(part1, True)
+            pick_tile(part1, t)
+            hs[2, t] = hidden_tile(2, t)
+        z1 = round_z(part1, 0, PAIRS)
+        for c in range(GROUPS):
+            round_w2(c)
+            quantize_w2(c)
 
         last = GROUPS - 1
         part2 = pick_tiles(last, 0, 384)
         for t in range(4):
-            pick_succ(part2, t)
-        for t in range(4):
-            pick_state(part2, t)
-        quantize_z(1, z1, 0, 0, PAIRS)
-        z = difference(part2, False)
+            if t == 3:
+                quantize_z(1, z1, 0, 0, PAIRS)
+            pick_tile(part2, t)
         part3 = pick_tiles(last, 384, PAIRS)
-        pick_succ(part3, 0)
-        quantize_z(last, z, 0, 0, 256)
-        quantize_z(last, z, 0, 256, 384)
-        for t in range(1, 4):
+        for t in range(4):
             pick_succ(part3, t)
+        za = round_z(part2, 0, 256)
+        zb = round_z(part2, 256, 384)
         for t in range(4):
             pick_state(part3, t)
-        heads(0, 256)
-        heads(256, 384)
-        z = difference(part3, False)
+        quantize_z(last, za, 0, 0, 256)
+        z = difference(part3)
+        quantize_z(last, zb, 256, 256, 384)
         quantize_z(last, z, 384, 384, PAIRS)
+        heads(0, 256)
         heads(384, PAIRS)
+        heads(256, 384)

@@ -1,6 +1,7 @@
 from contextlib import ExitStack
 
 import concourse.mybir as mybir
+from concourse.masks import make_identity
 
 K, T, S, PAIRS, H, N = 1024, 4096, 1024, 512, 1536, 256
 FLOPS = 2 * K * H * S + 2 * H * N * PAIRS
@@ -19,7 +20,9 @@ ALU = mybir.AluOpType
 P = 128
 PASSES = K // 512
 GROUPS = H // 512
+LAST = GROUPS - 1
 BANK = 512
+SPLIT = 256
 DISCOUNT = 0.99
 
 
@@ -39,7 +42,7 @@ def tile_list_replay_td_errors_kernel(
         keep = ctx.enter_context(tc.tile_pool(name="keep", bufs=1))
         shared = ctx.enter_context(tc.tile_pool(name="shared", bufs=1))
         ring = ctx.enter_context(tc.tile_pool(name="ring", bufs=2))
-        psum = ctx.enter_context(tc.psum_pool(name="psum", bufs=8))
+        psum = ctx.enter_context(tc.psum_pool(name="psum", bufs=1))
 
         idx = lists.tile([P, S // 16], U16, name="idx")
         p1 = lists.tile([P, PAIRS // 16], U16, name="p1")
@@ -58,11 +61,12 @@ def tile_list_replay_td_errors_kernel(
         table0 = keep.tile([P, T], I32, name="table0", align_bytes=64)
         nc.sync.dma_start(out=table0[:], in_=tab_words[0].rearrange("p t i -> p (t i)").bitcast(I32))
 
-        one = keep.tile([P, 1], F32, name="one")
-        nc.vector.memset(one[:], 1.0)
-        discount = keep.tile([P, 1], F32, name="discount")
-        nc.scalar.activation(out=discount[:], in_=one[:], func=ACT.Relu, scale=DISCOUNT)
+        ones = keep.tile([P, 16], F32, name="ones")
+        nc.vector.memset(ones[:], 1.0)
+        seed = keep.tile([P, 16], F32, name="seed")
+        nc.scalar.activation(out=seed[:], in_=ones[:], func=ACT.Relu, scale=DISCOUNT)
 
+        nc.vector.memset(ts_win[0:96, :], 0)
         w1s_hbm = w1_scales.rearrange("a q c -> q a c").bitcast(I32)
         w1s_raw = keep.tile([P, PASSES, H // 4], I32, name="w1s_raw", align_bytes=64)
         nc.vector.memset(w1s_raw[:], 0)
@@ -70,9 +74,10 @@ def tile_list_replay_td_errors_kernel(
             nc.scalar.dma_start(
                 out=w1s_raw[32 * quad : 32 * quad + 4, :, :], in_=w1s_hbm[4 * quad : 4 * quad + 4, :, :]
             )
-        nc.vector.memset(ts_win[0:96, :], 0)
         v_scales = keep.tile([P, PASSES, S // 4], I32, name="v_scales", align_bytes=64)
         nc.vector.memset(v_scales[:], 0)
+        ident_src = keep.tile([P, P], F32, name="ident_src")
+        make_identity(nc, ident_src[:])
 
         ts_picked = shared.tile([P, S], U8, name="ts_picked", offset=15 * 1024 + 512)
         nc.vector.tensor_copy(ts_picked[:], ts_win[:].bitcast(U8).indirect(idx[:]))
@@ -86,69 +91,80 @@ def tile_list_replay_td_errors_kernel(
         move_scales(nc.sync, 0, 0)
         table1 = keep.tile([P, T], I32, name="table1", tag="win_table", align_bytes=64)
         nc.sync.dma_start(out=table1[:], in_=tab_words[1].rearrange("p t i -> p (t i)").bitcast(I32))
-        table = [table0, table1]
         for n in range(1, 4 * PASSES):
             move_scales(nc.scalar, n // 4, n % 4)
 
-        w1w_rest = shared.tile([P, PASSES, 512], I32, name="w1w_rest", offset=16 * 1024)
+        w1w_rest = shared.tile([P, PASSES, 512], I32, name="w1w_rest", offset=16 * 1024, align_bytes=64)
         nc.sync.dma_start(out=w1w_rest[:], in_=w1w_hbm[:, :, 256:768])
         late = shared.tile([P, 16, N], F32, name="late", offset=0)
-        for c in range(GROUPS):
-            rows = w2[512 * c : 512 * (c + 1), :].rearrange("(b t u) n -> t b u n", t=4, u=8)
-            for t in range(4):
-                nc.sync.dma_start(out=late[:, 4 * c + t, :], in_=rows[t])
+        for c in range(LAST):
+            nc.sync.dma_start(
+                out=late[:, 4 * c : 4 * (c + 1), :],
+                in_=w2[512 * c : 512 * (c + 1), :].rearrange("(p t) n -> p t n", t=4),
+            )
+        rows = w2[512 * LAST : 512 * GROUPS, :].rearrange("(b t u) n -> t b u n", t=4, u=8)
+        for t in range(4):
+            nc.sync.dma_start(out=late[:, 4 * LAST + t, :], in_=rows[t])
         rew_sb = late[:, 12:16, :].rearrange("p (m x) n -> p m (x n)", m=2)
         nc.sync.dma_start(out=rew_sb, in_=rew.rearrange("(m p) j -> p m j", p=P))
 
-        w1w = keep.tile([P, GROUPS, PASSES, 256], I32, name="w1w", align_bytes=64)
-        w1s = keep.tile([P, GROUPS, PASSES, 128], I32, name="w1s", align_bytes=64)
-
-        def permute_words(c):
-            for a in range(PASSES):
-                src = w1w_first[:, a, :] if c == 0 else w1w_rest[:, a, 256 * (c - 1) : 256 * c]
-                nc.vector.tensor_copy(
-                    out=w1w[:, c, a, :].rearrange("p (t b w) -> p t b w", t=4, w=4),
-                    in_=src.rearrange("p (b t w) -> p t b w", t=4, w=4),
-                )
-
-        def permute_scales(c):
-            for a in range(PASSES):
-                nc.vector.tensor_copy(
-                    out=w1s[:, c, a, :].rearrange("p (t b w) -> p t b w", t=4, w=2),
-                    in_=w1s_raw[:, a, 128 * c : 128 * (c + 1)].rearrange("p (b t w) -> p t b w", t=4, w=2),
-                )
-
-        permute_words(0)
-        permute_scales(0)
-        v_words = keep.tile([P, PASSES, S], U32, name="v_words", align_bytes=64)
-        nc.vector.tensor_copy(v_words[:, 0, :], table[0][:].bitcast(U32).indirect(idx[:]))
-        permute_scales(1)
-        permute_scales(2)
+        discount = keep.tile([P, PAIRS], F32, name="discount")
+        nc.vector.tensor_scalar(
+            out=discount[:].rearrange("p (x s) -> p x s", s=16),
+            in0=seed[:].unsqueeze(1).to_broadcast([P, PAIRS // 16, 16]),
+            scalar1=-1.0,
+            scalar2=None,
+            op0=ALU.mult,
+        )
+        v_words = keep.tile([P, PASSES, S], U32, name="v_words", tag="words_ident", align_bytes=64)
+        nc.vector.tensor_copy(v_words[:, 0, :], table0[:].bitcast(U32).indirect(idx[:]))
+        w1s_last = keep.tile([P, PASSES, 128], I32, name="w1s_last", align_bytes=64)
+        for a in range(PASSES):
+            nc.vector.tensor_copy(
+                out=w1s_last[:, a, :].rearrange("p (t b w) -> p t b w", t=4, w=2),
+                in_=w1s_raw[:, a, 128 * LAST : 128 * GROUPS].rearrange("p (b t w) -> p t b w", t=4, w=2),
+            )
         for half in range(2):
             nc.vector.tensor_copy(
                 v_words[:, 1, BANK * half : BANK * (half + 1)],
-                table[1][:].bitcast(U32).indirect(idx[:, 32 * half : 32 * (half + 1)]),
+                table1[:].bitcast(U32).indirect(idx[:, 32 * half : 32 * (half + 1)]),
             )
-        permute_words(1)
-        permute_words(2)
+        w1w_last = keep.tile([P, PASSES, 256], I32, name="w1w_last", tag="win_table", align_bytes=64)
+
+        def permute_words():
+            for a in range(PASSES):
+                nc.vector.tensor_copy(
+                    out=w1w_last[:, a, :].rearrange("p (t b w) -> p t b w", t=4, w=4),
+                    in_=w1w_rest[:, a, 256:512].rearrange("p (b t w) -> p t b w", t=4, w=4),
+                )
+
+        hs = {}
 
         def hidden_tile(c, t):
+            words = (w1w_first, w1w_rest, w1w_last)[c]
             h = keep.tile([P, S], F32, name="h%d_%d" % (c, t))
             for half in range(2):
                 cols = slice(BANK * half, BANK * (half + 1))
-                acc = psum.tile([P, BANK], F32, name="acc", tag="bank")
+                if (2 * (4 * c + t) + half) % 7 < 4:
+                    acc = psum.tile([P, BANK], F32, name="acc", tag="zt", bufs=4)
+                else:
+                    acc = psum.tile([P, BANK], F32, name="acc", tag="bank", bufs=3)
                 for a in range(PASSES):
+                    if c == LAST:
+                        scales = w1s_last[:, a, 32 * t : 32 * (t + 1)]
+                    else:
+                        scales = w1s_raw[:, a, 128 * c + 32 * t : 128 * c + 32 * (t + 1)]
                     nc.tensor.matmul_mx(
                         out=acc[:],
-                        lhsT=w1w[:, c, a, 64 * t : 64 * (t + 1)].bitcast(U8).bitcast(FP4X4),
-                        lhsT_scale=w1s[:, c, a, 32 * t : 32 * (t + 1)].bitcast(U8),
+                        lhsT=words[:, a, 64 * t : 64 * (t + 1)].bitcast(U8).bitcast(FP4X4),
+                        lhsT_scale=scales.bitcast(U8),
                         rhs=v_words[:, a, cols].bitcast(FP8X4),
                         rhs_scale=v_scales[:, a, :].bitcast(U8)[:, cols],
                         start=(a == 0),
                         stop=(a == PASSES - 1),
                     )
                 nc.scalar.activation(out=h[:, cols], in_=acc[:], func=ACT.Relu)
-            return h
+            hs[c, t] = h
 
         w2_codes = keep.tile([P, GROUPS, N], U32, name="w2_codes", align_bytes=64)
         w2_scales = keep.tile([P, GROUPS, N], U8, name="w2_scales", align_bytes=64)
@@ -165,14 +181,11 @@ def tile_list_replay_td_errors_kernel(
                 in_=w2_bf[:, c, :, :].rearrange("p n t -> p (n t)"),
             )
 
-        hs = {}
-
-        def hidden_group(c):
-            for t in range(4):
-                hs[c, t] = hidden_tile(c, t)
-
         z_codes = keep.tile([P, GROUPS, PAIRS], U32, name="z_codes", align_bytes=64)
         z_scales = keep.tile([P, GROUPS, PAIRS], U8, name="z_scales", align_bytes=64)
+        z_bf = [
+            keep.tile([P, PAIRS, 4], BF16, name="z_bf%d" % c, tag="z%d" % c, align_bytes=64) for c in range(GROUPS)
+        ]
 
         def pick_tiles(c, j0, j1):
             state = ring.tile([P, 4, j1 - j0], F32, name="state", bufs=3)
@@ -181,101 +194,107 @@ def tile_list_replay_td_errors_kernel(
 
         def pick_succ(part, t):
             c, j0, j1, state, succ = part
-            nc.vector.tensor_copy(succ[:, t, :], hs[c, t][:].indirect(p2[:, j0 // 16 : j1 // 16]))
-            nc.scalar.activation(out=succ[:, t, :], in_=succ[:, t, :], func=ACT.Copy, scale=discount[:])
+            nc.vector.tensor_tensor(
+                succ[:, t, :], hs[c, t][:].indirect(p2[:, j0 // 16 : j1 // 16]), discount[:, j0:j1], ALU.mult
+            )
 
         def pick_state(part, t):
             c, j0, j1, state, succ = part
             nc.vector.tensor_copy(state[:, t, :], hs[c, t][:].indirect(p1[:, j0 // 16 : j1 // 16]))
 
-        def subtract_tile(part, t):
+        def add_turned(part, zt, block, t):
             c, j0, j1, state, succ = part
-            nc.gpsimd.tensor_tensor(out=state[:, t, :], in0=state[:, t, :], in1=succ[:, t, :], op=ALU.subtract)
+            cols = slice(P * block, P * (block + 1))
+            dst = zt[:, P * t : P * (t + 1)]
+            nc.tensor.matmul(dst, lhsT=succ[:, t, cols], rhs=ident[:], is_transpose=True, start=True, stop=False)
+            nc.tensor.matmul(dst, lhsT=state[:, t, cols], rhs=ident[:], is_transpose=True, start=False, stop=True)
 
-        def round_z(part, x0, x1):
-            c, j0, j1, state, succ = part
-            z = ring.tile([P, x1 - x0, 4], BF16, name="z", align_bytes=64, bufs=3)
-            dst, src = interleaved(z[:], state[:, :, x0 - j0 : x1 - j0])
-            nc.scalar.activation(out=dst, in_=src, func=ACT.Copy)
-            return z
+        def turn_back(c, zts, first):
+            back = psum.tile([P, 2, 2, P], F32, name="back")
+            for b in range(2):
+                rounded = ring.tile([P, 2, P, 2], BF16, name="rounded", bufs=3)
+                zt = zts[first + b]
+                if c == LAST:
+                    src = zt[:].rearrange("j (u e p) -> j u p e", u=2, e=2)
+                else:
+                    src = zt[:].rearrange("j (p u e) -> j u p e", u=2, e=2)
+                nc.scalar.activation(out=rounded[:], in_=src, func=ACT.Copy)
+                pairs = rounded[:].rearrange("j u p e -> j (u p e)").bitcast(F32)
+                for u in range(2):
+                    nc.tensor.transpose(back[:, b, u, :], pairs[:, P * u : P * (u + 1)], ident[:])
+            dst = z_bf[c][:, P * first : P * (first + 2), :].rearrange("p j t -> p (j t)").bitcast(F32)
+            nc.scalar.copy(
+                out=dst.rearrange("p (b j u) -> p b j u", b=2, u=2), in_=back[:].rearrange("p b u j -> p b j u")
+            )
 
-        def difference(part):
-            c, j0, j1, state, succ = part
-            z = ring.tile([P, j1 - j0, 4], BF16, name="z", align_bytes=64, bufs=3)
-            dst, in0 = interleaved(z[:], state[:])
-            dst, in1 = interleaved(z[:], succ[:])
-            nc.vector.tensor_tensor(out=dst, in0=in0, in1=in1, op=ALU.subtract)
-            return z
-
-        def quantize_z(c, z, z0, j0, j1):
+        def quantize_z(c, j0, j1):
             nc.vector.quantize_mx(
                 out=z_codes[:, c, j0:j1].bitcast(FP8X4),
                 scales=z_scales[:, c, j0:j1],
-                in_=z[:, j0 - z0 : j1 - z0, :].rearrange("p j t -> p (j t)"),
+                in_=z_bf[c][:, j0:j1, :].rearrange("p j t -> p (j t)"),
             )
 
         out_v = out.rearrange("(m p) j -> p m j", p=P)
 
-        def heads(j0, j1):
-            width = j1 - j0
-            err = ring.tile([P, 2, width], F32, name="err", bufs=3)
-            res = ring.tile([P, 2, width], F32, name="res", bufs=3)
+        def heads(pieces, tags):
+            j0, j1 = pieces[0][0], pieces[-1][1]
+            err = ring.tile([P, 2, j1 - j0], F32, name="err")
+            res = ring.tile([P, 2, j1 - j0], F32, name="res")
             for m in range(2):
-                acc = psum.tile([P, width], F32, name="acc_d", tag="bank")
-                for c in range(GROUPS):
-                    nc.tensor.matmul_mx(
-                        out=acc[:],
-                        lhsT=w2_codes[:, c, P * m : P * (m + 1)].bitcast(FP8X4),
-                        lhsT_scale=w2_scales[:, c, P * m : P * (m + 1)],
-                        rhs=z_codes[:, c, j0:j1].bitcast(FP8X4),
-                        rhs_scale=z_scales[:, c, j0:j1],
-                        start=(c == 0),
-                        stop=(c == GROUPS - 1),
-                    )
+                acc = psum.tile([P, j1 - j0], F32, name="acc_d", tag=tags[m][0], bufs=tags[m][1])
+                for x0, x1 in pieces:
+                    for c in range(GROUPS):
+                        nc.tensor.matmul_mx(
+                            out=acc[:, x0 - j0 : x1 - j0],
+                            lhsT=w2_codes[:, c, P * m : P * (m + 1)].bitcast(FP8X4),
+                            lhsT_scale=w2_scales[:, c, P * m : P * (m + 1)],
+                            rhs=z_codes[:, c, x0:x1].bitcast(FP8X4),
+                            rhs_scale=z_scales[:, c, x0:x1],
+                            start=(c == 0),
+                            stop=(c == LAST),
+                        )
                 nc.vector.tensor_tensor(out=err[:, m, :], in0=rew_sb[:, m, j0:j1], in1=acc[:], op=ALU.subtract)
-            nc.scalar.activation(out=res[:], in_=err[:], func=ACT.Tanh)
-            nc.sync.dma_start(out=out_v[:, :, j0:j1], in_=res[:])
+                nc.scalar.activation(out=res[:, m, :], in_=err[:, m, :], func=ACT.Tanh)
+                nc.sync.dma_start(out=out_v[:, m, j0:j1], in_=res[:, m, :])
 
-        def pick_tile(part, t):
-            pick_succ(part, t)
-            pick_state(part, t)
-            subtract_tile(part, t)
-
-        hidden_group(0)
-        part0 = pick_tiles(0, 0, PAIRS)
-        for t in range(4):
-            pick_tile(part0, t)
-            hs[1, t] = hidden_tile(1, t)
-        z0 = round_z(part0, 0, PAIRS)
-
-        part1 = pick_tiles(1, 0, PAIRS)
-        for t in range(4):
-            if t == 3:
-                quantize_z(0, z0, 0, 0, PAIRS)
-            pick_tile(part1, t)
-            hs[2, t] = hidden_tile(2, t)
-        z1 = round_z(part1, 0, PAIRS)
+        for c in range(GROUPS):
+            if c == LAST:
+                permute_words()
+            for t in range(4):
+                hidden_tile(c, t)
+        ident = keep.tile([P, P], F32, name="ident", tag="words_ident", align_bytes=64)
+        nc.scalar.copy(out=ident[:], in_=ident_src[:])
         for c in range(GROUPS):
             round_w2(c)
+
+        for c in range(GROUPS):
+            width = SPLIT if c == LAST else PAIRS
+            part = pick_tiles(c, 0, width)
+            blocks = range(width // P)
+            zts = [psum.tile([P, BANK], F32, name="zt", tag="zt", bufs=4) for block in blocks]
+            for t in range(4):
+                pick_succ(part, t)
+                pick_state(part, t)
+                for block in blocks:
+                    add_turned(part, zts[block], block, t)
+            for first in range(0, len(zts), 2):
+                turn_back(c, zts, first)
+        for c in range(GROUPS):
             quantize_w2(c)
 
-        last = GROUPS - 1
-        part2 = pick_tiles(last, 0, 384)
+        quantize_z(0, 0, PAIRS)
+        succ = keep.tile([P, 4, PAIRS - SPLIT], F32, name="succ_tail", tag="z0", align_bytes=64)
+        state = keep.tile([P, 4, PAIRS - SPLIT], F32, name="state_tail", tag="z1", align_bytes=64)
+        narrow = (LAST, SPLIT, PAIRS, state, succ)
         for t in range(4):
-            if t == 3:
-                quantize_z(1, z1, 0, 0, PAIRS)
-            pick_tile(part2, t)
-        part3 = pick_tiles(last, 384, PAIRS)
+            pick_succ(narrow, t)
+        quantize_z(1, 0, PAIRS)
         for t in range(4):
-            pick_succ(part3, t)
-        za = round_z(part2, 0, 256)
-        zb = round_z(part2, 256, 384)
-        for t in range(4):
-            pick_state(part3, t)
-        quantize_z(last, za, 0, 0, 256)
-        z = difference(part3)
-        quantize_z(last, zb, 256, 256, 384)
-        quantize_z(last, z, 384, 384, PAIRS)
-        heads(0, 256)
-        heads(384, PAIRS)
-        heads(256, 384)
+            pick_state(narrow, t)
+        dst, in0 = interleaved(z_bf[LAST][:, SPLIT:PAIRS, :], state[:])
+        dst, in1 = interleaved(z_bf[LAST][:, SPLIT:PAIRS, :], succ[:])
+        nc.vector.tensor_tensor(out=dst, in0=in0, in1=in1, op=ALU.add)
+        quantize_z(LAST, 0, SPLIT)
+        quantize_z(LAST, SPLIT, PAIRS)
+        heads([(0, SPLIT)], [("bank", 3), ("bank", 3)])
+        heads([(SPLIT, PAIRS)], [("bank", 3), ("zt", 4)])

@@ -1,7 +1,6 @@
 from contextlib import ExitStack
 
 import concourse.mybir as mybir
-from concourse.masks import make_identity
 
 K, T, S, PAIRS, H, N = 1024, 4096, 1024, 512, 1536, 256
 FLOPS = 2 * K * H * S + 2 * H * N * PAIRS
@@ -22,6 +21,7 @@ PASSES = K // 512
 GROUPS = H // 512
 LAST = GROUPS - 1
 BANK = 512
+BANK_BYTES = 2048
 SPLIT = 256
 DISCOUNT = 0.99
 
@@ -58,7 +58,7 @@ def tile_list_replay_td_errors_kernel(
         w1w_hbm = w1_words.rearrange("a p c -> p a c").bitcast(I32)
         w1w_first = keep.tile([P, PASSES, 256], I32, name="w1w_first", align_bytes=64)
         nc.sync.dma_start(out=w1w_first[:], in_=w1w_hbm[:, :, 0:256])
-        table0 = keep.tile([P, T], I32, name="table0", align_bytes=64)
+        table0 = keep.tile([P, T], I32, name="table0", tag="table0", align_bytes=64)
         nc.sync.dma_start(out=table0[:], in_=tab_words[0].rearrange("p t i -> p (t i)").bitcast(I32))
 
         ones = keep.tile([P, 16], F32, name="ones")
@@ -76,8 +76,6 @@ def tile_list_replay_td_errors_kernel(
             )
         v_scales = keep.tile([P, PASSES, S // 4], I32, name="v_scales", align_bytes=64)
         nc.vector.memset(v_scales[:], 0)
-        ident_src = keep.tile([P, P], F32, name="ident_src")
-        make_identity(nc, ident_src[:])
 
         ts_picked = shared.tile([P, S], U8, name="ts_picked", offset=15 * 1024 + 512)
         nc.vector.tensor_copy(ts_picked[:], ts_win[:].bitcast(U8).indirect(idx[:]))
@@ -97,204 +95,142 @@ def tile_list_replay_td_errors_kernel(
         w1w_rest = shared.tile([P, PASSES, 512], I32, name="w1w_rest", offset=16 * 1024, align_bytes=64)
         nc.sync.dma_start(out=w1w_rest[:], in_=w1w_hbm[:, :, 256:768])
         late = shared.tile([P, 16, N], F32, name="late", offset=0)
-        for c in range(LAST):
-            nc.sync.dma_start(
-                out=late[:, 4 * c : 4 * (c + 1), :],
-                in_=w2[512 * c : 512 * (c + 1), :].rearrange("(p t) n -> p t n", t=4),
-            )
-        rows = w2[512 * LAST : 512 * GROUPS, :].rearrange("(b t u) n -> t b u n", t=4, u=8)
-        for t in range(4):
-            nc.sync.dma_start(out=late[:, 4 * LAST + t, :], in_=rows[t])
+        for c in range(GROUPS):
+            rows = w2[512 * c : 512 * (c + 1), :].rearrange("(b t u) n -> t b u n", t=4, u=8)
+            for t in range(4):
+                nc.sync.dma_start(out=late[:, 4 * c + t, :], in_=rows[t])
         rew_sb = late[:, 12:16, :].rearrange("p (m x) n -> p m (x n)", m=2)
         nc.sync.dma_start(out=rew_sb, in_=rew.rearrange("(m p) j -> p m j", p=P))
 
-        discount = keep.tile([P, PAIRS], F32, name="discount")
-        nc.vector.tensor_scalar(
-            out=discount[:].rearrange("p (x s) -> p x s", s=16),
-            in0=seed[:].unsqueeze(1).to_broadcast([P, PAIRS // 16, 16]),
-            scalar1=-1.0,
-            scalar2=None,
-            op0=ALU.mult,
-        )
-        v_words = keep.tile([P, PASSES, S], U32, name="v_words", tag="words_ident", align_bytes=64)
-        nc.vector.tensor_copy(v_words[:, 0, :], table0[:].bitcast(U32).indirect(idx[:]))
-        w1s_last = keep.tile([P, PASSES, 128], I32, name="w1s_last", align_bytes=64)
-        for a in range(PASSES):
+        def dealt(name, raw, run):
+            width = 64 * run
+            tile = keep.tile([P, PASSES, width], I32, name=name, tag=name, align_bytes=64)
             nc.vector.tensor_copy(
-                out=w1s_last[:, a, :].rearrange("p (t b w) -> p t b w", t=4, w=2),
-                in_=w1s_raw[:, a, 128 * LAST : 128 * GROUPS].rearrange("p (b t w) -> p t b w", t=4, w=2),
+                out=tile[:].rearrange("p a (t b w) -> p a t b w", t=4, w=run),
+                in_=raw.rearrange("p a (b t w) -> p a t b w", t=4, w=run),
             )
+            return tile
+
+        w1s = [dealt("w1s%d" % c, w1s_raw[:, :, 128 * c : 128 * (c + 1)], 2) for c in range(GROUPS)]
+        w1w = [dealt("w1w0", w1w_first[:], 4)]
+        v_words = keep.tile([P, PASSES, S], U32, name="v_words", align_bytes=64)
+        nc.vector.tensor_copy(v_words[:, 0, :], table0[:].bitcast(U32).indirect(idx[:]))
         for half in range(2):
             nc.vector.tensor_copy(
                 v_words[:, 1, BANK * half : BANK * (half + 1)],
                 table1[:].bitcast(U32).indirect(idx[:, 32 * half : 32 * (half + 1)]),
             )
-        w1w_last = keep.tile([P, PASSES, 256], I32, name="w1w_last", tag="win_table", align_bytes=64)
+        for c in range(1, GROUPS):
+            w1w.append(dealt("w1w%d" % c, w1w_rest[:, :, 256 * (c - 1) : 256 * c], 4))
 
-        def permute_words():
-            for a in range(PASSES):
-                nc.vector.tensor_copy(
-                    out=w1w_last[:, a, :].rearrange("p (t b w) -> p t b w", t=4, w=4),
-                    in_=w1w_rest[:, a, 256:512].rearrange("p (b t w) -> p t b w", t=4, w=4),
-                )
+        def bank(name, n):
+            return psum.tile([P, BANK], F32, name=name, offset=n * BANK_BYTES)
 
-        hs = {}
+        hs = [keep.tile([P, 2 * S], F32, name="h%d" % i) for i in range(4 * GROUPS)]
 
         def hidden_tile(c, t):
-            words = (w1w_first, w1w_rest, w1w_last)[c]
-            h = keep.tile([P, S], F32, name="h%d_%d" % (c, t))
             for half in range(2):
                 cols = slice(BANK * half, BANK * (half + 1))
-                if (2 * (4 * c + t) + half) % 7 < 4:
-                    acc = psum.tile([P, BANK], F32, name="acc", tag="zt", bufs=4)
-                else:
-                    acc = psum.tile([P, BANK], F32, name="acc", tag="bank", bufs=3)
+                acc = bank("acc%d_%d_%d" % (c, t, half), (t + 2 * half - 1) % 4)
                 for a in range(PASSES):
-                    if c == LAST:
-                        scales = w1s_last[:, a, 32 * t : 32 * (t + 1)]
-                    else:
-                        scales = w1s_raw[:, a, 128 * c + 32 * t : 128 * c + 32 * (t + 1)]
                     nc.tensor.matmul_mx(
                         out=acc[:],
-                        lhsT=words[:, a, 64 * t : 64 * (t + 1)].bitcast(U8).bitcast(FP4X4),
-                        lhsT_scale=scales.bitcast(U8),
+                        lhsT=w1w[c][:, a, 64 * t : 64 * (t + 1)].bitcast(U8).bitcast(FP4X4),
+                        lhsT_scale=w1s[c][:, a, 32 * t : 32 * (t + 1)].bitcast(U8),
                         rhs=v_words[:, a, cols].bitcast(FP8X4),
                         rhs_scale=v_scales[:, a, :].bitcast(U8)[:, cols],
                         start=(a == 0),
                         stop=(a == PASSES - 1),
                     )
-                nc.scalar.activation(out=h[:, cols], in_=acc[:], func=ACT.Relu)
-            hs[c, t] = h
+                nc.scalar.activation(out=hs[4 * c + t][:, cols], in_=acc[:], func=ACT.Relu)
 
         w2_codes = keep.tile([P, GROUPS, N], U32, name="w2_codes", align_bytes=64)
         w2_scales = keep.tile([P, GROUPS, N], U8, name="w2_scales", align_bytes=64)
-        w2_bf = keep.tile([P, GROUPS, N, 4], BF16, name="w2_bf", align_bytes=64)
+        z_codes = keep.tile([P, GROUPS, PAIRS], U32, name="z_codes", align_bytes=64)
+        z_scales = keep.tile([P, GROUPS, PAIRS], U8, name="z_scales", align_bytes=64)
+        succ = [keep.tile([P, 4, PAIRS], F32, name="succ", bufs=2) for c in range(GROUPS)]
+        z = []
 
-        def round_w2(c):
+        def pick_succ(i):
+            nc.vector.tensor_scalar(
+                out=succ[i // 4][:, i % 4, :],
+                in0=hs[i][:].indirect(p2[:]),
+                scalar1=-DISCOUNT,
+                scalar2=0.0,
+                op0=ALU.mult,
+                op1=ALU.add,
+            )
+
+        def pick_state(i, j0, j1):
+            c, t = divmod(i, 4)
+            nc.vector.tensor_tensor(
+                z[c][:, t, j0:j1], hs[i][:].indirect(p1[:, j0 // 16 : j1 // 16]), succ[c][:, t, j0:j1], ALU.add
+            )
+
+        def quantize_z(c, j0, j1, on_vector, tag):
+            z_bf = keep.tile([P, j1 - j0, 4], BF16, name="z_bf", tag=tag, align_bytes=64)
+            dst, src = interleaved(z_bf[:], z[c][:, :, j0:j1])
+            if on_vector:
+                nc.vector.tensor_copy(out=dst, in_=src)
+            else:
+                nc.scalar.activation(out=dst, in_=src, func=ACT.Copy)
+            nc.vector.quantize_mx(
+                out=z_codes[:, c, j0:j1].bitcast(FP8X4),
+                scales=z_scales[:, c, j0:j1],
+                in_=z_bf[:].rearrange("p j t -> p (j t)"),
+            )
+
+        for c in range(GROUPS):
+            for t in range(4):
+                hidden_tile(c, t)
+
+        for c in range(LAST):
+            z.append(keep.tile([P, 4, PAIRS], F32, name="z", tag="w1w%d" % c, align_bytes=64))
+        pick_succ(0)
+        for i in range(4 * LAST):
+            pick_succ(i + 1)
+            pick_state(i, 0, PAIRS)
+        for i in range(4 * LAST + 1, 4 * GROUPS):
+            pick_succ(i)
+        w2_bf = keep.tile([P, GROUPS, N, 4], BF16, name="w2_bf", tag="w1s0", align_bytes=64)
+        quantize_z(0, 0, PAIRS, False, "table0")
+        for c in range(GROUPS):
             dst, src = interleaved(w2_bf[:, c, :, :], late[:, 4 * c : 4 * (c + 1), :])
             nc.scalar.activation(out=dst, in_=src, func=ACT.Copy)
-
-        def quantize_w2(c):
             nc.vector.quantize_mx(
                 out=w2_codes[:, c, :].bitcast(FP8X4),
                 scales=w2_scales[:, c, :],
                 in_=w2_bf[:, c, :, :].rearrange("p n t -> p (n t)"),
             )
-
-        z_codes = keep.tile([P, GROUPS, PAIRS], U32, name="z_codes", align_bytes=64)
-        z_scales = keep.tile([P, GROUPS, PAIRS], U8, name="z_scales", align_bytes=64)
-        z_bf = [
-            keep.tile([P, PAIRS, 4], BF16, name="z_bf%d" % c, tag="z%d" % c, align_bytes=64) for c in range(GROUPS)
-        ]
-
-        def pick_tiles(c, j0, j1):
-            state = ring.tile([P, 4, j1 - j0], F32, name="state", bufs=3)
-            succ = ring.tile([P, 4, j1 - j0], F32, name="succ", bufs=3)
-            return c, j0, j1, state, succ
-
-        def pick_succ(part, t):
-            c, j0, j1, state, succ = part
-            nc.vector.tensor_tensor(
-                succ[:, t, :], hs[c, t][:].indirect(p2[:, j0 // 16 : j1 // 16]), discount[:, j0:j1], ALU.mult
-            )
-
-        def pick_state(part, t):
-            c, j0, j1, state, succ = part
-            nc.vector.tensor_copy(state[:, t, :], hs[c, t][:].indirect(p1[:, j0 // 16 : j1 // 16]))
-
-        def add_turned(part, zt, block, t):
-            c, j0, j1, state, succ = part
-            cols = slice(P * block, P * (block + 1))
-            dst = zt[:, P * t : P * (t + 1)]
-            nc.tensor.matmul(dst, lhsT=succ[:, t, cols], rhs=ident[:], is_transpose=True, start=True, stop=False)
-            nc.tensor.matmul(dst, lhsT=state[:, t, cols], rhs=ident[:], is_transpose=True, start=False, stop=True)
-
-        def turn_back(c, zts, first):
-            back = psum.tile([P, 2, 2, P], F32, name="back")
-            for b in range(2):
-                rounded = ring.tile([P, 2, P, 2], BF16, name="rounded", bufs=3)
-                zt = zts[first + b]
-                if c == LAST:
-                    src = zt[:].rearrange("j (u e p) -> j u p e", u=2, e=2)
-                else:
-                    src = zt[:].rearrange("j (p u e) -> j u p e", u=2, e=2)
-                nc.scalar.activation(out=rounded[:], in_=src, func=ACT.Copy)
-                pairs = rounded[:].rearrange("j u p e -> j (u p e)").bitcast(F32)
-                for u in range(2):
-                    nc.tensor.transpose(back[:, b, u, :], pairs[:, P * u : P * (u + 1)], ident[:])
-            dst = z_bf[c][:, P * first : P * (first + 2), :].rearrange("p j t -> p (j t)").bitcast(F32)
-            nc.scalar.copy(
-                out=dst.rearrange("p (b j u) -> p b j u", b=2, u=2), in_=back[:].rearrange("p b u j -> p b j u")
-            )
-
-        def quantize_z(c, j0, j1):
-            nc.vector.quantize_mx(
-                out=z_codes[:, c, j0:j1].bitcast(FP8X4),
-                scales=z_scales[:, c, j0:j1],
-                in_=z_bf[c][:, j0:j1, :].rearrange("p j t -> p (j t)"),
-            )
+        quantize_z(1, 0, PAIRS, False, "win_table")
+        z.append(keep.tile([P, 4, PAIRS], F32, name="z", tag="win_table", align_bytes=64))
+        pieces = ((0, 256), (256, 384), (384, 512))
+        for j0, j1 in pieces:
+            for t in range(4):
+                pick_state(4 * LAST + t, j0, j1)
+        for j0, j1 in pieces:
+            quantize_z(LAST, j0, j1, j1 == PAIRS, "z_last%d" % j0)
 
         out_v = out.rearrange("(m p) j -> p m j", p=P)
-
-        def heads(pieces, tags):
-            j0, j1 = pieces[0][0], pieces[-1][1]
-            err = ring.tile([P, 2, j1 - j0], F32, name="err")
-            res = ring.tile([P, 2, j1 - j0], F32, name="res")
+        for half in range(2):
+            cols = slice(SPLIT * half, SPLIT * (half + 1))
+            err = ring.tile([P, 2, SPLIT], F32, name="err")
+            res = ring.tile([P, 2, SPLIT], F32, name="res")
+            d = [bank("d%d_%d" % (half, m), 4 + 2 * half + m) for m in range(2)]
+            for c in range(GROUPS):
+                for m in range(2):
+                    nc.tensor.matmul_mx(
+                        out=d[m][:, 0:SPLIT],
+                        lhsT=w2_codes[:, c, P * m : P * (m + 1)].bitcast(FP8X4),
+                        lhsT_scale=w2_scales[:, c, P * m : P * (m + 1)],
+                        rhs=z_codes[:, c, cols].bitcast(FP8X4),
+                        rhs_scale=z_scales[:, c, cols],
+                        start=(c == 0),
+                        stop=(c == LAST),
+                    )
             for m in range(2):
-                acc = psum.tile([P, j1 - j0], F32, name="acc_d", tag=tags[m][0], bufs=tags[m][1])
-                for x0, x1 in pieces:
-                    for c in range(GROUPS):
-                        nc.tensor.matmul_mx(
-                            out=acc[:, x0 - j0 : x1 - j0],
-                            lhsT=w2_codes[:, c, P * m : P * (m + 1)].bitcast(FP8X4),
-                            lhsT_scale=w2_scales[:, c, P * m : P * (m + 1)],
-                            rhs=z_codes[:, c, x0:x1].bitcast(FP8X4),
-                            rhs_scale=z_scales[:, c, x0:x1],
-                            start=(c == 0),
-                            stop=(c == LAST),
-                        )
-                nc.vector.tensor_tensor(out=err[:, m, :], in0=rew_sb[:, m, j0:j1], in1=acc[:], op=ALU.subtract)
+                nc.vector.tensor_tensor(
+                    out=err[:, m, :], in0=rew_sb[:, m, cols], in1=d[m][:, 0:SPLIT], op=ALU.subtract
+                )
                 nc.scalar.activation(out=res[:, m, :], in_=err[:, m, :], func=ACT.Tanh)
-                nc.sync.dma_start(out=out_v[:, m, j0:j1], in_=res[:, m, :])
-
-        for c in range(GROUPS):
-            if c == LAST:
-                permute_words()
-            for t in range(4):
-                hidden_tile(c, t)
-        ident = keep.tile([P, P], F32, name="ident", tag="words_ident", align_bytes=64)
-        nc.scalar.copy(out=ident[:], in_=ident_src[:])
-        for c in range(GROUPS):
-            round_w2(c)
-
-        for c in range(GROUPS):
-            width = SPLIT if c == LAST else PAIRS
-            part = pick_tiles(c, 0, width)
-            blocks = range(width // P)
-            zts = [psum.tile([P, BANK], F32, name="zt", tag="zt", bufs=4) for block in blocks]
-            for t in range(4):
-                pick_succ(part, t)
-                pick_state(part, t)
-                for block in blocks:
-                    add_turned(part, zts[block], block, t)
-            for first in range(0, len(zts), 2):
-                turn_back(c, zts, first)
-        for c in range(GROUPS):
-            quantize_w2(c)
-
-        quantize_z(0, 0, PAIRS)
-        succ = keep.tile([P, 4, PAIRS - SPLIT], F32, name="succ_tail", tag="z0", align_bytes=64)
-        state = keep.tile([P, 4, PAIRS - SPLIT], F32, name="state_tail", tag="z1", align_bytes=64)
-        narrow = (LAST, SPLIT, PAIRS, state, succ)
-        for t in range(4):
-            pick_succ(narrow, t)
-        quantize_z(1, 0, PAIRS)
-        for t in range(4):
-            pick_state(narrow, t)
-        dst, in0 = interleaved(z_bf[LAST][:, SPLIT:PAIRS, :], state[:])
-        dst, in1 = interleaved(z_bf[LAST][:, SPLIT:PAIRS, :], succ[:])
-        nc.vector.tensor_tensor(out=dst, in0=in0, in1=in1, op=ALU.add)
-        quantize_z(LAST, 0, SPLIT)
-        quantize_z(LAST, SPLIT, PAIRS)
-        heads([(0, SPLIT)], [("bank", 3), ("bank", 3)])
-        heads([(SPLIT, PAIRS)], [("bank", 3), ("zt", 4)])
+                nc.sync.dma_start(out=out_v[:, m, cols], in_=res[:, m, :])

@@ -48,49 +48,44 @@ def tile_list_replay_td_errors_kernel(
         p1 = lists.tile([P, PAIRS // 16], U16, name="p1")
         p2 = lists.tile([P, PAIRS // 16], U16, name="p2")
 
-        ts_win = keep.tile([P, T // 4], I32, name="ts_win", tag="win_table", align_bytes=64)
-        nc.sync.dma_start(
-            out=ts_win[96:P, :], in_=tab_scales.rearrange("a q t -> (a q) t").bitcast(I32)
-        )
+        ts_win = keep.tile([P, T // 4], I32, name="ts_win", align_bytes=64)
         nc.sync.dma_start(idx[:], offs)
-        nc.sync.dma_start(p1[:], pos1)
+        nc.sync.dma_start(out=ts_win[0:32, :], in_=tab_scales.rearrange("a q t -> (a q) t").bitcast(I32))
         nc.sync.dma_start(p2[:], pos2)
-        w1w_hbm = w1_words.rearrange("a p c -> p a c").bitcast(I32)
-        w1w_first = keep.tile([P, PASSES, 256], I32, name="w1w_first", align_bytes=64)
-        nc.sync.dma_start(out=w1w_first[:], in_=w1w_hbm[:, :, 0:256])
+        nc.sync.dma_start(p1[:], pos1)
         table0 = keep.tile([P, T], I32, name="table0", tag="table0", align_bytes=64)
         nc.sync.dma_start(out=table0[:], in_=tab_words[0].rearrange("p t i -> p (t i)").bitcast(I32))
-
-        ones = keep.tile([P, 16], F32, name="ones")
-        nc.vector.memset(ones[:], 1.0)
-        seed = keep.tile([P, 16], F32, name="seed")
-        nc.scalar.activation(out=seed[:], in_=ones[:], func=ACT.Relu, scale=DISCOUNT)
-
-        nc.vector.memset(ts_win[0:96, :], 0)
+        w1w_hbm = w1_words.rearrange("a p c -> p a c").bitcast(I32)
+        w1w_first = keep.tile([P, PASSES, 256], I32, name="w1w_first", align_bytes=64)
+        nc.scalar.dma_start(out=w1w_first[:], in_=w1w_hbm[:, :, 0:256])
         w1s_hbm = w1_scales.rearrange("a q c -> q a c").bitcast(I32)
         w1s_raw = keep.tile([P, PASSES, H // 4], I32, name="w1s_raw", align_bytes=64)
-        nc.vector.memset(w1s_raw[:], 0)
         for quad in range(4):
             nc.scalar.dma_start(
                 out=w1s_raw[32 * quad : 32 * quad + 4, :, :], in_=w1s_hbm[4 * quad : 4 * quad + 4, :, :]
             )
+
+        ones = keep.tile([P, 16], F32, name="ones", tag="win_table", align_bytes=64)
+        nc.vector.memset(ones[:], 1.0)
+        seed = keep.tile([P, 16], F32, name="seed")
+        nc.scalar.activation(out=seed[:], in_=ones[:], func=ACT.Tanh)
+        table1 = keep.tile([P, T], I32, name="table1", tag="win_table", align_bytes=64)
+        nc.sync.dma_start(out=table1[:], in_=tab_words[1].rearrange("p t i -> p (t i)").bitcast(I32))
+
+        nc.gpsimd.memset(ts_win[32:64, :], 0)
+        nc.vector.memset(ts_win[64:P, :], 0)
         v_scales = keep.tile([P, PASSES, S // 4], I32, name="v_scales", align_bytes=64)
         nc.vector.memset(v_scales[:], 0)
 
         ts_picked = shared.tile([P, S], U8, name="ts_picked", offset=15 * 1024 + 512)
         nc.vector.tensor_copy(ts_picked[:], ts_win[:].bitcast(U8).indirect(idx[:]))
 
-        def move_scales(queue, a, quad):
-            first = 96 + 16 * a + 4 * quad
-            queue.dma_start(
-                out=v_scales[32 * quad : 32 * quad + 4, a, :], in_=ts_picked[first : first + 4, :].bitcast(I32)
-            )
-
-        move_scales(nc.sync, 0, 0)
-        table1 = keep.tile([P, T], I32, name="table1", tag="win_table", align_bytes=64)
-        nc.sync.dma_start(out=table1[:], in_=tab_words[1].rearrange("p t i -> p (t i)").bitcast(I32))
+        nc.vector.tensor_copy(out=v_scales[0:4, 0, :], in_=ts_picked[0:4, :].bitcast(I32))
         for n in range(1, 4 * PASSES):
-            move_scales(nc.scalar, n // 4, n % 4)
+            a, quad = divmod(n, 4)
+            nc.scalar.dma_start(
+                out=v_scales[32 * quad : 32 * quad + 4, a, :], in_=ts_picked[4 * n : 4 * n + 4, :].bitcast(I32)
+            )
 
         w1w_rest = shared.tile([P, PASSES, 512], I32, name="w1w_rest", offset=16 * 1024, align_bytes=64)
         nc.sync.dma_start(out=w1w_rest[:], in_=w1w_hbm[:, :, 256:768])
@@ -111,7 +106,14 @@ def tile_list_replay_td_errors_kernel(
             )
             return tile
 
-        w1s = [dealt("w1s%d" % c, w1s_raw[:, :, 128 * c : 128 * (c + 1)], 2) for c in range(GROUPS)]
+        w1s = keep.tile([P, PASSES, H // 4], I32, name="w1s", align_bytes=64)
+        nc.gpsimd.memset(w1s[:], 0)
+        for quad in range(4):
+            rows = slice(32 * quad, 32 * quad + 4)
+            nc.vector.tensor_copy(
+                out=w1s[rows, :, :].rearrange("p a (c t b w) -> p (a c) t b w", t=4, b=16, w=2),
+                in_=w1s_raw[rows, :, :].rearrange("p a (c b t w) -> p (a c) t b w", t=4, b=16, w=2),
+            )
         w1w = [dealt("w1w0", w1w_first[:], 4)]
         v_words = keep.tile([P, PASSES, S], U32, name="v_words", align_bytes=64)
         nc.vector.tensor_copy(v_words[:, 0, :], table0[:].bitcast(U32).indirect(idx[:]))
@@ -122,6 +124,7 @@ def tile_list_replay_td_errors_kernel(
             )
         for c in range(1, GROUPS):
             w1w.append(dealt("w1w%d" % c, w1w_rest[:, :, 256 * (c - 1) : 256 * c], 4))
+
 
         def bank(name, n):
             return psum.tile([P, BANK], F32, name=name, offset=n * BANK_BYTES)
@@ -136,7 +139,7 @@ def tile_list_replay_td_errors_kernel(
                     nc.tensor.matmul_mx(
                         out=acc[:],
                         lhsT=w1w[c][:, a, 64 * t : 64 * (t + 1)].bitcast(U8).bitcast(FP4X4),
-                        lhsT_scale=w1s[c][:, a, 32 * t : 32 * (t + 1)].bitcast(U8),
+                        lhsT_scale=w1s[:, a, 128 * c + 32 * t : 128 * c + 32 * (t + 1)].bitcast(U8),
                         rhs=v_words[:, a, cols].bitcast(FP8X4),
                         rhs_scale=v_scales[:, a, :].bitcast(U8)[:, cols],
                         start=(a == 0),
@@ -192,8 +195,8 @@ def tile_list_replay_td_errors_kernel(
             pick_state(i, 0, PAIRS)
         for i in range(4 * LAST + 1, 4 * GROUPS):
             pick_succ(i)
-        w2_bf = keep.tile([P, GROUPS, N, 4], BF16, name="w2_bf", tag="w1s0", align_bytes=64)
         quantize_z(0, 0, PAIRS, False, "table0")
+        w2_bf = keep.tile([P, GROUPS, N, 4], BF16, name="w2_bf", tag="w1w0", align_bytes=64)
         for c in range(GROUPS):
             dst, src = interleaved(w2_bf[:, c, :, :], late[:, 4 * c : 4 * (c + 1), :])
             nc.scalar.activation(out=dst, in_=src, func=ACT.Copy)

@@ -50,52 +50,20 @@ def tile_list_replay_td_errors_kernel(
 
         ts_win = keep.tile([P, T // 4], I32, name="ts_win", align_bytes=64)
         nc.sync.dma_start(idx[:], offs)
+        w1w_hbm = w1_words.rearrange("a p c -> p a c").bitcast(I32)
+        w1w_first = shared.tile([P, PASSES, 256], I32, name="w1w_first", offset=15 * 1024, align_bytes=64)
+        nc.sync.dma_start(out=w1w_first[:], in_=w1w_hbm[:, :, 0:256])
         nc.sync.dma_start(out=ts_win[0:32, :], in_=tab_scales.rearrange("a q t -> (a q) t").bitcast(I32))
         nc.sync.dma_start(p2[:], pos2)
         nc.sync.dma_start(p1[:], pos1)
         table0 = keep.tile([P, T], I32, name="table0", tag="table0", align_bytes=64)
         nc.sync.dma_start(out=table0[:], in_=tab_words[0].rearrange("p t i -> p (t i)").bitcast(I32))
-        w1w_hbm = w1_words.rearrange("a p c -> p a c").bitcast(I32)
-        w1w_first = keep.tile([P, PASSES, 256], I32, name="w1w_first", align_bytes=64)
-        nc.scalar.dma_start(out=w1w_first[:], in_=w1w_hbm[:, :, 0:256])
         w1s_hbm = w1_scales.rearrange("a q c -> q a c").bitcast(I32)
         w1s_raw = keep.tile([P, PASSES, H // 4], I32, name="w1s_raw", align_bytes=64)
         for quad in range(4):
             nc.scalar.dma_start(
                 out=w1s_raw[32 * quad : 32 * quad + 4, :, :], in_=w1s_hbm[4 * quad : 4 * quad + 4, :, :]
             )
-
-        ones = keep.tile([P, 16], F32, name="ones", tag="win_table", align_bytes=64)
-        nc.vector.memset(ones[:], 1.0)
-        seed = keep.tile([P, 16], F32, name="seed")
-        nc.scalar.activation(out=seed[:], in_=ones[:], func=ACT.Tanh)
-        table1 = keep.tile([P, T], I32, name="table1", tag="win_table", align_bytes=64)
-        nc.sync.dma_start(out=table1[:], in_=tab_words[1].rearrange("p t i -> p (t i)").bitcast(I32))
-
-        nc.gpsimd.memset(ts_win[32:64, :], 0)
-        nc.vector.memset(ts_win[64:P, :], 0)
-        v_scales = keep.tile([P, PASSES, S // 4], I32, name="v_scales", align_bytes=64)
-        nc.vector.memset(v_scales[:], 0)
-
-        ts_picked = shared.tile([P, S], U8, name="ts_picked", offset=15 * 1024 + 512)
-        nc.vector.tensor_copy(ts_picked[:], ts_win[:].bitcast(U8).indirect(idx[:]))
-
-        nc.vector.tensor_copy(out=v_scales[0:4, 0, :], in_=ts_picked[0:4, :].bitcast(I32))
-        for n in range(1, 4 * PASSES):
-            a, quad = divmod(n, 4)
-            nc.scalar.dma_start(
-                out=v_scales[32 * quad : 32 * quad + 4, a, :], in_=ts_picked[4 * n : 4 * n + 4, :].bitcast(I32)
-            )
-
-        w1w_rest = shared.tile([P, PASSES, 512], I32, name="w1w_rest", offset=16 * 1024, align_bytes=64)
-        nc.sync.dma_start(out=w1w_rest[:], in_=w1w_hbm[:, :, 256:768])
-        late = shared.tile([P, 16, N], F32, name="late", offset=0)
-        for c in range(GROUPS):
-            rows = w2[512 * c : 512 * (c + 1), :].rearrange("(b t u) n -> t b u n", t=4, u=8)
-            for t in range(4):
-                nc.sync.dma_start(out=late[:, 4 * c + t, :], in_=rows[t])
-        rew_sb = late[:, 12:16, :].rearrange("p (m x) n -> p m (x n)", m=2)
-        nc.sync.dma_start(out=rew_sb, in_=rew.rearrange("(m p) j -> p m j", p=P))
 
         def dealt(name, raw, run):
             width = 64 * run
@@ -106,6 +74,35 @@ def tile_list_replay_td_errors_kernel(
             )
             return tile
 
+        w1w = [dealt("w1w0", w1w_first[:], 4)]
+        table1 = shared.tile([P, T], I32, name="table1", offset=0, align_bytes=64)
+        nc.sync.dma_start(out=table1[:], in_=tab_words[1].rearrange("p t i -> p (t i)").bitcast(I32))
+
+        nc.gpsimd.memset(ts_win[32:64, :], 0)
+        nc.vector.memset(ts_win[64:P, :], 0)
+        v_scales = keep.tile([P, PASSES, S // 4], I32, name="v_scales", align_bytes=64)
+        nc.vector.memset(v_scales[:], 0)
+
+        ts_picked = shared.tile([P, S], U8, name="ts_picked", offset=16 * 1024)
+        nc.vector.tensor_copy(ts_picked[:], ts_win[:].bitcast(U8).indirect(idx[:]))
+
+        nc.vector.tensor_copy(out=v_scales[0:4, 0, :], in_=ts_picked[0:4, :].bitcast(I32))
+        for n in range(1, 4 * PASSES):
+            a, quad = divmod(n, 4)
+            nc.scalar.dma_start(
+                out=v_scales[32 * quad : 32 * quad + 4, a, :], in_=ts_picked[4 * n : 4 * n + 4, :].bitcast(I32)
+            )
+
+        w1w_rest = shared.tile([P, PASSES, 512], I32, name="w1w_rest", offset=16 * 1024 + 512, align_bytes=64)
+        nc.sync.dma_start(out=w1w_rest[:], in_=w1w_hbm[:, :, 256:768])
+        late = shared.tile([P, 16, N], F32, name="late", offset=0)
+        for c in range(GROUPS):
+            rows = w2[512 * c : 512 * (c + 1), :].rearrange("(b t u) n -> t b u n", t=4, u=8)
+            for t in range(4):
+                nc.sync.dma_start(out=late[:, 4 * c + t, :], in_=rows[t])
+        rew_sb = late[:, 12:16, :].rearrange("p (m x) n -> p m (x n)", m=2)
+        nc.sync.dma_start(out=rew_sb, in_=rew.rearrange("(m p) j -> p m j", p=P))
+
         w1s = keep.tile([P, PASSES, H // 4], I32, name="w1s", align_bytes=64)
         nc.gpsimd.memset(w1s[:], 0)
         for quad in range(4):
@@ -114,7 +111,6 @@ def tile_list_replay_td_errors_kernel(
                 out=w1s[rows, :, :].rearrange("p a (c t b w) -> p (a c) t b w", t=4, b=16, w=2),
                 in_=w1s_raw[rows, :, :].rearrange("p a (c b t w) -> p (a c) t b w", t=4, b=16, w=2),
             )
-        w1w = [dealt("w1w0", w1w_first[:], 4)]
         v_words = keep.tile([P, PASSES, S], U32, name="v_words", align_bytes=64)
         nc.vector.tensor_copy(v_words[:, 0, :], table0[:].bitcast(U32).indirect(idx[:]))
         for half in range(2):

@@ -22,8 +22,10 @@ GROUPS = H // 512
 LAST = GROUPS - 1
 BANK = 512
 BANK_BYTES = 2048
-SPLIT = 256
+HALF = PAIRS // 2
 DISCOUNT = 0.99
+V_WORDS = S // 4
+W_WORDS = H // 4
 
 
 def interleaved(dst, src):
@@ -48,69 +50,60 @@ def tile_list_replay_td_errors_kernel(
         p1 = lists.tile([P, PAIRS // 16], U16, name="p1")
         p2 = lists.tile([P, PAIRS // 16], U16, name="p2")
 
-        ts_win = keep.tile([P, T // 4], I32, name="ts_win", align_bytes=64)
         nc.sync.dma_start(idx[:], offs)
+        ts_win = keep.tile([P, T // 4], I32, name="ts_win", align_bytes=64)
+        nc.scalar.dma_start(out=ts_win[0:32, :], in_=tab_scales.rearrange("a q t -> (a q) t").bitcast(I32))
+        w1s_raw = keep.tile([P, W_WORDS], I32, name="w1s_raw", align_bytes=64)
+        nc.scalar.dma_start(out=w1s_raw[0:32, :], in_=w1_scales.rearrange("a q c -> (a q) c").bitcast(I32))
         w1w_hbm = w1_words.rearrange("a p c -> p a c").bitcast(I32)
-        w1w_first = shared.tile([P, PASSES, 256], I32, name="w1w_first", offset=15 * 1024, align_bytes=64)
-        nc.sync.dma_start(out=w1w_first[:], in_=w1w_hbm[:, :, 0:256])
-        nc.sync.dma_start(out=ts_win[0:32, :], in_=tab_scales.rearrange("a q t -> (a q) t").bitcast(I32))
+        w1w_first = keep.tile([P, PASSES, 256], I32, name="w1w_first", align_bytes=64)
+        nc.scalar.dma_start(out=w1w_first[:], in_=w1w_hbm[:, :, 0:256])
         nc.sync.dma_start(p2[:], pos2)
         nc.sync.dma_start(p1[:], pos1)
         table0 = keep.tile([P, T], I32, name="table0", tag="table0", align_bytes=64)
         nc.sync.dma_start(out=table0[:], in_=tab_words[0].rearrange("p t i -> p (t i)").bitcast(I32))
-        w1s_hbm = w1_scales.rearrange("a q c -> q a c").bitcast(I32)
-        w1s_raw = keep.tile([P, PASSES, H // 4], I32, name="w1s_raw", align_bytes=64)
-        for quad in range(4):
-            nc.scalar.dma_start(
-                out=w1s_raw[32 * quad : 32 * quad + 4, :, :], in_=w1s_hbm[4 * quad : 4 * quad + 4, :, :]
-            )
-
-        def dealt(name, raw, run):
-            width = 64 * run
-            tile = keep.tile([P, PASSES, width], I32, name=name, tag=name, align_bytes=64)
-            nc.vector.tensor_copy(
-                out=tile[:].rearrange("p a (t b w) -> p a t b w", t=4, w=run),
-                in_=raw.rearrange("p a (b t w) -> p a t b w", t=4, w=run),
-            )
-            return tile
-
-        w1w = [dealt("w1w0", w1w_first[:], 4)]
         table1 = shared.tile([P, T], I32, name="table1", offset=0, align_bytes=64)
         nc.sync.dma_start(out=table1[:], in_=tab_words[1].rearrange("p t i -> p (t i)").bitcast(I32))
 
         nc.gpsimd.memset(ts_win[32:64, :], 0)
         nc.vector.memset(ts_win[64:P, :], 0)
-        v_scales = keep.tile([P, PASSES, S // 4], I32, name="v_scales", align_bytes=64)
-        nc.vector.memset(v_scales[:], 0)
+        planes = [keep.tile([P, V_WORDS + W_WORDS], I32, name="plane%d" % a, align_bytes=64) for a in range(PASSES)]
+        for a in range(PASSES):
+            nc.gpsimd.memset(planes[a][:], 0)
 
+        rows = keep.tile([P, V_WORDS + W_WORDS], I32, name="rows", align_bytes=64)
+        nc.vector.tensor_copy(
+            out=rows[0:32, V_WORDS:].rearrange("p (c t b w) -> p c t b w", t=4, b=16, w=2),
+            in_=w1s_raw[0:32, :].rearrange("p (c b t w) -> p c t b w", t=4, b=16, w=2),
+        )
         ts_picked = shared.tile([P, S], U8, name="ts_picked", offset=16 * 1024)
         nc.vector.tensor_copy(ts_picked[:], ts_win[:].bitcast(U8).indirect(idx[:]))
-
-        nc.vector.tensor_copy(out=v_scales[0:4, 0, :], in_=ts_picked[0:4, :].bitcast(I32))
+        nc.vector.tensor_copy(out=rows[0:32, 0:V_WORDS], in_=ts_picked[0:32, :].bitcast(I32))
+        nc.vector.tensor_copy(out=planes[0][0:4, :], in_=rows[0:4, :])
         for n in range(1, 4 * PASSES):
             a, quad = divmod(n, 4)
-            nc.scalar.dma_start(
-                out=v_scales[32 * quad : 32 * quad + 4, a, :], in_=ts_picked[4 * n : 4 * n + 4, :].bitcast(I32)
-            )
+            queue = nc.scalar if a == 0 else nc.sync
+            queue.dma_start(out=planes[a][32 * quad : 32 * quad + 4, :], in_=rows[4 * n : 4 * n + 4, :])
 
-        w1w_rest = shared.tile([P, PASSES, 512], I32, name="w1w_rest", offset=16 * 1024 + 512, align_bytes=64)
+        w1w_rest = shared.tile([P, PASSES, 512], I32, name="w1w_rest", offset=16 * 1024, align_bytes=64)
         nc.sync.dma_start(out=w1w_rest[:], in_=w1w_hbm[:, :, 256:768])
         late = shared.tile([P, 16, N], F32, name="late", offset=0)
         for c in range(GROUPS):
-            rows = w2[512 * c : 512 * (c + 1), :].rearrange("(b t u) n -> t b u n", t=4, u=8)
+            w2_rows = w2[512 * c : 512 * (c + 1), :].rearrange("(b t u) n -> t b u n", t=4, u=8)
             for t in range(4):
-                nc.sync.dma_start(out=late[:, 4 * c + t, :], in_=rows[t])
+                nc.sync.dma_start(out=late[:, 4 * c + t, :], in_=w2_rows[t])
         rew_sb = late[:, 12:16, :].rearrange("p (m x) n -> p m (x n)", m=2)
         nc.sync.dma_start(out=rew_sb, in_=rew.rearrange("(m p) j -> p m j", p=P))
 
-        w1s = keep.tile([P, PASSES, H // 4], I32, name="w1s", align_bytes=64)
-        nc.gpsimd.memset(w1s[:], 0)
-        for quad in range(4):
-            rows = slice(32 * quad, 32 * quad + 4)
+        def dealt(name, raw, t0, t1):
+            tile = keep.tile([P, PASSES, 64 * (t1 - t0)], I32, name=name, tag=name, align_bytes=64)
             nc.vector.tensor_copy(
-                out=w1s[rows, :, :].rearrange("p a (c t b w) -> p (a c) t b w", t=4, b=16, w=2),
-                in_=w1s_raw[rows, :, :].rearrange("p a (c b t w) -> p (a c) t b w", t=4, b=16, w=2),
+                out=tile[:].rearrange("p a (t b w) -> p a t b w", b=16, w=4),
+                in_=raw.rearrange("p a (b t w) -> p a t b w", t=4, w=4)[:, :, t0:t1],
             )
+            return [tile[:, :, 64 * t : 64 * (t + 1)] for t in range(t1 - t0)]
+
+        w1w = dealt("w1w0", w1w_first[:], 0, 4)
         v_words = keep.tile([P, PASSES, S], U32, name="v_words", align_bytes=64)
         nc.vector.tensor_copy(v_words[:, 0, :], table0[:].bitcast(U32).indirect(idx[:]))
         for half in range(2):
@@ -119,35 +112,38 @@ def tile_list_replay_td_errors_kernel(
                 table1[:].bitcast(U32).indirect(idx[:, 32 * half : 32 * (half + 1)]),
             )
         for c in range(1, GROUPS):
-            w1w.append(dealt("w1w%d" % c, w1w_rest[:, :, 256 * (c - 1) : 256 * c], 4))
-
+            raw = w1w_rest[:, :, 256 * (c - 1) : 256 * c]
+            w1w.extend(dealt("w1a%d" % c, raw, 0, 2))
+            w1w.extend(dealt("w1b%d" % c, raw, 2, 4))
 
         def bank(name, n):
             return psum.tile([P, BANK], F32, name=name, offset=n * BANK_BYTES)
 
         hs = [keep.tile([P, 2 * S], F32, name="h%d" % i) for i in range(4 * GROUPS)]
 
-        def hidden_tile(c, t):
+        def hidden_tile(i):
             for half in range(2):
                 cols = slice(BANK * half, BANK * (half + 1))
-                acc = bank("acc%d_%d_%d" % (c, t, half), (t + 2 * half - 1) % 4)
+                acc = bank("acc%d_%d" % (i, half), (i + 2 * half - 1) % 4)
                 for a in range(PASSES):
                     nc.tensor.matmul_mx(
                         out=acc[:],
-                        lhsT=w1w[c][:, a, 64 * t : 64 * (t + 1)].bitcast(U8).bitcast(FP4X4),
-                        lhsT_scale=w1s[:, a, 128 * c + 32 * t : 128 * c + 32 * (t + 1)].bitcast(U8),
+                        lhsT=w1w[i][:, a, :].bitcast(U8).bitcast(FP4X4),
+                        lhsT_scale=planes[a][:, V_WORDS + 32 * i : V_WORDS + 32 * (i + 1)].bitcast(U8),
                         rhs=v_words[:, a, cols].bitcast(FP8X4),
-                        rhs_scale=v_scales[:, a, :].bitcast(U8)[:, cols],
+                        rhs_scale=planes[a][:, 0:V_WORDS].bitcast(U8)[:, cols],
                         start=(a == 0),
                         stop=(a == PASSES - 1),
                     )
-                nc.scalar.activation(out=hs[4 * c + t][:, cols], in_=acc[:], func=ACT.Relu)
+                nc.scalar.activation(out=hs[i][:, cols], in_=acc[:], func=ACT.Relu)
 
         w2_codes = keep.tile([P, GROUPS, N], U32, name="w2_codes", align_bytes=64)
         w2_scales = keep.tile([P, GROUPS, N], U8, name="w2_scales", align_bytes=64)
         z_codes = keep.tile([P, GROUPS, PAIRS], U32, name="z_codes", align_bytes=64)
         z_scales = keep.tile([P, GROUPS, PAIRS], U8, name="z_scales", align_bytes=64)
         succ = [keep.tile([P, 4, PAIRS], F32, name="succ", bufs=2) for c in range(GROUPS)]
+        w2_bf = keep.tile([P, GROUPS, N, 4], BF16, name="w2_bf", tag="table0", align_bytes=64)
+        z_bf = [keep.tile([P, PAIRS, 4], BF16, name="z_bf%d" % c, align_bytes=64) for c in range(GROUPS)]
         z = []
 
         def pick_succ(i):
@@ -166,60 +162,71 @@ def tile_list_replay_td_errors_kernel(
                 z[c][:, t, j0:j1], hs[i][:].indirect(p1[:, j0 // 16 : j1 // 16]), succ[c][:, t, j0:j1], ALU.add
             )
 
-        def quantize_z(c, j0, j1, on_vector, tag):
-            z_bf = keep.tile([P, j1 - j0, 4], BF16, name="z_bf", tag=tag, align_bytes=64)
-            dst, src = interleaved(z_bf[:], z[c][:, :, j0:j1])
+        def round_z(c, j0, j1, on_vector):
+            dst, src = interleaved(z_bf[c][:, j0:j1, :], z[c][:, :, j0:j1])
             if on_vector:
                 nc.vector.tensor_copy(out=dst, in_=src)
             else:
                 nc.scalar.activation(out=dst, in_=src, func=ACT.Copy)
+
+        def quantize_z(c, j0, j1):
             nc.vector.quantize_mx(
                 out=z_codes[:, c, j0:j1].bitcast(FP8X4),
                 scales=z_scales[:, c, j0:j1],
-                in_=z_bf[:].rearrange("p j t -> p (j t)"),
+                in_=z_bf[c][:, j0:j1, :].rearrange("p j t -> p (j t)"),
             )
 
-        for c in range(GROUPS):
-            for t in range(4):
-                hidden_tile(c, t)
-
-        for c in range(LAST):
-            z.append(keep.tile([P, 4, PAIRS], F32, name="z", tag="w1w%d" % c, align_bytes=64))
-        pick_succ(0)
-        for i in range(4 * LAST):
-            pick_succ(i + 1)
-            pick_state(i, 0, PAIRS)
-        for i in range(4 * LAST + 1, 4 * GROUPS):
-            pick_succ(i)
-        quantize_z(0, 0, PAIRS, False, "table0")
-        w2_bf = keep.tile([P, GROUPS, N, 4], BF16, name="w2_bf", tag="w1w0", align_bytes=64)
-        for c in range(GROUPS):
+        def round_w2(c):
             dst, src = interleaved(w2_bf[:, c, :, :], late[:, 4 * c : 4 * (c + 1), :])
             nc.scalar.activation(out=dst, in_=src, func=ACT.Copy)
+
+        def quantize_w2(c):
             nc.vector.quantize_mx(
                 out=w2_codes[:, c, :].bitcast(FP8X4),
                 scales=w2_scales[:, c, :],
                 in_=w2_bf[:, c, :, :].rearrange("p n t -> p (n t)"),
             )
-        quantize_z(1, 0, PAIRS, False, "win_table")
-        z.append(keep.tile([P, 4, PAIRS], F32, name="z", tag="win_table", align_bytes=64))
-        pieces = ((0, 256), (256, 384), (384, 512))
-        for j0, j1 in pieces:
+
+        for i in range(4 * GROUPS):
+            hidden_tile(i)
+
+        for c in range(LAST):
+            z.append(keep.tile([P, 4, PAIRS], F32, name="z", tag="w1a%d" % (c + 1), align_bytes=64))
             for t in range(4):
-                pick_state(4 * LAST + t, j0, j1)
-        for j0, j1 in pieces:
-            quantize_z(LAST, j0, j1, j1 == PAIRS, "z_last%d" % j0)
+                pick_succ(4 * c + t)
+            for t in range(4):
+                pick_state(4 * c + t, 0, PAIRS)
+        for t in range(4):
+            pick_succ(4 * LAST + t)
+        for c in range(LAST):
+            round_w2(c)
+            quantize_w2(c)
+            round_z(c, 0, PAIRS, False)
+            quantize_z(c, 0, PAIRS)
+        round_w2(LAST)
+        z.append(keep.tile([P, 4, PAIRS], F32, name="z", tag="w1a%d" % LAST, align_bytes=64))
+        for t in range(2):
+            pick_state(4 * LAST + t, 0, PAIRS)
+        for half in range(2):
+            for t in range(2, 4):
+                pick_state(4 * LAST + t, HALF * half, HALF * (half + 1))
+        quantize_w2(LAST)
+        round_z(LAST, 0, HALF, False)
+        round_z(LAST, HALF, 384, False)
+        round_z(LAST, 384, PAIRS, True)
+        for half in range(2):
+            quantize_z(LAST, HALF * half, HALF * (half + 1))
 
         out_v = out.rearrange("(m p) j -> p m j", p=P)
         for half in range(2):
-            cols = slice(SPLIT * half, SPLIT * (half + 1))
-            err = ring.tile([P, 2, SPLIT], F32, name="err")
-            res = ring.tile([P, 2, SPLIT], F32, name="res")
+            cols = slice(HALF * half, HALF * (half + 1))
+            err = ring.tile([P, 2, HALF], F32, name="err")
+            res = ring.tile([P, 2, HALF], F32, name="res")
             d = [bank("d%d_%d" % (half, m), 4 + 2 * half + m) for m in range(2)]
             for c in range(GROUPS):
                 for m in range(2):
                     nc.tensor.matmul_mx(
-                        out=d[m][:, 0:SPLIT],
+                        out=d[m][:, 0:HALF],
                         lhsT=w2_codes[:, c, P * m : P * (m + 1)].bitcast(FP8X4),
                         lhsT_scale=w2_scales[:, c, P * m : P * (m + 1)],
                         rhs=z_codes[:, c, cols].bitcast(FP8X4),
@@ -229,7 +236,7 @@ def tile_list_replay_td_errors_kernel(
                     )
             for m in range(2):
                 nc.vector.tensor_tensor(
-                    out=err[:, m, :], in0=rew_sb[:, m, cols], in1=d[m][:, 0:SPLIT], op=ALU.subtract
+                    out=err[:, m, :], in0=rew_sb[:, m, cols], in1=d[m][:, 0:HALF], op=ALU.subtract
                 )
                 nc.scalar.activation(out=res[:, m, :], in_=err[:, m, :], func=ACT.Tanh)
                 nc.sync.dma_start(out=out_v[:, m, cols], in_=res[:, m, :])

@@ -24,8 +24,10 @@ BANK = 512
 BANK_BYTES = 2048
 HALF = PAIRS // 2
 DISCOUNT = 0.99
+KIB = 1024
 V_WORDS = S // 4
-W_WORDS = H // 4
+G_WORDS = 512 // 4
+W_WORDS = GROUPS * G_WORDS
 
 
 def interleaved(dst, src):
@@ -60,90 +62,141 @@ def tile_list_replay_td_errors_kernel(
         nc.scalar.dma_start(out=w1w_first[:], in_=w1w_hbm[:, :, 0:256])
         nc.sync.dma_start(p2[:], pos2)
         nc.sync.dma_start(p1[:], pos1)
-        table0 = keep.tile([P, T], I32, name="table0", tag="table0", align_bytes=64)
+        table0 = shared.tile([P, T], I32, name="table0", offset=33 * KIB, align_bytes=64)
         nc.sync.dma_start(out=table0[:], in_=tab_words[0].rearrange("p t i -> p (t i)").bitcast(I32))
-        table1 = shared.tile([P, T], I32, name="table1", offset=0, align_bytes=64)
+        table1 = shared.tile([P, T], I32, name="table1", offset=8 * KIB, align_bytes=64)
         nc.sync.dma_start(out=table1[:], in_=tab_words[1].rearrange("p t i -> p (t i)").bitcast(I32))
 
         nc.gpsimd.memset(ts_win[32:64, :], 0)
         nc.vector.memset(ts_win[64:P, :], 0)
-        planes = [keep.tile([P, V_WORDS + W_WORDS], I32, name="plane%d" % a, align_bytes=64) for a in range(PASSES)]
+        planes = [keep.tile([P, V_WORDS + G_WORDS], I32, name="plane%d" % a, align_bytes=64) for a in range(PASSES)]
+        planes_rest = keep.tile([P, PASSES, LAST * G_WORDS], I32, name="planes_rest", align_bytes=64)
         for a in range(PASSES):
             nc.gpsimd.memset(planes[a][:], 0)
+        nc.gpsimd.memset(planes_rest[:], 0)
 
-        rows = keep.tile([P, V_WORDS + W_WORDS], I32, name="rows", align_bytes=64)
-        nc.vector.tensor_copy(
-            out=rows[0:32, V_WORDS:].rearrange("p (c t b w) -> p c t b w", t=4, b=16, w=2),
-            in_=w1s_raw[0:32, :].rearrange("p (c b t w) -> p c t b w", t=4, b=16, w=2),
-        )
-        ts_picked = shared.tile([P, S], U8, name="ts_picked", offset=16 * 1024)
+        def deal_scales(dst, src):
+            nc.vector.tensor_copy(
+                out=dst.rearrange("p (c t b w) -> p c t b w", t=4, b=16, w=2),
+                in_=src.rearrange("p (c b t w) -> p c t b w", t=4, b=16, w=2),
+            )
+
+        def move_rows(dst, rows):
+            nc.vector.tensor_copy(out=dst[0][0:4, :], in_=rows[0:4, :])
+            for n in range(1, 4 * PASSES):
+                a, quad = divmod(n, 4)
+                queue = nc.scalar if a == 0 else nc.sync
+                queue.dma_start(out=dst[a][32 * quad : 32 * quad + 4, :], in_=rows[4 * n : 4 * n + 4, :])
+
+        rows = keep.tile([P, V_WORDS + G_WORDS], I32, name="rows", align_bytes=64)
+        deal_scales(rows[0:32, V_WORDS:], w1s_raw[0:32, 0:G_WORDS])
+        ts_picked = keep.tile([P, S], U8, name="ts_picked", align_bytes=64)
         nc.vector.tensor_copy(ts_picked[:], ts_win[:].bitcast(U8).indirect(idx[:]))
         nc.vector.tensor_copy(out=rows[0:32, 0:V_WORDS], in_=ts_picked[0:32, :].bitcast(I32))
-        nc.vector.tensor_copy(out=planes[0][0:4, :], in_=rows[0:4, :])
+        move_rows(planes, rows)
+
+        w1w_rest = []
+        for c in range(1, GROUPS):
+            offset = 33 * KIB + 2 * KIB * (c - 1)
+            w1w_rest.append(shared.tile([P, PASSES, 256], I32, name="w1w_rest%d" % c, offset=offset, align_bytes=64))
+            nc.sync.dma_start(out=w1w_rest[-1][:], in_=w1w_hbm[:, :, 256 * c : 256 * (c + 1)])
+        rows_rest = shared.tile([P, LAST * G_WORDS], I32, name="rows_rest", offset=47 * KIB, align_bytes=64)
+        deal_scales(rows_rest[0:32, :], w1s_raw[0:32, G_WORDS:])
+        nc.vector.tensor_copy(out=planes_rest[0:4, 0, :], in_=rows_rest[0:4, :])
         for n in range(1, 4 * PASSES):
             a, quad = divmod(n, 4)
-            queue = nc.scalar if a == 0 else nc.sync
-            queue.dma_start(out=planes[a][32 * quad : 32 * quad + 4, :], in_=rows[4 * n : 4 * n + 4, :])
-
-        w1w_rest = shared.tile([P, PASSES, 512], I32, name="w1w_rest", offset=16 * 1024, align_bytes=64)
-        nc.sync.dma_start(out=w1w_rest[:], in_=w1w_hbm[:, :, 256:768])
-        late = shared.tile([P, 16, N], F32, name="late", offset=0)
+            nc.sync.dma_start(out=planes_rest[32 * quad : 32 * quad + 4, a, :], in_=rows_rest[4 * n : 4 * n + 4, :])
+        late = shared.tile([P, 12, N], F32, name="late", offset=12 * KIB - 128)
         for c in range(GROUPS):
             w2_rows = w2[512 * c : 512 * (c + 1), :].rearrange("(b t u) n -> t b u n", t=4, u=8)
             for t in range(4):
                 nc.sync.dma_start(out=late[:, 4 * c + t, :], in_=w2_rows[t])
-        rew_sb = late[:, 12:16, :].rearrange("p (m x) n -> p m (x n)", m=2)
-        nc.sync.dma_start(out=rew_sb, in_=rew.rearrange("(m p) j -> p m j", p=P))
+        rew_sb = shared.tile([P, 2, PAIRS], F32, name="rew_sb", offset=37 * KIB)
+        nc.sync.dma_start(out=rew_sb[:], in_=rew.rearrange("(m p) j -> p m j", p=P))
 
-        def dealt(name, raw, t0, t1):
-            tile = keep.tile([P, PASSES, 64 * (t1 - t0)], I32, name=name, tag=name, align_bytes=64)
+        def dealt(tile, raw, t0, t1):
             nc.vector.tensor_copy(
                 out=tile[:].rearrange("p a (t b w) -> p a t b w", b=16, w=4),
                 in_=raw.rearrange("p a (b t w) -> p a t b w", t=4, w=4)[:, :, t0:t1],
             )
             return [tile[:, :, 64 * t : 64 * (t + 1)] for t in range(t1 - t0)]
 
-        w1w = dealt("w1w0", w1w_first[:], 0, 4)
-        v_words = keep.tile([P, PASSES, S], U32, name="v_words", align_bytes=64)
-        nc.vector.tensor_copy(v_words[:, 0, :], table0[:].bitcast(U32).indirect(idx[:]))
+        w1w_0 = keep.tile([P, PASSES, 256], I32, name="w1w_0", align_bytes=64)
+        w1w = dealt(w1w_0, w1w_first[:], 0, 4)
+        v0 = keep.tile([P, S], U32, name="v0", align_bytes=64)
+        nc.vector.tensor_copy(v0[:], table0[:].bitcast(U32).indirect(idx[:]))
+        v_words = [[v0[:, 0:BANK], v0[:, BANK:S]], []]
         for half in range(2):
-            nc.vector.tensor_copy(
-                v_words[:, 1, BANK * half : BANK * (half + 1)],
-                table1[:].bitcast(U32).indirect(idx[:, 32 * half : 32 * (half + 1)]),
-            )
-        for c in range(1, GROUPS):
-            raw = w1w_rest[:, :, 256 * (c - 1) : 256 * c]
-            w1w.extend(dealt("w1a%d" % c, raw, 0, 2))
-            w1w.extend(dealt("w1b%d" % c, raw, 2, 4))
+            v1 = keep.tile([P, BANK], U32, name="v1_%d" % half, align_bytes=64)
+            nc.vector.tensor_copy(v1[:], table1[:].bitcast(U32).indirect(idx[:, 32 * half : 32 * (half + 1)]))
+            v_words[1].append(v1[:])
+        for c, t0, t1, offset in ((1, 0, 2, 24 * KIB - 64), (1, 2, 4, 9 * KIB), (2, 0, 2, 7 * KIB + 64), (2, 2, 4, 10 * KIB)):
+            name = "w1w%d_%d" % (c, t0)
+            tile = shared.tile([P, PASSES, 64 * (t1 - t0)], I32, name=name, offset=offset, align_bytes=64)
+            w1w.extend(dealt(tile, w1w_rest[c - 1][:], t0, t1))
 
         def bank(name, n):
             return psum.tile([P, BANK], F32, name=name, offset=n * BANK_BYTES)
 
+        idle = bank("idle", 4)
+        for n in range(5):
+            nc.tensor.matmul_mx(
+                out=idle[:],
+                lhsT=w1w[0][:, 0, :].bitcast(U8).bitcast(FP4X4),
+                lhsT_scale=ts_picked[:, 0:P],
+                rhs=v_words[0][0].bitcast(FP8X4),
+                rhs_scale=ts_picked[:, 0:BANK],
+                start=True,
+                stop=True,
+            )
+
         hs = [keep.tile([P, 2 * S], F32, name="h%d" % i) for i in range(4 * GROUPS)]
 
-        def hidden_tile(i):
-            for half in range(2):
-                cols = slice(BANK * half, BANK * (half + 1))
-                acc = bank("acc%d_%d" % (i, half), (i + 2 * half - 1) % 4)
-                for a in range(PASSES):
-                    nc.tensor.matmul_mx(
-                        out=acc[:],
-                        lhsT=w1w[i][:, a, :].bitcast(U8).bitcast(FP4X4),
-                        lhsT_scale=planes[a][:, V_WORDS + 32 * i : V_WORDS + 32 * (i + 1)].bitcast(U8),
-                        rhs=v_words[:, a, cols].bitcast(FP8X4),
-                        rhs_scale=planes[a][:, 0:V_WORDS].bitcast(U8)[:, cols],
-                        start=(a == 0),
-                        stop=(a == PASSES - 1),
-                    )
-                nc.scalar.activation(out=hs[i][:, cols], in_=acc[:], func=ACT.Relu)
+        def hidden_pass(acc, i, a, j0, width, start, stop):
+            if i < 4:
+                w1_plane = planes[a][:, V_WORDS + 32 * i : V_WORDS + 32 * (i + 1)]
+            else:
+                w1_plane = planes_rest[:, a, 32 * (i - 4) : 32 * (i - 3)]
+            half, j = divmod(j0, BANK)
+            nc.tensor.matmul_mx(
+                out=acc,
+                lhsT=w1w[i][:, a, :].bitcast(U8).bitcast(FP4X4),
+                lhsT_scale=w1_plane.bitcast(U8),
+                rhs=v_words[a][half][:, j : j + width].bitcast(FP8X4),
+                rhs_scale=planes[a][:, 0:V_WORDS].bitcast(U8)[:, j0 : j0 + width],
+                start=start,
+                stop=stop,
+            )
 
-        w2_codes = keep.tile([P, GROUPS, N], U32, name="w2_codes", align_bytes=64)
-        w2_scales = keep.tile([P, GROUPS, N], U8, name="w2_scales", align_bytes=64)
-        z_codes = keep.tile([P, GROUPS, PAIRS], U32, name="z_codes", align_bytes=64)
-        z_scales = keep.tile([P, GROUPS, PAIRS], U8, name="z_scales", align_bytes=64)
+        def first_tile():
+            low = bank("acc0_0", 0)
+            high = [bank("acc0_1", 1), bank("acc0_2", 3)]
+            for a in range(PASSES):
+                hidden_pass(low[:], 0, a, 0, BANK, a == 0, a == 1)
+                if a == 1:
+                    nc.scalar.activation(out=hs[0][:, 0:BANK], in_=low[:], func=ACT.Relu)
+                for n in range(2):
+                    j0 = BANK + 256 * n
+                    for k in range(2):
+                        acc = high[n][:, P * k : P * (k + 1)]
+                        hidden_pass(acc, 0, a, j0 + P * k, P, a == 0 and k == 0, a == 1 and k == 1)
+                    if a == 1:
+                        nc.scalar.activation(out=hs[0][:, j0 : j0 + 256], in_=high[n][:, 0:256], func=ACT.Relu)
+
+        def hidden_tile(i):
+            for half in (1, 0):
+                acc = bank("acc%d_%d" % (i, half), (2, 0, 1, 3)[(2 * i - 1 - half) % 4])
+                for a in (1, 0):
+                    hidden_pass(acc[:], i, a, BANK * half, BANK, a == 1, a == 0)
+                nc.scalar.activation(out=hs[i][:, BANK * half : BANK * (half + 1)], in_=acc[:], func=ACT.Relu)
+
+        w2_codes = keep.tile([P, GROUPS * N], U32, name="w2_codes", align_bytes=64)
+        w2_scales = keep.tile([P, GROUPS * N], U8, name="w2_scales", align_bytes=64)
+        z_codes = keep.tile([P, GROUPS * PAIRS], U32, name="z_codes", align_bytes=64)
+        z_scales = keep.tile([P, GROUPS * PAIRS], U8, name="z_scales", align_bytes=64)
         succ = [keep.tile([P, 4, PAIRS], F32, name="succ", bufs=2) for c in range(GROUPS)]
-        w2_bf = keep.tile([P, GROUPS, N, 4], BF16, name="w2_bf", tag="table0", align_bytes=64)
-        z_bf = [keep.tile([P, PAIRS, 4], BF16, name="z_bf%d" % c, align_bytes=64) for c in range(GROUPS)]
+        w2_bf = shared.tile([P, GROUPS, N, 4], BF16, name="w2_bf", offset=41 * KIB, align_bytes=64)
+        z_bf = keep.tile([P, GROUPS * PAIRS, 4], BF16, name="z_bf", align_bytes=64)
         z = []
 
         def pick_succ(i):
@@ -163,35 +216,36 @@ def tile_list_replay_td_errors_kernel(
             )
 
         def round_z(c, j0, j1, on_vector):
-            dst, src = interleaved(z_bf[c][:, j0:j1, :], z[c][:, :, j0:j1])
+            dst, src = interleaved(z_bf[:, PAIRS * c + j0 : PAIRS * c + j1, :], z[c][:, :, j0:j1])
             if on_vector:
                 nc.vector.tensor_copy(out=dst, in_=src)
             else:
                 nc.scalar.activation(out=dst, in_=src, func=ACT.Copy)
 
-        def quantize_z(c, j0, j1):
+        def quantize_z(x0, x1):
             nc.vector.quantize_mx(
-                out=z_codes[:, c, j0:j1].bitcast(FP8X4),
-                scales=z_scales[:, c, j0:j1],
-                in_=z_bf[c][:, j0:j1, :].rearrange("p j t -> p (j t)"),
+                out=z_codes[:, x0:x1].bitcast(FP8X4),
+                scales=z_scales[:, x0:x1],
+                in_=z_bf[:, x0:x1, :].rearrange("p j t -> p (j t)"),
             )
 
         def round_w2(c):
             dst, src = interleaved(w2_bf[:, c, :, :], late[:, 4 * c : 4 * (c + 1), :])
             nc.scalar.activation(out=dst, in_=src, func=ACT.Copy)
 
-        def quantize_w2(c):
+        def quantize_w2(c0, c1):
             nc.vector.quantize_mx(
-                out=w2_codes[:, c, :].bitcast(FP8X4),
-                scales=w2_scales[:, c, :],
-                in_=w2_bf[:, c, :, :].rearrange("p n t -> p (n t)"),
+                out=w2_codes[:, N * c0 : N * c1].bitcast(FP8X4),
+                scales=w2_scales[:, N * c0 : N * c1],
+                in_=w2_bf[:, c0:c1, :, :].rearrange("p c n t -> p (c n t)"),
             )
 
-        for i in range(4 * GROUPS):
+        first_tile()
+        for i in range(1, 4 * GROUPS):
             hidden_tile(i)
 
         for c in range(LAST):
-            z.append(keep.tile([P, 4, PAIRS], F32, name="z", tag="w1a%d" % (c + 1), align_bytes=64))
+            z.append(shared.tile([P, 4, PAIRS], F32, name="z%d" % c, offset=(24 * KIB + 512, 0)[c], align_bytes=64))
             for t in range(4):
                 pick_succ(4 * c + t)
             for t in range(4):
@@ -200,22 +254,23 @@ def tile_list_replay_td_errors_kernel(
             pick_succ(4 * LAST + t)
         for c in range(LAST):
             round_w2(c)
-            quantize_w2(c)
+        quantize_w2(0, LAST)
+        for c in range(LAST):
             round_z(c, 0, PAIRS, False)
-            quantize_z(c, 0, PAIRS)
+        quantize_z(0, LAST * PAIRS)
         round_w2(LAST)
-        z.append(keep.tile([P, 4, PAIRS], F32, name="z", tag="w1a%d" % LAST, align_bytes=64))
+        z.append(shared.tile([P, 4, PAIRS], F32, name="z%d" % LAST, offset=0, align_bytes=64))
         for t in range(2):
             pick_state(4 * LAST + t, 0, PAIRS)
         for half in range(2):
             for t in range(2, 4):
                 pick_state(4 * LAST + t, HALF * half, HALF * (half + 1))
-        quantize_w2(LAST)
+        quantize_w2(LAST, GROUPS)
         round_z(LAST, 0, HALF, False)
         round_z(LAST, HALF, 384, False)
         round_z(LAST, 384, PAIRS, True)
         for half in range(2):
-            quantize_z(LAST, HALF * half, HALF * (half + 1))
+            quantize_z(PAIRS * LAST + HALF * half, PAIRS * LAST + HALF * (half + 1))
 
         out_v = out.rearrange("(m p) j -> p m j", p=P)
         for half in range(2):
@@ -224,13 +279,15 @@ def tile_list_replay_td_errors_kernel(
             res = ring.tile([P, 2, HALF], F32, name="res")
             d = [bank("d%d_%d" % (half, m), 4 + 2 * half + m) for m in range(2)]
             for c in range(GROUPS):
+                pairs = slice(PAIRS * c + HALF * half, PAIRS * c + HALF * (half + 1))
                 for m in range(2):
+                    heads = slice(N * c + P * m, N * c + P * (m + 1))
                     nc.tensor.matmul_mx(
                         out=d[m][:, 0:HALF],
-                        lhsT=w2_codes[:, c, P * m : P * (m + 1)].bitcast(FP8X4),
-                        lhsT_scale=w2_scales[:, c, P * m : P * (m + 1)],
-                        rhs=z_codes[:, c, cols].bitcast(FP8X4),
-                        rhs_scale=z_scales[:, c, cols],
+                        lhsT=w2_codes[:, heads].bitcast(FP8X4),
+                        lhsT_scale=w2_scales[:, heads],
+                        rhs=z_codes[:, pairs].bitcast(FP8X4),
+                        rhs_scale=z_scales[:, pairs],
                         start=(c == 0),
                         stop=(c == LAST),
                     )
@@ -239,4 +296,5 @@ def tile_list_replay_td_errors_kernel(
                     out=err[:, m, :], in0=rew_sb[:, m, cols], in1=d[m][:, 0:HALF], op=ALU.subtract
                 )
                 nc.scalar.activation(out=res[:, m, :], in_=err[:, m, :], func=ACT.Tanh)
-                nc.sync.dma_start(out=out_v[:, m, cols], in_=res[:, m, :])
+                queue = nc.scalar if (half, m) == (1, 1) else nc.sync
+                queue.dma_start(out=out_v[:, m, cols], in_=res[:, m, :])

@@ -138,18 +138,6 @@ def tile_list_replay_td_errors_kernel(
         def bank(name, n):
             return psum.tile([P, BANK], F32, name=name, offset=n * BANK_BYTES)
 
-        idle = bank("idle", 4)
-        for n in range(5):
-            nc.tensor.matmul_mx(
-                out=idle[:],
-                lhsT=w1w[0][:, 0, :].bitcast(U8).bitcast(FP4X4),
-                lhsT_scale=ts_picked[:, 0:P],
-                rhs=v_words[0][0].bitcast(FP8X4),
-                rhs_scale=ts_picked[:, 0:BANK],
-                start=True,
-                stop=True,
-            )
-
         hs = [keep.tile([P, 2 * S], F32, name="h%d" % i) for i in range(4 * GROUPS)]
 
         def hidden_pass(acc, i, a, j0, width, start, stop):

@@ -85,7 +85,7 @@ def tile_list_replay_td_errors_kernel(
             nc.vector.tensor_copy(out=dst[0][0:4, :], in_=rows[0:4, :])
             for n in range(1, 4 * PASSES):
                 a, quad = divmod(n, 4)
-                queue = nc.scalar if a == 0 else nc.sync
+                queue = nc.gpsimd if a == 0 else nc.sync
                 queue.dma_start(out=dst[a][32 * quad : 32 * quad + 4, :], in_=rows[4 * n : 4 * n + 4, :])
 
         rows = keep.tile([P, V_WORDS + G_WORDS], I32, name="rows", align_bytes=64)

@@ -58,14 +58,15 @@ def tile_list_replay_td_errors_kernel(
         w1s_raw = keep.tile([P, W_WORDS], I32, name="w1s_raw", align_bytes=64)
         nc.scalar.dma_start(out=w1s_raw[0:32, :], in_=w1_scales.rearrange("a q c -> (a q) c").bitcast(I32))
         w1w_hbm = w1_words.rearrange("a p c -> p a c").bitcast(I32)
-        w1w_first = keep.tile([P, PASSES, 256], I32, name="w1w_first", align_bytes=64)
-        nc.scalar.dma_start(out=w1w_first[:], in_=w1w_hbm[:, :, 0:256])
+        w1w_first = [keep.tile([P, 1, 256], I32, name="w1w_first%d" % a, align_bytes=64) for a in range(PASSES)]
+        nc.scalar.dma_start(out=w1w_first[0][:], in_=w1w_hbm[:, 0:1, 0:256])
         nc.sync.dma_start(p2[:], pos2)
         nc.sync.dma_start(p1[:], pos1)
         table0 = shared.tile([P, T], I32, name="table0", offset=33 * KIB, align_bytes=64)
         nc.sync.dma_start(out=table0[:], in_=tab_words[0].rearrange("p t i -> p (t i)").bitcast(I32))
         table1 = shared.tile([P, T], I32, name="table1", offset=8 * KIB, align_bytes=64)
         nc.sync.dma_start(out=table1[:], in_=tab_words[1].rearrange("p t i -> p (t i)").bitcast(I32))
+        nc.sync.dma_start(out=w1w_first[1][:], in_=w1w_hbm[:, 1:2, 0:256])
 
         nc.gpsimd.memset(ts_win[32:64, :], 0)
         nc.vector.memset(ts_win[64:P, :], 0)
@@ -85,7 +86,7 @@ def tile_list_replay_td_errors_kernel(
             nc.vector.tensor_copy(out=dst[0][0:4, :], in_=rows[0:4, :])
             for n in range(1, 4 * PASSES):
                 a, quad = divmod(n, 4)
-                queue = nc.gpsimd if a == 0 else nc.sync
+                queue = nc.gpsimd if n == 1 else nc.scalar if a == 0 else nc.sync
                 queue.dma_start(out=dst[a][32 * quad : 32 * quad + 4, :], in_=rows[4 * n : 4 * n + 4, :])
 
         rows = keep.tile([P, V_WORDS + G_WORDS], I32, name="rows", align_bytes=64)
@@ -114,15 +115,19 @@ def tile_list_replay_td_errors_kernel(
         rew_sb = shared.tile([P, 2, PAIRS], F32, name="rew_sb", offset=37 * KIB)
         nc.sync.dma_start(out=rew_sb[:], in_=rew.rearrange("(m p) j -> p m j", p=P))
 
-        def dealt(tile, raw, t0, t1):
-            nc.vector.tensor_copy(
+        def dealt(engine, tile, raw, t0, t1):
+            engine.tensor_copy(
                 out=tile[:].rearrange("p a (t b w) -> p a t b w", b=16, w=4),
                 in_=raw.rearrange("p a (b t w) -> p a t b w", t=4, w=4)[:, :, t0:t1],
             )
-            return [tile[:, :, 64 * t : 64 * (t + 1)] for t in range(t1 - t0)]
+            return [[tile[:, a, 64 * t : 64 * (t + 1)] for a in range(raw.shape[1])] for t in range(t1 - t0)]
 
-        w1w_0 = keep.tile([P, PASSES, 256], I32, name="w1w_0", align_bytes=64)
-        w1w = dealt(w1w_0, w1w_first[:], 0, 4)
+        w1w_00 = keep.tile([P, 1, 256], I32, name="w1w_00", align_bytes=64)
+        w1w = dealt(nc.vector, w1w_00, w1w_first[0][:], 0, 4)
+        for t0, t1, offset in ((0, 1, 48 * KIB), (1, 4, 48 * KIB + 256)):
+            tile = shared.tile([P, 1, 64 * (t1 - t0)], I32, name="w1w01_%d" % t0, offset=offset, align_bytes=64)
+            for t, words in enumerate(dealt(nc.gpsimd, tile, w1w_first[1][:], t0, t1)):
+                w1w[t0 + t].extend(words)
         v0 = keep.tile([P, S], U32, name="v0", align_bytes=64)
         nc.vector.tensor_copy(v0[:], table0[:].bitcast(U32).indirect(idx[:]))
         v_words = [[v0[:, 0:BANK], v0[:, BANK:S]], []]
@@ -133,7 +138,7 @@ def tile_list_replay_td_errors_kernel(
         for c, t0, t1, offset in ((1, 0, 2, 24 * KIB - 64), (1, 2, 4, 9 * KIB), (2, 0, 2, 7 * KIB + 64), (2, 2, 4, 10 * KIB)):
             name = "w1w%d_%d" % (c, t0)
             tile = shared.tile([P, PASSES, 64 * (t1 - t0)], I32, name=name, offset=offset, align_bytes=64)
-            w1w.extend(dealt(tile, w1w_rest[c - 1][:], t0, t1))
+            w1w.extend(dealt(nc.vector, tile, w1w_rest[c - 1][:], t0, t1))
 
         def bank(name, n):
             return psum.tile([P, BANK], F32, name=name, offset=n * BANK_BYTES)
@@ -148,7 +153,7 @@ def tile_list_replay_td_errors_kernel(
             half, j = divmod(j0, BANK)
             nc.tensor.matmul_mx(
                 out=acc,
-                lhsT=w1w[i][:, a, :].bitcast(U8).bitcast(FP4X4),
+                lhsT=w1w[i][a].bitcast(U8).bitcast(FP4X4),
                 lhsT_scale=w1_plane.bitcast(U8),
                 rhs=v_words[a][half][:, j : j + width].bitcast(FP8X4),
                 rhs_scale=planes[a][:, 0:V_WORDS].bitcast(U8)[:, j0 : j0 + width],
@@ -242,16 +247,14 @@ def tile_list_replay_td_errors_kernel(
             pick_succ(4 * LAST + t)
         for c in range(LAST):
             round_w2(c)
-        quantize_w2(0, LAST)
-        for c in range(LAST):
+            quantize_w2(c, c + 1)
             round_z(c, 0, PAIRS, False)
-        quantize_z(0, LAST * PAIRS)
+            quantize_z(PAIRS * c, PAIRS * (c + 1))
         round_w2(LAST)
-        z.append(shared.tile([P, 4, PAIRS], F32, name="z%d" % LAST, offset=0, align_bytes=64))
-        for t in range(2):
-            pick_state(4 * LAST + t, 0, PAIRS)
+        z.append(shared.tile([P, 4, PAIRS], F32, name="z%d" % LAST, offset=24 * KIB + 512, align_bytes=64))
+        pick_state(4 * LAST, 0, PAIRS)
         for half in range(2):
-            for t in range(2, 4):
+            for t in range(1, 4):
                 pick_state(4 * LAST + t, HALF * half, HALF * (half + 1))
         quantize_w2(LAST, GROUPS)
         round_z(LAST, 0, HALF, False)

@@ -143,7 +143,7 @@ def tile_list_replay_td_errors_kernel(
         def bank(name, n):
             return psum.tile([P, BANK], F32, name=name, offset=n * BANK_BYTES)
 
-        hs = [keep.tile([P, 2 * S], F32, name="h%d" % i) for i in range(4 * GROUPS)]
+        hs = [keep.tile([P, 2 * S], F32, name="h%d" % i, tag="h%d" % i, align_bytes=64) for i in range(4 * GROUPS)]
 
         def hidden_pass(acc, i, a, j0, width, start, stop):
             if i < 4:
@@ -183,7 +183,7 @@ def tile_list_replay_td_errors_kernel(
                     hidden_pass(acc[:], i, a, BANK * half, BANK, a == 1, a == 0)
                 nc.scalar.activation(out=hs[i][:, BANK * half : BANK * (half + 1)], in_=acc[:], func=ACT.Relu)
 
-        w2_codes = keep.tile([P, GROUPS * N], U32, name="w2_codes", align_bytes=64)
+        w2_codes = {}
         w2_scales = keep.tile([P, GROUPS * N], U8, name="w2_scales", align_bytes=64)
         z_codes = keep.tile([P, GROUPS * PAIRS], U32, name="z_codes", align_bytes=64)
         z_scales = keep.tile([P, GROUPS * PAIRS], U8, name="z_scales", align_bytes=64)
@@ -226,12 +226,15 @@ def tile_list_replay_td_errors_kernel(
             dst, src = interleaved(w2_bf[:, c, :, :], late[:, 4 * c : 4 * (c + 1), :])
             nc.scalar.activation(out=dst, in_=src, func=ACT.Copy)
 
-        def quantize_w2(c0, c1):
+        def quantize_w2(c0, c1, tag):
+            codes = keep.tile([P, (c1 - c0) * N], U32, name="w2_codes", tag=tag, align_bytes=64)
             nc.vector.quantize_mx(
-                out=w2_codes[:, N * c0 : N * c1].bitcast(FP8X4),
+                out=codes[:].bitcast(FP8X4),
                 scales=w2_scales[:, N * c0 : N * c1],
                 in_=w2_bf[:, c0:c1, :, :].rearrange("p c n t -> p (c n t)"),
             )
+            for c in range(c0, c1):
+                w2_codes[c] = codes[:, N * (c - c0) : N * (c - c0 + 1)]
 
         first_tile()
         for i in range(1, 4 * GROUPS):
@@ -247,16 +250,20 @@ def tile_list_replay_td_errors_kernel(
             pick_succ(4 * LAST + t)
         for c in range(LAST):
             round_w2(c)
-            quantize_w2(c, c + 1)
+        for c in range(LAST):
             round_z(c, 0, PAIRS, False)
-            quantize_z(PAIRS * c, PAIRS * (c + 1))
+            quantize_z(PAIRS * c, PAIRS * c + HALF)
         round_w2(LAST)
         z.append(shared.tile([P, 4, PAIRS], F32, name="z%d" % LAST, offset=24 * KIB + 512, align_bytes=64))
         pick_state(4 * LAST, 0, PAIRS)
         for half in range(2):
             for t in range(1, 4):
                 pick_state(4 * LAST + t, HALF * half, HALF * (half + 1))
-        quantize_w2(LAST, GROUPS)
+            if half == 0:
+                quantize_w2(0, LAST, "h%d" % (4 * LAST))
+        for c in range(LAST):
+            quantize_z(PAIRS * c + HALF, PAIRS * (c + 1))
+        quantize_w2(LAST, GROUPS, "w2_last")
         round_z(LAST, 0, HALF, False)
         round_z(LAST, HALF, 384, False)
         round_z(LAST, 384, PAIRS, True)
@@ -275,7 +282,7 @@ def tile_list_replay_td_errors_kernel(
                     heads = slice(N * c + P * m, N * c + P * (m + 1))
                     nc.tensor.matmul_mx(
                         out=d[m][:, 0:HALF],
-                        lhsT=w2_codes[:, heads].bitcast(FP8X4),
+                        lhsT=w2_codes[c][:, P * m : P * (m + 1)].bitcast(FP8X4),
                         lhsT_scale=w2_scales[:, heads],
                         rhs=z_codes[:, pairs].bitcast(FP8X4),
                         rhs_scale=z_scales[:, pairs],

@@ -28,6 +28,9 @@ KIB = 1024
 V_WORDS = S // 4
 G_WORDS = 512 // 4
 W_WORDS = GROUPS * G_WORDS
+C_WORDS = 512 // 2
+T_WORDS = C_WORDS // 4
+PIECES = ((0, 512), (512, 768), (768, 1024))
 
 
 def interleaved(dst, src):
@@ -52,21 +55,23 @@ def tile_list_replay_td_errors_kernel(
         p1 = lists.tile([P, PAIRS // 16], U16, name="p1")
         p2 = lists.tile([P, PAIRS // 16], U16, name="p2")
 
+        def placed(name, shape, dtype, offset):
+            return shared.tile(shape, dtype, name=name, offset=offset, align_bytes=64)
+
         nc.sync.dma_start(idx[:], offs)
         ts_win = keep.tile([P, T // 4], I32, name="ts_win", align_bytes=64)
         nc.scalar.dma_start(out=ts_win[0:32, :], in_=tab_scales.rearrange("a q t -> (a q) t").bitcast(I32))
         w1s_raw = keep.tile([P, W_WORDS], I32, name="w1s_raw", align_bytes=64)
-        nc.scalar.dma_start(out=w1s_raw[0:32, :], in_=w1_scales.rearrange("a q c -> (a q) c").bitcast(I32))
+        nc.sync.dma_start(out=w1s_raw[0:32, :], in_=w1_scales.rearrange("a q c -> (a q) c").bitcast(I32))
         w1w_hbm = w1_words.rearrange("a p c -> p a c").bitcast(I32)
-        w1w_first = [keep.tile([P, 1, 256], I32, name="w1w_first%d" % a, align_bytes=64) for a in range(PASSES)]
-        nc.scalar.dma_start(out=w1w_first[0][:], in_=w1w_hbm[:, 0:1, 0:256])
+        raw00 = keep.tile([P, 1, C_WORDS], I32, name="raw00", align_bytes=64)
+        nc.scalar.dma_start(out=raw00[:], in_=w1w_hbm[:, 0:1, 0:C_WORDS])
+        table = []
+        for a in range(PASSES):
+            table.append(placed("table%d" % a, [P, T], I32, 16 * KIB * a))
+            nc.sync.dma_start(out=table[a][:], in_=tab_words[a].rearrange("p t i -> p (t i)").bitcast(I32))
         nc.sync.dma_start(p2[:], pos2)
         nc.sync.dma_start(p1[:], pos1)
-        table0 = shared.tile([P, T], I32, name="table0", offset=33 * KIB, align_bytes=64)
-        nc.sync.dma_start(out=table0[:], in_=tab_words[0].rearrange("p t i -> p (t i)").bitcast(I32))
-        table1 = shared.tile([P, T], I32, name="table1", offset=8 * KIB, align_bytes=64)
-        nc.sync.dma_start(out=table1[:], in_=tab_words[1].rearrange("p t i -> p (t i)").bitcast(I32))
-        nc.sync.dma_start(out=w1w_first[1][:], in_=w1w_hbm[:, 1:2, 0:256])
 
         nc.gpsimd.memset(ts_win[32:64, :], 0)
         nc.vector.memset(ts_win[64:P, :], 0)
@@ -82,113 +87,102 @@ def tile_list_replay_td_errors_kernel(
                 in_=src.rearrange("p (c b t w) -> p c t b w", t=4, b=16, w=2),
             )
 
-        def move_rows(dst, rows):
-            nc.vector.tensor_copy(out=dst[0][0:4, :], in_=rows[0:4, :])
-            for n in range(1, 4 * PASSES):
-                a, quad = divmod(n, 4)
-                queue = nc.gpsimd if n == 1 else nc.scalar if a == 0 else nc.sync
-                queue.dma_start(out=dst[a][32 * quad : 32 * quad + 4, :], in_=rows[4 * n : 4 * n + 4, :])
-
         rows = keep.tile([P, V_WORDS + G_WORDS], I32, name="rows", align_bytes=64)
         deal_scales(rows[0:32, V_WORDS:], w1s_raw[0:32, 0:G_WORDS])
-        ts_picked = keep.tile([P, S], U8, name="ts_picked", align_bytes=64)
+        ts_picked = placed("ts_picked", [P, S], U8, 32 * KIB)
         nc.vector.tensor_copy(ts_picked[:], ts_win[:].bitcast(U8).indirect(idx[:]))
         nc.vector.tensor_copy(out=rows[0:32, 0:V_WORDS], in_=ts_picked[0:32, :].bitcast(I32))
-        move_rows(planes, rows)
+        nc.vector.tensor_copy(out=planes[0][0:4, :], in_=rows[0:4, :])
+        for n in range(1, 4 * PASSES):
+            a, quad = divmod(n, 4)
+            queue = nc.gpsimd if a == 0 else nc.sync
+            queue.dma_start(out=planes[a][32 * quad : 32 * quad + 4, :], in_=rows[4 * n : 4 * n + 4, :])
+        raw01 = placed("raw01", [P, 1, C_WORDS], I32, 32 * KIB)
+        nc.sync.dma_start(out=raw01[:], in_=w1w_hbm[:, 1:2, 0:C_WORDS])
 
-        w1w_rest = []
+        raw = [None]
         for c in range(1, GROUPS):
-            offset = 33 * KIB + 2 * KIB * (c - 1)
-            w1w_rest.append(shared.tile([P, PASSES, 256], I32, name="w1w_rest%d" % c, offset=offset, align_bytes=64))
-            nc.sync.dma_start(out=w1w_rest[-1][:], in_=w1w_hbm[:, :, 256 * c : 256 * (c + 1)])
-        rows_rest = shared.tile([P, LAST * G_WORDS], I32, name="rows_rest", offset=47 * KIB, align_bytes=64)
+            raw.append(placed("raw%d" % c, [P, PASSES, C_WORDS], I32, 8 * KIB * (c - 1)))
+            nc.sync.dma_start(out=raw[c][:], in_=w1w_hbm[:, :, C_WORDS * c : C_WORDS * (c + 1)])
+        rows_rest = placed("rows_rest", [P, LAST * G_WORDS], I32, 15 * KIB)
         deal_scales(rows_rest[0:32, :], w1s_raw[0:32, G_WORDS:])
         nc.vector.tensor_copy(out=planes_rest[0:4, 0, :], in_=rows_rest[0:4, :])
         for n in range(1, 4 * PASSES):
             a, quad = divmod(n, 4)
             nc.sync.dma_start(out=planes_rest[32 * quad : 32 * quad + 4, a, :], in_=rows_rest[4 * n : 4 * n + 4, :])
-        late = shared.tile([P, 12, N], F32, name="late", offset=12 * KIB - 128)
+        w2_raw = []
         for c in range(GROUPS):
+            w2_raw.append(placed("w2_raw%d" % c, [P, 4, N], F32, 16 * KIB + 4 * KIB * (1, 3, 0)[c]))
             w2_rows = w2[512 * c : 512 * (c + 1), :].rearrange("(b t u) n -> t b u n", t=4, u=8)
             for t in range(4):
-                nc.sync.dma_start(out=late[:, 4 * c + t, :], in_=w2_rows[t])
-        rew_sb = shared.tile([P, 2, PAIRS], F32, name="rew_sb", offset=37 * KIB)
+                nc.sync.dma_start(out=w2_raw[c][:, t, :], in_=w2_rows[t])
+        rew_sb = placed("rew_sb", [P, 2, PAIRS], F32, 24 * KIB)
         nc.sync.dma_start(out=rew_sb[:], in_=rew.rearrange("(m p) j -> p m j", p=P))
 
-        def dealt(engine, tile, raw, t0, t1):
-            engine.tensor_copy(
-                out=tile[:].rearrange("p a (t b w) -> p a t b w", b=16, w=4),
-                in_=raw.rearrange("p a (b t w) -> p a t b w", t=4, w=4)[:, :, t0:t1],
-            )
-            return [[tile[:, a, 64 * t : 64 * (t + 1)] for a in range(raw.shape[1])] for t in range(t1 - t0)]
+        def dealt_tile(c):
+            return keep.tile([P, PASSES * C_WORDS], U32, name="dealt%d" % c, tag="dealt", align_bytes=64)
 
-        w1w_00 = keep.tile([P, 1, 256], I32, name="w1w_00", align_bytes=64)
-        w1w = dealt(nc.vector, w1w_00, w1w_first[0][:], 0, 4)
-        for t0, t1, offset in ((0, 1, 48 * KIB), (1, 4, 48 * KIB + 256)):
-            tile = shared.tile([P, 1, 64 * (t1 - t0)], I32, name="w1w01_%d" % t0, offset=offset, align_bytes=64)
-            for t, words in enumerate(dealt(nc.gpsimd, tile, w1w_first[1][:], t0, t1)):
-                w1w[t0 + t].extend(words)
+        def deal(copy, dst, src):
+            copy(
+                out=dst.rearrange("p (a t b w) -> p a t b w", t=4, b=16, w=4),
+                in_=src.rearrange("p a (b t w) -> p a t b w", t=4, w=4),
+            )
+
+        dealt = [dealt_tile(0)]
+        deal(nc.vector.tensor_copy, dealt[0][:, 0:C_WORDS].bitcast(I32), raw00[:])
+        deal(nc.scalar.copy, dealt[0][:, C_WORDS:], raw01[:].bitcast(U32))
         v0 = keep.tile([P, S], U32, name="v0", align_bytes=64)
-        nc.vector.tensor_copy(v0[:], table0[:].bitcast(U32).indirect(idx[:]))
-        v_words = [[v0[:, 0:BANK], v0[:, BANK:S]], []]
-        for half in range(2):
-            v1 = keep.tile([P, BANK], U32, name="v1_%d" % half, align_bytes=64)
-            nc.vector.tensor_copy(v1[:], table1[:].bitcast(U32).indirect(idx[:, 32 * half : 32 * (half + 1)]))
-            v_words[1].append(v1[:])
-        for c, t0, t1, offset in ((1, 0, 2, 24 * KIB - 64), (1, 2, 4, 9 * KIB), (2, 0, 2, 7 * KIB + 64), (2, 2, 4, 10 * KIB)):
-            name = "w1w%d_%d" % (c, t0)
-            tile = shared.tile([P, PASSES, 64 * (t1 - t0)], I32, name=name, offset=offset, align_bytes=64)
-            w1w.extend(dealt(nc.vector, tile, w1w_rest[c - 1][:], t0, t1))
+        nc.vector.tensor_copy(v0[:], table[0][:].bitcast(U32).indirect(idx[:]))
+        v1 = keep.tile([P, S], U32, name="v1", align_bytes=64)
+        for j0, j1 in PIECES:
+            nc.vector.tensor_copy(v1[:, j0:j1], table[1][:].bitcast(U32).indirect(idx[:, j0 // 16 : j1 // 16]))
+        v_words = [v0, v1]
 
         def bank(name, n):
             return psum.tile([P, BANK], F32, name=name, offset=n * BANK_BYTES)
 
         hs = [keep.tile([P, 2 * S], F32, name="h%d" % i, tag="h%d" % i, align_bytes=64) for i in range(4 * GROUPS)]
 
-        def hidden_pass(acc, i, a, j0, width, start, stop):
-            if i < 4:
+        def hidden_pass(acc, i, a, j0, j1, start, stop):
+            c, t = divmod(i, 4)
+            if c == 0:
                 w1_plane = planes[a][:, V_WORDS + 32 * i : V_WORDS + 32 * (i + 1)]
             else:
                 w1_plane = planes_rest[:, a, 32 * (i - 4) : 32 * (i - 3)]
-            half, j = divmod(j0, BANK)
+            w0 = C_WORDS * a + T_WORDS * t
             nc.tensor.matmul_mx(
-                out=acc,
-                lhsT=w1w[i][a].bitcast(U8).bitcast(FP4X4),
+                out=acc[:, 0 : j1 - j0],
+                lhsT=dealt[c][:, w0 : w0 + T_WORDS].bitcast(U8).bitcast(FP4X4),
                 lhsT_scale=w1_plane.bitcast(U8),
-                rhs=v_words[a][half][:, j : j + width].bitcast(FP8X4),
-                rhs_scale=planes[a][:, 0:V_WORDS].bitcast(U8)[:, j0 : j0 + width],
+                rhs=v_words[a][:, j0:j1].bitcast(FP8X4),
+                rhs_scale=planes[a][:, 0:V_WORDS].bitcast(U8)[:, j0:j1],
                 start=start,
                 stop=stop,
             )
 
+        def relu(acc, i, j0, j1):
+            nc.scalar.activation(out=hs[i][:, j0:j1], in_=acc[:, 0 : j1 - j0], func=ACT.Relu)
+
         def first_tile():
-            low = bank("acc0_0", 0)
-            high = [bank("acc0_1", 1), bank("acc0_2", 3)]
-            for a in range(PASSES):
-                hidden_pass(low[:], 0, a, 0, BANK, a == 0, a == 1)
+            accs = [bank("acc0_%d" % n, (0, 1, 3)[n]) for n in range(3)]
+            for n, a in ((0, 0), (0, 1), (1, 0), (2, 0), (1, 1), (2, 1)):
+                hidden_pass(accs[n], 0, a, *PIECES[n], a == 0, a == 1)
                 if a == 1:
-                    nc.scalar.activation(out=hs[0][:, 0:BANK], in_=low[:], func=ACT.Relu)
-                for n in range(2):
-                    j0 = BANK + 256 * n
-                    for k in range(2):
-                        acc = high[n][:, P * k : P * (k + 1)]
-                        hidden_pass(acc, 0, a, j0 + P * k, P, a == 0 and k == 0, a == 1 and k == 1)
-                    if a == 1:
-                        nc.scalar.activation(out=hs[0][:, j0 : j0 + 256], in_=high[n][:, 0:256], func=ACT.Relu)
+                    relu(accs[n], 0, *PIECES[n])
 
         def hidden_tile(i):
             for half in (1, 0):
                 acc = bank("acc%d_%d" % (i, half), (2, 0, 1, 3)[(2 * i - 1 - half) % 4])
                 for a in (1, 0):
-                    hidden_pass(acc[:], i, a, BANK * half, BANK, a == 1, a == 0)
-                nc.scalar.activation(out=hs[i][:, BANK * half : BANK * (half + 1)], in_=acc[:], func=ACT.Relu)
+                    hidden_pass(acc, i, a, BANK * half, BANK * (half + 1), a == 1, a == 0)
+                relu(acc, i, BANK * half, BANK * (half + 1))
 
         w2_codes = {}
         w2_scales = keep.tile([P, GROUPS * N], U8, name="w2_scales", align_bytes=64)
-        z_codes = keep.tile([P, GROUPS * PAIRS], U32, name="z_codes", align_bytes=64)
+        z_codes = {}
         z_scales = keep.tile([P, GROUPS * PAIRS], U8, name="z_scales", align_bytes=64)
         succ = [keep.tile([P, 4, PAIRS], F32, name="succ", bufs=2) for c in range(GROUPS)]
-        w2_bf = shared.tile([P, GROUPS, N, 4], BF16, name="w2_bf", offset=41 * KIB, align_bytes=64)
+        w2_bf = keep.tile([P, GROUPS, N, 4], BF16, name="w2_bf", align_bytes=64)
         z_bf = keep.tile([P, GROUPS * PAIRS, 4], BF16, name="z_bf", align_bytes=64)
         z = []
 
@@ -215,15 +209,18 @@ def tile_list_replay_td_errors_kernel(
             else:
                 nc.scalar.activation(out=dst, in_=src, func=ACT.Copy)
 
-        def quantize_z(x0, x1):
+        def quantize_z(c, half, tag):
+            x0 = PAIRS * c + HALF * half
+            codes = keep.tile([P, HALF], U32, name="z_codes", tag=tag, align_bytes=64)
             nc.vector.quantize_mx(
-                out=z_codes[:, x0:x1].bitcast(FP8X4),
-                scales=z_scales[:, x0:x1],
-                in_=z_bf[:, x0:x1, :].rearrange("p j t -> p (j t)"),
+                out=codes[:].bitcast(FP8X4),
+                scales=z_scales[:, x0 : x0 + HALF],
+                in_=z_bf[:, x0 : x0 + HALF, :].rearrange("p j t -> p (j t)"),
             )
+            z_codes[c, half] = codes
 
         def round_w2(c):
-            dst, src = interleaved(w2_bf[:, c, :, :], late[:, 4 * c : 4 * (c + 1), :])
+            dst, src = interleaved(w2_bf[:, c, :, :], w2_raw[c][:])
             nc.scalar.activation(out=dst, in_=src, func=ACT.Copy)
 
         def quantize_w2(c0, c1, tag):
@@ -236,39 +233,43 @@ def tile_list_replay_td_errors_kernel(
             for c in range(c0, c1):
                 w2_codes[c] = codes[:, N * (c - c0) : N * (c - c0 + 1)]
 
-        first_tile()
-        for i in range(1, 4 * GROUPS):
-            hidden_tile(i)
-
-        for c in range(LAST):
-            z.append(shared.tile([P, 4, PAIRS], F32, name="z%d" % c, offset=(24 * KIB + 512, 0)[c], align_bytes=64))
+        z_offsets = (0, 8 * KIB, 28 * KIB)
+        for c in range(GROUPS):
             for t in range(4):
+                if c == 0 and t == 0:
+                    first_tile()
+                else:
+                    hidden_tile(4 * c + t)
                 pick_succ(4 * c + t)
-            for t in range(4):
-                pick_state(4 * c + t, 0, PAIRS)
-        for t in range(4):
-            pick_succ(4 * LAST + t)
-        for c in range(LAST):
-            round_w2(c)
-        for c in range(LAST):
-            round_z(c, 0, PAIRS, False)
-            quantize_z(PAIRS * c, PAIRS * c + HALF)
+            if c < LAST:
+                dealt.append(dealt_tile(c + 1))
+                deal(nc.scalar.copy, dealt[c + 1][:], raw[c + 1][:].bitcast(U32))
+            if c == 1:
+                round_z(0, 0, PAIRS, False)
+                quantize_z(0, 0, "z00")
+            else:
+                round_w2(c // 2)
+            z.append(placed("z%d" % c, [P, 4, PAIRS], F32, z_offsets[c]))
+            if c < LAST:
+                for t in range(4):
+                    pick_state(4 * c + t, 0, PAIRS)
+        round_z(1, 0, PAIRS, False)
+        quantize_z(1, 0, "z10")
         round_w2(LAST)
-        z.append(shared.tile([P, 4, PAIRS], F32, name="z%d" % LAST, offset=24 * KIB + 512, align_bytes=64))
         pick_state(4 * LAST, 0, PAIRS)
         for half in range(2):
             for t in range(1, 4):
                 pick_state(4 * LAST + t, HALF * half, HALF * (half + 1))
             if half == 0:
                 quantize_w2(0, LAST, "h%d" % (4 * LAST))
-        for c in range(LAST):
-            quantize_z(PAIRS * c + HALF, PAIRS * (c + 1))
+        quantize_z(0, 1, "h%d" % (4 * LAST + 1))
+        quantize_z(1, 1, "h%d" % (4 * LAST + 2))
         quantize_w2(LAST, GROUPS, "w2_last")
         round_z(LAST, 0, HALF, False)
         round_z(LAST, HALF, 384, False)
         round_z(LAST, 384, PAIRS, True)
         for half in range(2):
-            quantize_z(PAIRS * LAST + HALF * half, PAIRS * LAST + HALF * (half + 1))
+            quantize_z(LAST, half, "z2%d" % half)
 
         out_v = out.rearrange("(m p) j -> p m j", p=P)
         for half in range(2):
@@ -284,7 +285,7 @@ def tile_list_replay_td_errors_kernel(
                         out=d[m][:, 0:HALF],
                         lhsT=w2_codes[c][:, P * m : P * (m + 1)].bitcast(FP8X4),
                         lhsT_scale=w2_scales[:, heads],
-                        rhs=z_codes[:, pairs].bitcast(FP8X4),
+                        rhs=z_codes[c, half][:].bitcast(FP8X4),
                         rhs_scale=z_scales[:, pairs],
                         start=(c == 0),
                         stop=(c == LAST),

@@ -141,6 +141,18 @@ def tile_list_replay_td_errors_kernel(
         def bank(name, n):
             return psum.tile([P, BANK], F32, name=name, offset=n * BANK_BYTES)
 
+        warm = bank("warm", 7)
+        for n in range(4):
+            nc.tensor.matmul_mx(
+                out=warm[:],
+                lhsT=dealt[0][:, 0:T_WORDS].bitcast(U8).bitcast(FP4X4),
+                lhsT_scale=ts_win[:].bitcast(U8)[:, 0:P],
+                rhs=v0[:, 0:BANK].bitcast(FP8X4),
+                rhs_scale=ts_win[:].bitcast(U8)[:, 0:BANK],
+                start=True,
+                stop=True,
+            )
+
         hs = [keep.tile([P, 2 * S], F32, name="h%d" % i, tag="h%d" % i, align_bytes=64) for i in range(4 * GROUPS)]
 
         def hidden_pass(acc, i, a, j0, j1, start, stop):
@@ -166,16 +178,23 @@ def tile_list_replay_td_errors_kernel(
         def first_tile():
             accs = [bank("acc0_%d" % n, (0, 1, 3)[n]) for n in range(3)]
             for n, a in ((0, 0), (0, 1), (1, 0), (2, 0), (1, 1), (2, 1)):
+                if (n, a) == (2, 1):
+                    hidden_half(1, 0, 2)
                 hidden_pass(accs[n], 0, a, *PIECES[n], a == 0, a == 1)
-                if a == 1:
+                if (n, a) == (2, 1):
+                    nc.vector.tensor_scalar_max(hs[0][:, 768:1024], accs[n][:, 0:256], 0.0)
+                elif a == 1:
                     relu(accs[n], 0, *PIECES[n])
 
+        def hidden_half(i, half, n):
+            acc = bank("acc%d_%d" % (i, half), n)
+            for a in (1, 0):
+                hidden_pass(acc, i, a, BANK * half, BANK * (half + 1), a == 1, a == 0)
+            relu(acc, i, BANK * half, BANK * (half + 1))
+
         def hidden_tile(i):
-            for half in (1, 0):
-                acc = bank("acc%d_%d" % (i, half), (2, 0, 1, 3)[(2 * i - 1 - half) % 4])
-                for a in (1, 0):
-                    hidden_pass(acc, i, a, BANK * half, BANK * (half + 1), a == 1, a == 0)
-                relu(acc, i, BANK * half, BANK * (half + 1))
+            for half in (1,) if i == 1 else (1, 0):
+                hidden_half(i, half, (2, 0, 1, 3)[(2 * i - 1 - half) % 4] if i > 1 else 0)
 
         w2_codes = {}
         w2_scales = keep.tile([P, GROUPS * N], U8, name="w2_scales", align_bytes=64)

@@ -70,6 +70,8 @@ def tile_list_replay_td_errors_kernel(
         for a in range(PASSES):
             table.append(placed("table%d" % a, [P, T], I32, 16 * KIB * a))
             nc.sync.dma_start(out=table[a][:], in_=tab_words[a].rearrange("p t i -> p (t i)").bitcast(I32))
+        raw01 = keep.tile([P, 1, C_WORDS], I32, name="raw01", align_bytes=64)
+        nc.sync.dma_start(out=raw01[:], in_=w1w_hbm[:, 1:2, 0:C_WORDS])
         nc.sync.dma_start(p2[:], pos2)
         nc.sync.dma_start(p1[:], pos1)
 
@@ -95,10 +97,7 @@ def tile_list_replay_td_errors_kernel(
         nc.vector.tensor_copy(out=planes[0][0:4, :], in_=rows[0:4, :])
         for n in range(1, 4 * PASSES):
             a, quad = divmod(n, 4)
-            queue = nc.gpsimd if a == 0 else nc.sync
-            queue.dma_start(out=planes[a][32 * quad : 32 * quad + 4, :], in_=rows[4 * n : 4 * n + 4, :])
-        raw01 = placed("raw01", [P, 1, C_WORDS], I32, 32 * KIB)
-        nc.sync.dma_start(out=raw01[:], in_=w1w_hbm[:, 1:2, 0:C_WORDS])
+            nc.gpsimd.dma_start(out=planes[a][32 * quad : 32 * quad + 4, :], in_=rows[4 * n : 4 * n + 4, :])
 
         raw = [None]
         for c in range(1, GROUPS):
@@ -140,18 +139,6 @@ def tile_list_replay_td_errors_kernel(
 
         def bank(name, n):
             return psum.tile([P, BANK], F32, name=name, offset=n * BANK_BYTES)
-
-        warm = bank("warm", 7)
-        for n in range(4):
-            nc.tensor.matmul_mx(
-                out=warm[:],
-                lhsT=dealt[0][:, 0:T_WORDS].bitcast(U8).bitcast(FP4X4),
-                lhsT_scale=ts_win[:].bitcast(U8)[:, 0:P],
-                rhs=v0[:, 0:BANK].bitcast(FP8X4),
-                rhs_scale=ts_win[:].bitcast(U8)[:, 0:BANK],
-                start=True,
-                stop=True,
-            )
 
         hs = [keep.tile([P, 2 * S], F32, name="h%d" % i, tag="h%d" % i, align_bytes=64) for i in range(4 * GROUPS)]
 

@@ -97,7 +97,8 @@ def tile_list_replay_td_errors_kernel(
         nc.vector.tensor_copy(out=planes[0][0:4, :], in_=rows[0:4, :])
         for n in range(1, 4 * PASSES):
             a, quad = divmod(n, 4)
-            nc.gpsimd.dma_start(out=planes[a][32 * quad : 32 * quad + 4, :], in_=rows[4 * n : 4 * n + 4, :])
+            queue = nc.scalar if n <= 4 else nc.gpsimd
+            queue.dma_start(out=planes[a][32 * quad : 32 * quad + 4, :], in_=rows[4 * n : 4 * n + 4, :])
 
         raw = [None]
         for c in range(1, GROUPS):
@@ -139,6 +140,18 @@ def tile_list_replay_td_errors_kernel(
 
         def bank(name, n):
             return psum.tile([P, BANK], F32, name=name, offset=n * BANK_BYTES)
+
+        warm = bank("warm", 7)
+        for n in range(4):
+            nc.tensor.matmul_mx(
+                out=warm[:],
+                lhsT=dealt[0][:, 0:T_WORDS].bitcast(U8).bitcast(FP4X4),
+                lhsT_scale=ts_win[:].bitcast(U8)[:, 0:P],
+                rhs=v0[:, 0:BANK].bitcast(FP8X4),
+                rhs_scale=ts_win[:].bitcast(U8)[:, 0:BANK],
+                start=True,
+                stop=True,
+            )
 
         hs = [keep.tile([P, 2 * S], F32, name="h%d" % i, tag="h%d" % i, align_bytes=64) for i in range(4 * GROUPS)]
 

@@ -112,7 +112,7 @@ def tile_list_replay_td_errors_kernel(
             nc.sync.dma_start(out=planes_rest[32 * quad : 32 * quad + 4, a, :], in_=rows_rest[4 * n : 4 * n + 4, :])
         w2_raw = []
         for c in range(GROUPS):
-            w2_raw.append(placed("w2_raw%d" % c, [P, 4, N], F32, 16 * KIB + 4 * KIB * (1, 3, 0)[c]))
+            w2_raw.append(placed("w2_raw%d" % c, [P, 4, N], F32, (20, 30, 16)[c] * KIB))
             w2_rows = w2[512 * c : 512 * (c + 1), :].rearrange("(b t u) n -> t b u n", t=4, u=8)
             for t in range(4):
                 nc.sync.dma_start(out=w2_raw[c][:, t, :], in_=w2_rows[t])
@@ -203,7 +203,7 @@ def tile_list_replay_td_errors_kernel(
         succ = [keep.tile([P, 4, PAIRS], F32, name="succ", bufs=2) for c in range(GROUPS)]
         w2_bf = keep.tile([P, GROUPS, N, 4], BF16, name="w2_bf", align_bytes=64)
         z_bf = keep.tile([P, GROUPS * PAIRS, 4], BF16, name="z_bf", align_bytes=64)
-        z = []
+        z = {}
 
         def pick_succ(i):
             nc.vector.tensor_scalar(
@@ -218,19 +218,22 @@ def tile_list_replay_td_errors_kernel(
         def pick_state(i, j0, j1):
             c, t = divmod(i, 4)
             nc.vector.tensor_tensor(
-                z[c][:, t, j0:j1], hs[i][:].indirect(p1[:, j0 // 16 : j1 // 16]), succ[c][:, t, j0:j1], ALU.add
+                z[c, j0][:, t, :], hs[i][:].indirect(p1[:, j0 // 16 : j1 // 16]), succ[c][:, t, j0:j1], ALU.add
             )
 
         def round_z(c, j0, j1, on_vector):
-            dst, src = interleaved(z_bf[:, PAIRS * c + j0 : PAIRS * c + j1, :], z[c][:, :, j0:j1])
+            first = HALF if (c, j0 // HALF) == (LAST, 1) else 0
+            dst, src = interleaved(
+                z_bf[:, PAIRS * c + j0 : PAIRS * c + j1, :], z[c, first][:, :, j0 - first : j1 - first]
+            )
             if on_vector:
                 nc.vector.tensor_copy(out=dst, in_=src)
             else:
                 nc.scalar.activation(out=dst, in_=src, func=ACT.Copy)
 
-        def quantize_z(c, half, tag):
+        def quantize_z(c, half, offset):
             x0 = PAIRS * c + HALF * half
-            codes = keep.tile([P, HALF], U32, name="z_codes", tag=tag, align_bytes=64)
+            codes = placed("z_codes%d_%d" % (c, half), [P, HALF], U32, offset)
             nc.vector.quantize_mx(
                 out=codes[:].bitcast(FP8X4),
                 scales=z_scales[:, x0 : x0 + HALF],
@@ -265,34 +268,33 @@ def tile_list_replay_td_errors_kernel(
                 deal(nc.scalar.copy, dealt[c + 1][:], raw[c + 1][:].bitcast(U32))
             if c == 1:
                 round_z(0, 0, PAIRS, False)
-                quantize_z(0, 0, "z00")
+                for half in range(2):
+                    quantize_z(0, half, (36 + 4 * half) * KIB)
             else:
                 round_w2(c // 2)
-            z.append(placed("z%d" % c, [P, 4, PAIRS], F32, z_offsets[c]))
             if c < LAST:
+                z[c, 0] = placed("z%d" % c, [P, 4, PAIRS], F32, z_offsets[c])
                 for t in range(4):
                     pick_state(4 * c + t, 0, PAIRS)
         round_z(1, 0, PAIRS, False)
-        quantize_z(1, 0, "z10")
+        quantize_z(1, 0, 37 * KIB)
         round_w2(LAST)
-        pick_state(4 * LAST, 0, PAIRS)
         for half in range(2):
-            for t in range(1, 4):
+            z[LAST, HALF * half] = placed("z%d_%d" % (LAST, half), [P, 4, HALF], F32, z_offsets[LAST] + 4 * KIB * half)
+            for t in range(4):
+                if (half, t) == (1, 1):
+                    quantize_w2(0, LAST, "h%d" % (4 * LAST))
                 pick_state(4 * LAST + t, HALF * half, HALF * (half + 1))
-            if half == 0:
-                quantize_w2(0, LAST, "h%d" % (4 * LAST))
-        quantize_z(0, 1, "h%d" % (4 * LAST + 1))
-        quantize_z(1, 1, "h%d" % (4 * LAST + 2))
-        quantize_w2(LAST, GROUPS, "w2_last")
+        quantize_w2(LAST, GROUPS, "h%d" % (4 * LAST + 2))
         round_z(LAST, 0, HALF, False)
         round_z(LAST, HALF, 384, False)
         round_z(LAST, 384, PAIRS, True)
-        for half in range(2):
-            quantize_z(LAST, half, "z2%d" % half)
+        quantize_z(LAST, 0, 38 * KIB)
+        quantize_z(1, 1, z_offsets[LAST])
+        quantize_z(LAST, 1, 39 * KIB)
 
         out_v = out.rearrange("(m p) j -> p m j", p=P)
         for half in range(2):
-            cols = slice(HALF * half, HALF * (half + 1))
             err = ring.tile([P, 2, HALF], F32, name="err")
             res = ring.tile([P, 2, HALF], F32, name="res")
             d = [bank("d%d_%d" % (half, m), 4 + 2 * half + m) for m in range(2)]
@@ -310,9 +312,12 @@ def tile_list_replay_td_errors_kernel(
                         stop=(c == LAST),
                     )
             for m in range(2):
-                nc.vector.tensor_tensor(
-                    out=err[:, m, :], in0=rew_sb[:, m, cols], in1=d[m][:, 0:HALF], op=ALU.subtract
-                )
-                nc.scalar.activation(out=res[:, m, :], in_=err[:, m, :], func=ACT.Tanh)
-                queue = nc.scalar if (half, m) == (1, 1) else nc.sync
-                queue.dma_start(out=out_v[:, m, cols], in_=res[:, m, :])
+                last = (half, m) == (1, 1)
+                for j0, j1 in ((0, P), (P, HALF)) if last else ((0, HALF),):
+                    js = slice(HALF * half + j0, HALF * half + j1)
+                    nc.vector.tensor_tensor(
+                        out=err[:, m, j0:j1], in0=rew_sb[:, m, js], in1=d[m][:, j0:j1], op=ALU.subtract
+                    )
+                    nc.scalar.activation(out=res[:, m, j0:j1], in_=err[:, m, j0:j1], func=ACT.Tanh)
+                    queue = nc.scalar if last and j1 == HALF else nc.sync
+                    queue.dma_start(out=out_v[:, m, js], in_=res[:, m, j0:j1])

@@ -231,15 +231,16 @@ def tile_list_replay_td_errors_kernel(
             else:
                 nc.scalar.activation(out=dst, in_=src, func=ACT.Copy)
 
-        def quantize_z(c, half, offset):
-            x0 = PAIRS * c + HALF * half
-            codes = placed("z_codes%d_%d" % (c, half), [P, HALF], U32, offset)
+        def quantize_z(c, halves, offset):
+            x0, x1 = PAIRS * c + HALF * halves[0], PAIRS * c + HALF * (halves[-1] + 1)
+            codes = placed("z_codes%d_%d" % (c, halves[0]), [P, x1 - x0], U32, offset)
             nc.vector.quantize_mx(
                 out=codes[:].bitcast(FP8X4),
-                scales=z_scales[:, x0 : x0 + HALF],
-                in_=z_bf[:, x0 : x0 + HALF, :].rearrange("p j t -> p (j t)"),
+                scales=z_scales[:, x0:x1],
+                in_=z_bf[:, x0:x1, :].rearrange("p j t -> p (j t)"),
             )
-            z_codes[c, half] = codes
+            for n, half in enumerate(halves):
+                z_codes[c, half] = codes[:, HALF * n : HALF * (n + 1)]
 
         def round_w2(c):
             dst, src = interleaved(w2_bf[:, c, :, :], w2_raw[c][:])
@@ -268,8 +269,7 @@ def tile_list_replay_td_errors_kernel(
                 deal(nc.scalar.copy, dealt[c + 1][:], raw[c + 1][:].bitcast(U32))
             if c == 1:
                 round_z(0, 0, PAIRS, False)
-                for half in range(2):
-                    quantize_z(0, half, (36 + 4 * half) * KIB)
+                quantize_z(0, (0, 1), 40 * KIB)
             else:
                 round_w2(c // 2)
             if c < LAST:
@@ -277,21 +277,21 @@ def tile_list_replay_td_errors_kernel(
                 for t in range(4):
                     pick_state(4 * c + t, 0, PAIRS)
         round_z(1, 0, PAIRS, False)
-        quantize_z(1, 0, 37 * KIB)
+        quantize_z(1, (0,), 37 * KIB)
         round_w2(LAST)
         for half in range(2):
             z[LAST, HALF * half] = placed("z%d_%d" % (LAST, half), [P, 4, HALF], F32, z_offsets[LAST] + 4 * KIB * half)
             for t in range(4):
                 if (half, t) == (1, 1):
-                    quantize_w2(0, LAST, "h%d" % (4 * LAST))
+                    quantize_w2(0, LAST, "w2_first")
                 pick_state(4 * LAST + t, HALF * half, HALF * (half + 1))
         quantize_w2(LAST, GROUPS, "h%d" % (4 * LAST + 2))
         round_z(LAST, 0, HALF, False)
         round_z(LAST, HALF, 384, False)
         round_z(LAST, 384, PAIRS, True)
-        quantize_z(LAST, 0, 38 * KIB)
-        quantize_z(1, 1, z_offsets[LAST])
-        quantize_z(LAST, 1, 39 * KIB)
+        quantize_z(LAST, (0,), 38 * KIB)
+        quantize_z(1, (1,), z_offsets[LAST])
+        quantize_z(LAST, (1,), 39 * KIB)
 
         out_v = out.rearrange("(m p) j -> p m j", p=P)
         for half in range(2):
@@ -306,7 +306,7 @@ def tile_list_replay_td_errors_kernel(
                         out=d[m][:, 0:HALF],
                         lhsT=w2_codes[c][:, P * m : P * (m + 1)].bitcast(FP8X4),
                         lhsT_scale=w2_scales[:, heads],
-                        rhs=z_codes[c, half][:].bitcast(FP8X4),
+                        rhs=z_codes[c, half].bitcast(FP8X4),
                         rhs_scale=z_scales[:, pairs],
                         start=(c == 0),
                         stop=(c == LAST),

@@ -175,22 +175,28 @@ def tile_list_replay_td_errors_kernel(
         def relu(acc, i, j0, j1):
             nc.scalar.activation(out=hs[i][:, j0:j1], in_=acc[:, 0 : j1 - j0], func=ACT.Relu)
 
-        def first_tile():
-            accs = [bank("acc0_%d" % n, (0, 1, 3)[n]) for n in range(3)]
-            for n, a in ((0, 0), (0, 1), (1, 0), (2, 0), (1, 1), (2, 1)):
-                if (n, a) == (2, 1):
-                    hidden_half(1, 0, 2)
-                hidden_pass(accs[n], 0, a, *PIECES[n], a == 0, a == 1)
-                if (n, a) == (2, 1):
-                    nc.vector.tensor_scalar_max(hs[0][:, 768:1024], accs[n][:, 0:256], 0.0)
-                elif a == 1:
-                    relu(accs[n], 0, *PIECES[n])
-
-        def hidden_half(i, half, n):
+        def half_passes(i, half, n):
             acc = bank("acc%d_%d" % (i, half), n)
             for a in (1, 0):
                 hidden_pass(acc, i, a, BANK * half, BANK * (half + 1), a == 1, a == 0)
-            relu(acc, i, BANK * half, BANK * (half + 1))
+            return acc
+
+        def first_tile():
+            parts = ((0, 512), (512, 768), (768, 896), (896, 1024))
+            accs = [bank("acc0_%d" % n, (0, 1, 3, 4)[n]) for n in range(4)]
+            for n, a in ((0, 0), (0, 1), (1, 0), (2, 0), (3, 0), (1, 1)):
+                hidden_pass(accs[n], 0, a, *parts[n], a == 0, a == 1)
+                if a == 1:
+                    relu(accs[n], 0, *parts[n])
+            early = half_passes(1, 0, 2)
+            for n in (2, 3):
+                hidden_pass(accs[n], 0, 1, *parts[n], False, True)
+            relu(accs[2], 0, *parts[2])
+            nc.vector.tensor_scalar_max(hs[0][:, 896:1024], accs[3][:, 0:P], 0.0)
+            relu(early, 1, 0, BANK)
+
+        def hidden_half(i, half, n):
+            relu(half_passes(i, half, n), i, BANK * half, BANK * (half + 1))
 
         def hidden_tile(i):
             for half in (1,) if i == 1 else (1, 0):
@@ -283,12 +289,12 @@ def tile_list_replay_td_errors_kernel(
             z[LAST, HALF * half] = placed("z%d_%d" % (LAST, half), [P, 4, HALF], F32, z_offsets[LAST] + 4 * KIB * half)
             for t in range(4):
                 if (half, t) == (1, 1):
-                    quantize_w2(0, LAST, "w2_first")
+                    quantize_w2(0, LAST, "h%d" % (4 * LAST))
                 pick_state(4 * LAST + t, HALF * half, HALF * (half + 1))
         quantize_w2(LAST, GROUPS, "h%d" % (4 * LAST + 2))
         round_z(LAST, 0, HALF, False)
-        round_z(LAST, HALF, 384, False)
-        round_z(LAST, 384, PAIRS, True)
+        round_z(LAST, HALF, 416, False)
+        round_z(LAST, 416, PAIRS, True)
         quantize_z(LAST, (0,), 38 * KIB)
         quantize_z(1, (1,), z_offsets[LAST])
         quantize_z(LAST, (1,), 39 * KIB)

@@ -75,8 +75,13 @@ def tile_list_replay_td_errors_kernel(
         nc.sync.dma_start(p2[:], pos2)
         nc.sync.dma_start(p1[:], pos1)
 
+        blank = keep.tile([P, 4 * BANK], BF16, name="blank", align_bytes=64)
+        nc.vector.memset(blank[:].bitcast(I32), 0)
         nc.gpsimd.memset(ts_win[32:64, :], 0)
-        nc.vector.memset(ts_win[64:P, :], 0)
+        nc.gpsimd.memset(ts_win[64:P, :], 0)
+        blank_scales = keep.tile([P, BANK], U8, name="blank_scales", align_bytes=64)
+        blank_moving = keep.tile([P, BANK], U32, name="blank_moving", align_bytes=64)
+        nc.vector.quantize_mx(out=blank_moving[:].bitcast(FP8X4), scales=blank_scales[:], in_=blank[:])
         planes = [keep.tile([P, V_WORDS + G_WORDS], I32, name="plane%d" % a, align_bytes=64) for a in range(PASSES)]
         planes_rest = keep.tile([P, PASSES, LAST * G_WORDS], I32, name="planes_rest", align_bytes=64)
         for a in range(PASSES):
@@ -128,8 +133,23 @@ def tile_list_replay_td_errors_kernel(
                 in_=src.rearrange("p a (b t w) -> p a t b w", t=4, w=4),
             )
 
+        blank_still = placed("blank_still", [P, P], I32, 4 * KIB)
+        nc.vector.tensor_copy(out=blank_still[:], in_=blank_moving[:, 0:P].bitcast(I32))
+        warm = psum.tile([P, BANK], F32, name="warm", offset=7 * BANK_BYTES)
+        for n in range(4):
+            nc.tensor.matmul_mx(
+                out=warm[:],
+                lhsT=blank_still[:].bitcast(FP8X4),
+                lhsT_scale=blank_scales[:, 0:P],
+                rhs=blank_moving[:].bitcast(FP8X4),
+                rhs_scale=blank_scales[:],
+                start=True,
+                stop=True,
+            )
+
         dealt = [dealt_tile(0)]
-        deal(nc.vector.tensor_copy, dealt[0][:, 0:C_WORDS].bitcast(I32), raw00[:])
+        dealt00 = placed("dealt00", [P, C_WORDS], I32, 10 * KIB)
+        deal(nc.vector.tensor_copy, dealt00[:], raw00[:])
         deal(nc.scalar.copy, dealt[0][:, C_WORDS:], raw01[:].bitcast(U32))
         v0 = keep.tile([P, S], U32, name="v0", align_bytes=64)
         nc.vector.tensor_copy(v0[:], table[0][:].bitcast(U32).indirect(idx[:]))
@@ -140,18 +160,6 @@ def tile_list_replay_td_errors_kernel(
 
         def bank(name, n):
             return psum.tile([P, BANK], F32, name=name, offset=n * BANK_BYTES)
-
-        warm = bank("warm", 7)
-        for n in range(4):
-            nc.tensor.matmul_mx(
-                out=warm[:],
-                lhsT=dealt[0][:, 0:T_WORDS].bitcast(U8).bitcast(FP4X4),
-                lhsT_scale=ts_win[:].bitcast(U8)[:, 0:P],
-                rhs=v0[:, 0:BANK].bitcast(FP8X4),
-                rhs_scale=ts_win[:].bitcast(U8)[:, 0:BANK],
-                start=True,
-                stop=True,
-            )
 
         hs = [keep.tile([P, 2 * S], F32, name="h%d" % i, tag="h%d" % i, align_bytes=64) for i in range(4 * GROUPS)]
 
@@ -164,7 +172,7 @@ def tile_list_replay_td_errors_kernel(
             w0 = C_WORDS * a + T_WORDS * t
             nc.tensor.matmul_mx(
                 out=acc[:, 0 : j1 - j0],
-                lhsT=dealt[c][:, w0 : w0 + T_WORDS].bitcast(U8).bitcast(FP4X4),
+                lhsT=(dealt00 if (c, a) == (0, 0) else dealt[c])[:, w0 : w0 + T_WORDS].bitcast(U8).bitcast(FP4X4),
                 lhsT_scale=w1_plane.bitcast(U8),
                 rhs=v_words[a][:, j0:j1].bitcast(FP8X4),
                 rhs_scale=planes[a][:, 0:V_WORDS].bitcast(U8)[:, j0:j1],

@@ -75,13 +75,8 @@ def tile_list_replay_td_errors_kernel(
         nc.sync.dma_start(p2[:], pos2)
         nc.sync.dma_start(p1[:], pos1)
 
-        blank = keep.tile([P, 4 * BANK], BF16, name="blank", align_bytes=64)
-        nc.vector.memset(blank[:].bitcast(I32), 0)
         nc.gpsimd.memset(ts_win[32:64, :], 0)
         nc.gpsimd.memset(ts_win[64:P, :], 0)
-        blank_scales = keep.tile([P, BANK], U8, name="blank_scales", align_bytes=64)
-        blank_moving = keep.tile([P, BANK], U32, name="blank_moving", align_bytes=64)
-        nc.vector.quantize_mx(out=blank_moving[:].bitcast(FP8X4), scales=blank_scales[:], in_=blank[:])
         planes = [keep.tile([P, V_WORDS + G_WORDS], I32, name="plane%d" % a, align_bytes=64) for a in range(PASSES)]
         planes_rest = keep.tile([P, PASSES, LAST * G_WORDS], I32, name="planes_rest", align_bytes=64)
         for a in range(PASSES):
@@ -131,20 +126,6 @@ def tile_list_replay_td_errors_kernel(
             copy(
                 out=dst.rearrange("p (a t b w) -> p a t b w", t=4, b=16, w=4),
                 in_=src.rearrange("p a (b t w) -> p a t b w", t=4, w=4),
-            )
-
-        blank_still = placed("blank_still", [P, P], I32, 4 * KIB)
-        nc.vector.tensor_copy(out=blank_still[:], in_=blank_moving[:, 0:P].bitcast(I32))
-        warm = psum.tile([P, BANK], F32, name="warm", offset=7 * BANK_BYTES)
-        for n in range(4):
-            nc.tensor.matmul_mx(
-                out=warm[:],
-                lhsT=blank_still[:].bitcast(FP8X4),
-                lhsT_scale=blank_scales[:, 0:P],
-                rhs=blank_moving[:].bitcast(FP8X4),
-                rhs_scale=blank_scales[:],
-                start=True,
-                stop=True,
             )
 
         dealt = [dealt_tile(0)]

@@ -102,17 +102,17 @@ def tile_list_replay_td_errors_kernel(
 
         raw = [None]
         for c in range(1, GROUPS):
-            raw.append(placed("raw%d" % c, [P, PASSES, C_WORDS], I32, 8 * KIB * (c - 1)))
+            raw.append(placed("raw%d" % c, [P, PASSES, C_WORDS], I32, 15 * KIB * (c - 1)))
             nc.sync.dma_start(out=raw[c][:], in_=w1w_hbm[:, :, C_WORDS * c : C_WORDS * (c + 1)])
-        rows_rest = placed("rows_rest", [P, LAST * G_WORDS], I32, 15 * KIB)
+        rows_rest = placed("rows_rest", [P, LAST * G_WORDS], I32, 12 * KIB)
         deal_scales(rows_rest[0:32, :], w1s_raw[0:32, G_WORDS:])
         nc.vector.tensor_copy(out=planes_rest[0:4, 0, :], in_=rows_rest[0:4, :])
         for n in range(1, 4 * PASSES):
             a, quad = divmod(n, 4)
             nc.sync.dma_start(out=planes_rest[32 * quad : 32 * quad + 4, a, :], in_=rows_rest[4 * n : 4 * n + 4, :])
-        w2_raw = []
-        for c in range(GROUPS):
-            w2_raw.append(placed("w2_raw%d" % c, [P, 4, N], F32, (20, 30, 16)[c] * KIB))
+        w2_raw = {}
+        for c in (LAST, 0, 1):
+            w2_raw[c] = (placed("w2_raw%d" % c, [P, 4, N], F32, (20, 30, 8)[c] * KIB))
             w2_rows = w2[512 * c : 512 * (c + 1), :].rearrange("(b t u) n -> t b u n", t=4, u=8)
             for t in range(4):
                 nc.sync.dma_start(out=w2_raw[c][:, t, :], in_=w2_rows[t])
@@ -120,7 +120,7 @@ def tile_list_replay_td_errors_kernel(
         nc.sync.dma_start(out=rew_sb[:], in_=rew.rearrange("(m p) j -> p m j", p=P))
 
         def dealt_tile(c):
-            return keep.tile([P, PASSES * C_WORDS], U32, name="dealt%d" % c, tag="dealt", align_bytes=64)
+            return placed("dealt%d" % c, [P, PASSES * C_WORDS], U32, 44 * KIB)
 
         def deal(copy, dst, src):
             copy(
@@ -129,7 +129,7 @@ def tile_list_replay_td_errors_kernel(
             )
 
         dealt = [dealt_tile(0)]
-        dealt00 = placed("dealt00", [P, C_WORDS], I32, 10 * KIB)
+        dealt00 = placed("dealt00", [P, C_WORDS], I32, 13 * KIB)
         deal(nc.vector.tensor_copy, dealt00[:], raw00[:])
         deal(nc.scalar.copy, dealt[0][:, C_WORDS:], raw01[:].bitcast(U32))
         v0 = keep.tile([P, S], U32, name="v0", align_bytes=64)
@@ -189,15 +189,18 @@ def tile_list_replay_td_errors_kernel(
 
         def hidden_tile(i):
             for half in (1,) if i == 1 else (1, 0):
-                hidden_half(i, half, (2, 0, 1, 3)[(2 * i - 1 - half) % 4] if i > 1 else 0)
+                if i < 4:
+                    hidden_half(i, half, (2, 0, 1, 3)[(2 * i - 1 - half) % 4] if i > 1 else 0)
+                else:
+                    hidden_half(i, half, (2 * i + 5 - half) % 8)
 
         w2_codes = {}
         w2_scales = keep.tile([P, GROUPS * N], U8, name="w2_scales", align_bytes=64)
         z_codes = {}
         z_scales = keep.tile([P, GROUPS * PAIRS], U8, name="z_scales", align_bytes=64)
         succ = [keep.tile([P, 4, PAIRS], F32, name="succ", bufs=2) for c in range(GROUPS)]
-        w2_bf = keep.tile([P, GROUPS, N, 4], BF16, name="w2_bf", align_bytes=64)
-        z_bf = keep.tile([P, GROUPS * PAIRS, 4], BF16, name="z_bf", align_bytes=64)
+        w2_bf = {}
+        z_bf = {}
         z = {}
 
         def pick_succ(i):
@@ -218,9 +221,9 @@ def tile_list_replay_td_errors_kernel(
 
         def round_z(c, j0, j1, on_vector):
             first = HALF if (c, j0 // HALF) == (LAST, 1) else 0
-            dst, src = interleaved(
-                z_bf[:, PAIRS * c + j0 : PAIRS * c + j1, :], z[c, first][:, :, j0 - first : j1 - first]
-            )
+            if c not in z_bf:
+                z_bf[c] = placed("z_bf%d" % c, [P, PAIRS, 4], BF16, (16, 41, 49)[c] * KIB)
+            dst, src = interleaved(z_bf[c][:, j0:j1, :], z[c, first][:, :, j0 - first : j1 - first])
             if on_vector:
                 nc.vector.tensor_copy(out=dst, in_=src)
             else:
@@ -232,13 +235,15 @@ def tile_list_replay_td_errors_kernel(
             nc.vector.quantize_mx(
                 out=codes[:].bitcast(FP8X4),
                 scales=z_scales[:, x0:x1],
-                in_=z_bf[:, x0:x1, :].rearrange("p j t -> p (j t)"),
+                in_=z_bf[c][:, x0 - PAIRS * c : x1 - PAIRS * c, :].rearrange("p j t -> p (j t)"),
             )
             for n, half in enumerate(halves):
                 z_codes[c, half] = codes[:, HALF * n : HALF * (n + 1)]
 
         def round_w2(c):
-            dst, src = interleaved(w2_bf[:, c, :, :], w2_raw[c][:])
+            if c // 2 not in w2_bf:
+                w2_bf[c // 2] = placed("w2_bf%d" % c, [P, 2 - c // 2, N, 4], BF16, (45, 53)[c // 2] * KIB)
+            dst, src = interleaved(w2_bf[c // 2][:, c % 2, :, :], w2_raw[c][:])
             nc.scalar.activation(out=dst, in_=src, func=ACT.Copy)
 
         def quantize_w2(c0, c1, tag):
@@ -246,7 +251,7 @@ def tile_list_replay_td_errors_kernel(
             nc.vector.quantize_mx(
                 out=codes[:].bitcast(FP8X4),
                 scales=w2_scales[:, N * c0 : N * c1],
-                in_=w2_bf[:, c0:c1, :, :].rearrange("p c n t -> p (c n t)"),
+                in_=w2_bf[c0 // 2][:].rearrange("p c n t -> p (c n t)"),
             )
             for c in range(c0, c1):
                 w2_codes[c] = codes[:, N * (c - c0) : N * (c - c0 + 1)]
@@ -264,16 +269,18 @@ def tile_list_replay_td_errors_kernel(
                 deal(nc.scalar.copy, dealt[c + 1][:], raw[c + 1][:].bitcast(U32))
             if c == 1:
                 round_z(0, 0, PAIRS, False)
-                quantize_z(0, (0, 1), 40 * KIB)
+                quantize_z(0, (0, 1), 36 * KIB)
+            elif c == 0:
+                round_w2(LAST)
             else:
-                round_w2(c // 2)
+                round_w2(0)
+                round_w2(1)
             if c < LAST:
                 z[c, 0] = placed("z%d" % c, [P, 4, PAIRS], F32, z_offsets[c])
                 for t in range(4):
                     pick_state(4 * c + t, 0, PAIRS)
         round_z(1, 0, PAIRS, False)
-        quantize_z(1, (0,), 37 * KIB)
-        round_w2(LAST)
+        quantize_z(1, (0,), 38 * KIB)
         for half in range(2):
             z[LAST, HALF * half] = placed("z%d_%d" % (LAST, half), [P, 4, HALF], F32, z_offsets[LAST] + 4 * KIB * half)
             for t in range(4):
@@ -284,9 +291,9 @@ def tile_list_replay_td_errors_kernel(
         round_z(LAST, 0, HALF, False)
         round_z(LAST, HALF, 416, False)
         round_z(LAST, 416, PAIRS, True)
-        quantize_z(LAST, (0,), 38 * KIB)
+        quantize_z(LAST, (0,), 39 * KIB)
         quantize_z(1, (1,), z_offsets[LAST])
-        quantize_z(LAST, (1,), 39 * KIB)
+        quantize_z(LAST, (1,), 40 * KIB)
 
         out_v = out.rearrange("(m p) j -> p m j", p=P)
         for half in range(2):

@@ -70,6 +70,7 @@ def tile_list_replay_td_errors_kernel(
         for a in range(PASSES):
             table.append(placed("table%d" % a, [P, T], I32, 16 * KIB * a))
             nc.sync.dma_start(out=table[a][:], in_=tab_words[a].rearrange("p t i -> p (t i)").bitcast(I32))
+        raw = [None]
         raw01 = keep.tile([P, 1, C_WORDS], I32, name="raw01", align_bytes=64)
         nc.sync.dma_start(out=raw01[:], in_=w1w_hbm[:, 1:2, 0:C_WORDS])
         nc.sync.dma_start(p2[:], pos2)
@@ -100,7 +101,25 @@ def tile_list_replay_td_errors_kernel(
             queue = nc.scalar if n <= 4 else nc.gpsimd
             queue.dma_start(out=planes[a][32 * quad : 32 * quad + 4, :], in_=rows[4 * n : 4 * n + 4, :])
 
-        raw = [None]
+        zeros = keep.tile([P, 4 * BANK], BF16, name="zeros", align_bytes=64)
+        nc.vector.memset(zeros[:].bitcast(I32), 0)
+        idle_codes = keep.tile([P, BANK], U32, name="idle_codes", align_bytes=64)
+        idle_scales = keep.tile([P, BANK], U8, name="idle_scales", align_bytes=64)
+        nc.vector.quantize_mx(out=idle_codes[:].bitcast(FP8X4), scales=idle_scales[:], in_=zeros[:])
+        idle_still = placed("idle_still", [P, P], I32, 13 * KIB)
+        nc.vector.tensor_copy(out=idle_still[:], in_=idle_codes[:, 0:P].bitcast(I32))
+        idle_bank = psum.tile([P, BANK], F32, name="idle_bank", offset=7 * BANK_BYTES)
+        for n in range(4):
+            nc.tensor.matmul_mx(
+                out=idle_bank[:],
+                lhsT=idle_still[:].bitcast(FP8X4),
+                lhsT_scale=idle_scales[:, 0:P],
+                rhs=idle_codes[:].bitcast(FP8X4),
+                rhs_scale=idle_scales[:],
+                start=True,
+                stop=True,
+            )
+
         for c in range(1, GROUPS):
             raw.append(placed("raw%d" % c, [P, PASSES, C_WORDS], I32, 15 * KIB * (c - 1)))
             nc.sync.dma_start(out=raw[c][:], in_=w1w_hbm[:, :, C_WORDS * c : C_WORDS * (c + 1)])
@@ -129,7 +148,7 @@ def tile_list_replay_td_errors_kernel(
             )
 
         dealt = [dealt_tile(0)]
-        dealt00 = placed("dealt00", [P, C_WORDS], I32, 13 * KIB)
+        dealt00 = placed("dealt00", [P, C_WORDS], I32, 14 * KIB)
         deal(nc.vector.tensor_copy, dealt00[:], raw00[:])
         deal(nc.scalar.copy, dealt[0][:, C_WORDS:], raw01[:].bitcast(U32))
         v0 = keep.tile([P, S], U32, name="v0", align_bytes=64)
@@ -173,24 +192,32 @@ def tile_list_replay_td_errors_kernel(
         def first_tile():
             parts = ((0, 512), (512, 768), (768, 896), (896, 1024))
             accs = [bank("acc0_%d" % n, (0, 1, 3, 4)[n]) for n in range(4)]
-            for n, a in ((0, 0), (0, 1), (1, 0), (2, 0), (3, 0), (1, 1)):
-                hidden_pass(accs[n], 0, a, *parts[n], a == 0, a == 1)
-                if a == 1:
-                    relu(accs[n], 0, *parts[n])
-            early = half_passes(1, 0, 2)
+            early = bank("acc1_0", 2)
+            late = bank("acc1_1", 5)
+            for n in range(4):
+                hidden_pass(accs[n], 0, 0, *parts[n], True, False)
+            hidden_pass(early, 1, 0, 0, BANK, True, False)
+            hidden_pass(accs[0], 0, 1, *parts[0], False, True)
+            relu(accs[0], 0, *parts[0])
+            hidden_pass(early, 1, 1, 0, BANK, False, True)
+            nc.vector.tensor_scalar_max(hs[1][:, 0:BANK], early[:], 0.0)
+            hidden_pass(accs[1], 0, 1, *parts[1], False, True)
+            relu(accs[1], 0, *parts[1])
+            hidden_pass(late, 1, 0, BANK, S, True, False)
             for n in (2, 3):
                 hidden_pass(accs[n], 0, 1, *parts[n], False, True)
             relu(accs[2], 0, *parts[2])
             nc.vector.tensor_scalar_max(hs[0][:, 896:1024], accs[3][:, 0:P], 0.0)
-            relu(early, 1, 0, BANK)
+            hidden_pass(late, 1, 1, BANK, S, False, True)
+            relu(late, 1, BANK, S)
 
         def hidden_half(i, half, n):
             relu(half_passes(i, half, n), i, BANK * half, BANK * (half + 1))
 
         def hidden_tile(i):
-            for half in (1,) if i == 1 else (1, 0):
+            for half in () if i == 1 else (1, 0):
                 if i < 4:
-                    hidden_half(i, half, (2, 0, 1, 3)[(2 * i - 1 - half) % 4] if i > 1 else 0)
+                    hidden_half(i, half, 2 * i - 3 - half)
                 else:
                     hidden_half(i, half, (2 * i + 5 - half) % 8)
 

@@ -131,11 +131,11 @@ def tile_list_replay_td_errors_kernel(
             nc.sync.dma_start(out=planes_rest[32 * quad : 32 * quad + 4, a, :], in_=rows_rest[4 * n : 4 * n + 4, :])
         w2_raw = {}
         for c in (LAST, 0, 1):
-            w2_raw[c] = (placed("w2_raw%d" % c, [P, 4, N], F32, (20, 30, 8)[c] * KIB))
+            w2_raw[c] = (placed("w2_raw%d" % c, [P, 4, N], F32, (20, 24, 8)[c] * KIB))
             w2_rows = w2[512 * c : 512 * (c + 1), :].rearrange("(b t u) n -> t b u n", t=4, u=8)
             for t in range(4):
                 nc.sync.dma_start(out=w2_raw[c][:, t, :], in_=w2_rows[t])
-        rew_sb = placed("rew_sb", [P, 2, PAIRS], F32, 24 * KIB)
+        rew_sb = placed("rew_sb", [P, 2, PAIRS], F32, 31 * KIB)
         nc.sync.dma_start(out=rew_sb[:], in_=rew.rearrange("(m p) j -> p m j", p=P))
 
         def dealt_tile(c):
@@ -242,27 +242,35 @@ def tile_list_replay_td_errors_kernel(
 
         def pick_state(i, j0, j1):
             c, t = divmod(i, 4)
+            first = HALF if (c, j0 // HALF) == (LAST, 1) else 0
             nc.vector.tensor_tensor(
-                z[c, j0][:, t, :], hs[i][:].indirect(p1[:, j0 // 16 : j1 // 16]), succ[c][:, t, j0:j1], ALU.add
+                z[c, first][:, t, j0 - first : j1 - first],
+                hs[i][:].indirect(p1[:, j0 // 16 : j1 // 16]),
+                succ[c][:, t, j0:j1],
+                ALU.add,
             )
 
-        def round_z(c, j0, j1, on_vector):
+        def round_z(c, j0, j1, t0=0, t1=4):
             first = HALF if (c, j0 // HALF) == (LAST, 1) else 0
-            if c not in z_bf:
-                z_bf[c] = placed("z_bf%d" % c, [P, PAIRS, 4], BF16, (16, 41, 49)[c] * KIB)
-            dst, src = interleaved(z_bf[c][:, j0:j1, :], z[c, first][:, :, j0 - first : j1 - first])
-            if on_vector:
-                nc.vector.tensor_copy(out=dst, in_=src)
+            if (c, first) not in z_bf:
+                width = HALF if c == LAST else PAIRS
+                z_bf[c, first] = placed("z_bf%d_%d" % (c, first), [P, width, 4], BF16, (16, 41, 49)[c] * KIB + 8 * first)
+            js = slice(j0 - first, j1 - first)
+            dst, src = z_bf[c, first][:, js, t0:t1], z[c, first][:, t0:t1, js]
+            if t1 - t0 == 4:
+                dst, src = interleaved(dst, src)
             else:
-                nc.scalar.activation(out=dst, in_=src, func=ACT.Copy)
+                src = src.rearrange("p t j -> p j t")
+            nc.scalar.activation(out=dst, in_=src, func=ACT.Copy)
 
         def quantize_z(c, halves, offset):
             x0, x1 = PAIRS * c + HALF * halves[0], PAIRS * c + HALF * (halves[-1] + 1)
+            first = HALF if (c, halves[0]) == (LAST, 1) else 0
             codes = placed("z_codes%d_%d" % (c, halves[0]), [P, x1 - x0], U32, offset)
             nc.vector.quantize_mx(
                 out=codes[:].bitcast(FP8X4),
                 scales=z_scales[:, x0:x1],
-                in_=z_bf[c][:, x0 - PAIRS * c : x1 - PAIRS * c, :].rearrange("p j t -> p (j t)"),
+                in_=z_bf[c, first][:, x0 - PAIRS * c - first : x1 - PAIRS * c - first, :].rearrange("p j t -> p (j t)"),
             )
             for n, half in enumerate(halves):
                 z_codes[c, half] = codes[:, HALF * n : HALF * (n + 1)]
@@ -283,7 +291,7 @@ def tile_list_replay_td_errors_kernel(
             for c in range(c0, c1):
                 w2_codes[c] = codes[:, N * (c - c0) : N * (c - c0 + 1)]
 
-        z_offsets = (0, 8 * KIB, 28 * KIB)
+        z_offsets = (0, 8 * KIB, 21 * KIB)
         for c in range(GROUPS):
             for t in range(4):
                 if c == 0 and t == 0:
@@ -295,8 +303,7 @@ def tile_list_replay_td_errors_kernel(
                 dealt.append(dealt_tile(c + 1))
                 deal(nc.scalar.copy, dealt[c + 1][:], raw[c + 1][:].bitcast(U32))
             if c == 1:
-                round_z(0, 0, PAIRS, False)
-                quantize_z(0, (0, 1), 36 * KIB)
+                round_z(0, 0, PAIRS)
             elif c == 0:
                 round_w2(LAST)
             else:
@@ -306,25 +313,31 @@ def tile_list_replay_td_errors_kernel(
                 z[c, 0] = placed("z%d" % c, [P, 4, PAIRS], F32, z_offsets[c])
                 for t in range(4):
                     pick_state(4 * c + t, 0, PAIRS)
-        round_z(1, 0, PAIRS, False)
-        quantize_z(1, (0,), 38 * KIB)
+        round_z(1, 0, PAIRS)
+        quantize_w2(0, LAST, "w2_first")
+        between = {1: (0, 0, 25 * KIB), 2: (0, 1, 26 * KIB), 3: (1, 0, 38 * KIB)}
         for half in range(2):
-            z[LAST, HALF * half] = placed("z%d_%d" % (LAST, half), [P, 4, HALF], F32, z_offsets[LAST] + 4 * KIB * half)
+            z[LAST, HALF * half] = placed("z%d_%d" % (LAST, half), [P, 4, HALF], F32, z_offsets[LAST] + 6 * KIB * half)
             for t in range(4):
-                if (half, t) == (1, 1):
-                    quantize_w2(0, LAST, "h%d" % (4 * LAST))
-                pick_state(4 * LAST + t, HALF * half, HALF * (half + 1))
+                if half == 1 and t in between:
+                    quantize_z(between[t][0], (between[t][1],), between[t][2])
+                if (half, t) == (1, 3):
+                    pick_state(4 * LAST + t, HALF, HALF + P)
+                    pick_state(4 * LAST + t, HALF + P, PAIRS)
+                else:
+                    pick_state(4 * LAST + t, HALF * half, HALF * (half + 1))
         quantize_w2(LAST, GROUPS, "h%d" % (4 * LAST + 2))
-        round_z(LAST, 0, HALF, False)
-        round_z(LAST, HALF, 416, False)
-        round_z(LAST, 416, PAIRS, True)
+        round_z(LAST, 0, HALF)
+        round_z(LAST, HALF, PAIRS, 0, 2)
+        round_z(LAST, HALF, HALF + P, 2, 4)
+        round_z(LAST, HALF + P, PAIRS, 2, 4)
         quantize_z(LAST, (0,), 39 * KIB)
         quantize_z(1, (1,), z_offsets[LAST])
         quantize_z(LAST, (1,), 40 * KIB)
 
         out_v = out.rearrange("(m p) j -> p m j", p=P)
         for half in range(2):
-            err = ring.tile([P, 2, HALF], F32, name="err")
+            err = placed("err%d" % half, [P, 2, HALF], F32, (27 + 2 * half) * KIB)
             res = ring.tile([P, 2, HALF], F32, name="res")
             d = [bank("d%d_%d" % (half, m), 4 + 2 * half + m) for m in range(2)]
             for c in range(GROUPS):

@@ -106,8 +106,8 @@ def tile_list_replay_td_errors_kernel(
         idle_codes = keep.tile([P, BANK], U32, name="idle_codes", align_bytes=64)
         idle_scales = keep.tile([P, BANK], U8, name="idle_scales", align_bytes=64)
         nc.vector.quantize_mx(out=idle_codes[:].bitcast(FP8X4), scales=idle_scales[:], in_=zeros[:])
-        idle_still = placed("idle_still", [P, P], I32, 13 * KIB)
-        nc.vector.tensor_copy(out=idle_still[:], in_=idle_codes[:, 0:P].bitcast(I32))
+        idle_still = placed("idle_still", [P, P], U32, 32 * KIB)
+        nc.scalar.copy(out=idle_still[:], in_=idle_codes[:, 0:P])
         idle_bank = psum.tile([P, BANK], F32, name="idle_bank", offset=7 * BANK_BYTES)
         for n in range(4):
             nc.tensor.matmul_mx(
@@ -135,7 +135,7 @@ def tile_list_replay_td_errors_kernel(
             w2_rows = w2[512 * c : 512 * (c + 1), :].rearrange("(b t u) n -> t b u n", t=4, u=8)
             for t in range(4):
                 nc.sync.dma_start(out=w2_raw[c][:, t, :], in_=w2_rows[t])
-        rew_sb = placed("rew_sb", [P, 2, PAIRS], F32, 31 * KIB)
+        rew_sb = placed("rew_sb", [P, 2, PAIRS], F32, 31 * KIB + 512)
         nc.sync.dma_start(out=rew_sb[:], in_=rew.rearrange("(m p) j -> p m j", p=P))
 
         def dealt_tile(c):

@@ -27,7 +27,6 @@ DISCOUNT = 0.99
 KIB = 1024
 V_WORDS = S // 4
 G_WORDS = 512 // 4
-W_WORDS = GROUPS * G_WORDS
 C_WORDS = 512 // 2
 T_WORDS = C_WORDS // 4
 PIECES = ((0, 512), (512, 768), (768, 1024))
@@ -61,8 +60,9 @@ def tile_list_replay_td_errors_kernel(
         nc.sync.dma_start(idx[:], offs)
         ts_win = keep.tile([P, T // 4], I32, name="ts_win", align_bytes=64)
         nc.scalar.dma_start(out=ts_win[0:32, :], in_=tab_scales.rearrange("a q t -> (a q) t").bitcast(I32))
-        w1s_raw = keep.tile([P, W_WORDS], I32, name="w1s_raw", align_bytes=64)
-        nc.sync.dma_start(out=w1s_raw[0:32, :], in_=w1_scales.rearrange("a q c -> (a q) c").bitcast(I32))
+        w1s_hbm = w1_scales.rearrange("a q c -> (a q) c").bitcast(I32)
+        w1s_raw = keep.tile([P, G_WORDS], I32, name="w1s_raw", align_bytes=64)
+        nc.sync.dma_start(out=w1s_raw[0:32, :], in_=w1s_hbm[:, 0:G_WORDS])
         w1w_hbm = w1_words.rearrange("a p c -> p a c").bitcast(I32)
         raw00 = keep.tile([P, 1, C_WORDS], I32, name="raw00", align_bytes=64)
         nc.scalar.dma_start(out=raw00[:], in_=w1w_hbm[:, 0:1, 0:C_WORDS])
@@ -84,14 +84,14 @@ def tile_list_replay_td_errors_kernel(
             nc.gpsimd.memset(planes[a][:], 0)
         nc.gpsimd.memset(planes_rest[:], 0)
 
-        def deal_scales(dst, src):
-            nc.vector.tensor_copy(
+        def deal_scales(copy, dst, src):
+            copy(
                 out=dst.rearrange("p (c t b w) -> p c t b w", t=4, b=16, w=2),
                 in_=src.rearrange("p (c b t w) -> p c t b w", t=4, b=16, w=2),
             )
 
         rows = keep.tile([P, V_WORDS + G_WORDS], I32, name="rows", align_bytes=64)
-        deal_scales(rows[0:32, V_WORDS:], w1s_raw[0:32, 0:G_WORDS])
+        deal_scales(nc.vector.tensor_copy, rows[0:32, V_WORDS:], w1s_raw[0:32, :])
         ts_picked = placed("ts_picked", [P, S], U8, 32 * KIB)
         nc.vector.tensor_copy(ts_picked[:], ts_win[:].bitcast(U8).indirect(idx[:]))
         nc.vector.tensor_copy(out=rows[0:32, 0:V_WORDS], in_=ts_picked[0:32, :].bitcast(I32))
@@ -120,13 +120,14 @@ def tile_list_replay_td_errors_kernel(
                 stop=True,
             )
 
+        w1s_rest = placed("w1s_rest", [P, LAST * G_WORDS], I32, 13 * KIB)
+        nc.sync.dma_start(out=w1s_rest[0:32, :], in_=w1s_hbm[:, G_WORDS:])
         for c in range(1, GROUPS):
             raw.append(placed("raw%d" % c, [P, PASSES, C_WORDS], I32, 15 * KIB * (c - 1)))
             nc.sync.dma_start(out=raw[c][:], in_=w1w_hbm[:, :, C_WORDS * c : C_WORDS * (c + 1)])
         rows_rest = placed("rows_rest", [P, LAST * G_WORDS], I32, 12 * KIB)
-        deal_scales(rows_rest[0:32, :], w1s_raw[0:32, G_WORDS:])
-        nc.vector.tensor_copy(out=planes_rest[0:4, 0, :], in_=rows_rest[0:4, :])
-        for n in range(1, 4 * PASSES):
+        deal_scales(nc.gpsimd.tensor_copy, rows_rest[0:32, :], w1s_rest[0:32, :])
+        for n in range(4 * PASSES):
             a, quad = divmod(n, 4)
             nc.sync.dma_start(out=planes_rest[32 * quad : 32 * quad + 4, a, :], in_=rows_rest[4 * n : 4 * n + 4, :])
         w2_raw = {}

@@ -316,23 +316,24 @@ def tile_list_replay_td_errors_kernel(
                     pick_state(4 * c + t, 0, PAIRS)
         round_z(1, 0, PAIRS)
         quantize_w2(0, LAST, "w2_first")
-        between = {1: (0, 0, 25 * KIB), 2: (0, 1, 26 * KIB), 3: (1, 0, 38 * KIB)}
         for half in range(2):
             z[LAST, HALF * half] = placed("z%d_%d" % (LAST, half), [P, 4, HALF], F32, z_offsets[LAST] + 6 * KIB * half)
             for t in range(4):
-                if half == 1 and t in between:
-                    quantize_z(between[t][0], (between[t][1],), between[t][2])
+                if (half, t) == (1, 2):
+                    quantize_z(0, (0,), 25 * KIB)
+                    quantize_z(1, (0,), 38 * KIB)
                 if (half, t) == (1, 3):
                     pick_state(4 * LAST + t, HALF, HALF + P)
                     pick_state(4 * LAST + t, HALF + P, PAIRS)
                 else:
                     pick_state(4 * LAST + t, HALF * half, HALF * (half + 1))
-        quantize_w2(LAST, GROUPS, "h%d" % (4 * LAST + 2))
         round_z(LAST, 0, HALF)
         round_z(LAST, HALF, PAIRS, 0, 2)
         round_z(LAST, HALF, HALF + P, 2, 4)
         round_z(LAST, HALF + P, PAIRS, 2, 4)
         quantize_z(LAST, (0,), 39 * KIB)
+        quantize_w2(LAST, GROUPS, "h%d" % (4 * LAST + 3))
+        quantize_z(0, (1,), 26 * KIB)
         quantize_z(1, (1,), z_offsets[LAST])
         quantize_z(LAST, (1,), 40 * KIB)
 

@@ -315,12 +315,25 @@ def tile_list_replay_td_errors_kernel(
                 for t in range(4):
                     pick_state(4 * c + t, 0, PAIRS)
         round_z(1, 0, PAIRS)
-        quantize_w2(0, LAST, "w2_first")
         for half in range(2):
             z[LAST, HALF * half] = placed("z%d_%d" % (LAST, half), [P, 4, HALF], F32, z_offsets[LAST] + 6 * KIB * half)
             for t in range(4):
-                if (half, t) == (1, 2):
+                if (half, t) == (1, 0):
+                    quantize_w2(0, LAST, "w2_first")
+                if (half, t) == (1, 1):
                     quantize_z(0, (0,), 25 * KIB)
+                    idle_late = bank("idle_late", 0)
+                    for width in (HALF, HALF, P):
+                        nc.tensor.matmul_mx(
+                            out=idle_late[:, 0:width],
+                            lhsT=z_codes[0, 0][:, 0:P].bitcast(FP8X4),
+                            lhsT_scale=z_scales[:, 0:P],
+                            rhs=idle_codes[:, 0:width].bitcast(FP8X4),
+                            rhs_scale=idle_scales[:, 0:width],
+                            start=True,
+                            stop=True,
+                        )
+                if (half, t) == (1, 2):
                     quantize_z(1, (0,), 38 * KIB)
                 if (half, t) == (1, 3):
                     pick_state(4 * LAST + t, HALF, HALF + P)

@@ -322,17 +322,6 @@ def tile_list_replay_td_errors_kernel(
                     quantize_w2(0, LAST, "w2_first")
                 if (half, t) == (1, 1):
                     quantize_z(0, (0,), 25 * KIB)
-                    idle_late = bank("idle_late", 0)
-                    for width in (HALF, HALF, P):
-                        nc.tensor.matmul_mx(
-                            out=idle_late[:, 0:width],
-                            lhsT=z_codes[0, 0][:, 0:P].bitcast(FP8X4),
-                            lhsT_scale=z_scales[:, 0:P],
-                            rhs=idle_codes[:, 0:width].bitcast(FP8X4),
-                            rhs_scale=idle_scales[:, 0:width],
-                            start=True,
-                            stop=True,
-                        )
                 if (half, t) == (1, 2):
                     quantize_z(1, (0,), 38 * KIB)
                 if (half, t) == (1, 3):

from contextlib import ExitStack

import concourse.mybir as mybir

K, T, S, PAIRS, H, N = 1024, 4096, 1024, 512, 1536, 256
FLOPS = 2 * K * H * S + 2 * H * N * PAIRS

F32 = mybir.dt.float32
BF16 = mybir.dt.bfloat16
I32 = mybir.dt.int32
U32 = mybir.dt.uint32
U16 = mybir.dt.uint16
U8 = mybir.dt.uint8
FP8X4 = mybir.dt.float8_e4m3fn_x4
FP4X4 = mybir.dt.float4_e2m1fn_x4
ACT = mybir.ActivationFunctionType
ALU = mybir.AluOpType

P = 128
PASSES = K // 512
GROUPS = H // 512
LAST = GROUPS - 1
BANK = 512
BANK_BYTES = 2048
HALF = PAIRS // 2
DISCOUNT = 0.99
KIB = 1024
V_WORDS = S // 4
G_WORDS = 512 // 4
C_WORDS = 512 // 2
T_WORDS = C_WORDS // 4
PIECES = ((0, 512), (512, 768), (768, 1024))


def interleaved(dst, src):
    return (
        dst.rearrange("p (c i) t -> p c t i", i=2),
        src.rearrange("p t (c i) -> p c t i", i=2),
    )


def tile_list_replay_td_errors_kernel(
    tc, tab_words, tab_scales, offs, w1_words, w1_scales, pos1, pos2, w2, rew, out
):
    nc = tc.nc
    with ExitStack() as ctx:
        lists = ctx.enter_context(tc.tile_pool(name="lists", bufs=1))
        keep = ctx.enter_context(tc.tile_pool(name="keep", bufs=1))
        shared = ctx.enter_context(tc.tile_pool(name="shared", bufs=1))
        ring = ctx.enter_context(tc.tile_pool(name="ring", bufs=2))
        psum = ctx.enter_context(tc.psum_pool(name="psum", bufs=1))

        idx = lists.tile([P, S // 16], U16, name="idx")
        p1 = lists.tile([P, PAIRS // 16], U16, name="p1")
        p2 = lists.tile([P, PAIRS // 16], U16, name="p2")

        def placed(name, shape, dtype, offset):
            return shared.tile(shape, dtype, name=name, offset=offset, align_bytes=64)

        nc.sync.dma_start(idx[:], offs)
        ts_win = keep.tile([P, T // 4], I32, name="ts_win", align_bytes=64)
        nc.scalar.dma_start(out=ts_win[0:32, :], in_=tab_scales.rearrange("a q t -> (a q) t").bitcast(I32))
        w1s_hbm = w1_scales.rearrange("a q c -> (a q) c").bitcast(I32)
        w1s_raw = keep.tile([P, G_WORDS], I32, name="w1s_raw", align_bytes=64)
        nc.sync.dma_start(out=w1s_raw[0:32, :], in_=w1s_hbm[:, 0:G_WORDS])
        w1w_hbm = w1_words.rearrange("a p c -> p a c").bitcast(I32)
        raw00 = keep.tile([P, 1, C_WORDS], I32, name="raw00", align_bytes=64)
        nc.scalar.dma_start(out=raw00[:], in_=w1w_hbm[:, 0:1, 0:C_WORDS])
        table = []
        for a in range(PASSES):
            table.append(placed("table%d" % a, [P, T], I32, 16 * KIB * a))
            nc.sync.dma_start(out=table[a][:], in_=tab_words[a].rearrange("p t i -> p (t i)").bitcast(I32))
        raw = [None]
        raw01 = keep.tile([P, 1, C_WORDS], I32, name="raw01", align_bytes=64)
        nc.sync.dma_start(out=raw01[:], in_=w1w_hbm[:, 1:2, 0:C_WORDS])
        nc.sync.dma_start(p2[:], pos2)
        nc.sync.dma_start(p1[:], pos1)

        nc.gpsimd.memset(ts_win[32:64, :], 0)
        nc.gpsimd.memset(ts_win[64:P, :], 0)
        planes = [keep.tile([P, V_WORDS + G_WORDS], I32, name="plane%d" % a, align_bytes=64) for a in range(PASSES)]
        planes_rest = keep.tile([P, PASSES, LAST * G_WORDS], I32, name="planes_rest", align_bytes=64)
        for a in range(PASSES):
            nc.gpsimd.memset(planes[a][:], 0)
        nc.gpsimd.memset(planes_rest[:], 0)

        def deal_scales(copy, dst, src):
            copy(
                out=dst.rearrange("p (c t b w) -> p c t b w", t=4, b=16, w=2),
                in_=src.rearrange("p (c b t w) -> p c t b w", t=4, b=16, w=2),
            )

        rows = keep.tile([P, V_WORDS + G_WORDS], I32, name="rows", align_bytes=64)
        deal_scales(nc.vector.tensor_copy, rows[0:32, V_WORDS:], w1s_raw[0:32, :])
        ts_picked = placed("ts_picked", [P, S], U8, 32 * KIB)
        nc.vector.tensor_copy(ts_picked[:], ts_win[:].bitcast(U8).indirect(idx[:]))
        nc.vector.tensor_copy(out=rows[0:32, 0:V_WORDS], in_=ts_picked[0:32, :].bitcast(I32))
        nc.vector.tensor_copy(out=planes[0][0:4, :], in_=rows[0:4, :])
        for n in range(1, 4 * PASSES):
            a, quad = divmod(n, 4)
            queue = nc.scalar if n <= 4 else nc.gpsimd
            queue.dma_start(out=planes[a][32 * quad : 32 * quad + 4, :], in_=rows[4 * n : 4 * n + 4, :])

        zeros = keep.tile([P, 4 * BANK], BF16, name="zeros", align_bytes=64)
        nc.vector.memset(zeros[:].bitcast(I32), 0)
        idle_codes = keep.tile([P, BANK], U32, name="idle_codes", align_bytes=64)
        idle_scales = keep.tile([P, BANK], U8, name="idle_scales", align_bytes=64)
        nc.vector.quantize_mx(out=idle_codes[:].bitcast(FP8X4), scales=idle_scales[:], in_=zeros[:])
        idle_still = placed("idle_still", [P, P], U32, 32 * KIB)
        nc.scalar.copy(out=idle_still[:], in_=idle_codes[:, 0:P])
        idle_bank = psum.tile([P, BANK], F32, name="idle_bank", offset=7 * BANK_BYTES)
        for n in range(4):
            nc.tensor.matmul_mx(
                out=idle_bank[:],
                lhsT=idle_still[:].bitcast(FP8X4),
                lhsT_scale=idle_scales[:, 0:P],
                rhs=idle_codes[:].bitcast(FP8X4),
                rhs_scale=idle_scales[:],
                start=True,
                stop=True,
            )

        w1s_rest = placed("w1s_rest", [P, LAST * G_WORDS], I32, 13 * KIB)
        nc.sync.dma_start(out=w1s_rest[0:32, :], in_=w1s_hbm[:, G_WORDS:])
        for c in range(1, GROUPS):
            raw.append(placed("raw%d" % c, [P, PASSES, C_WORDS], I32, 15 * KIB * (c - 1)))
            nc.sync.dma_start(out=raw[c][:], in_=w1w_hbm[:, :, C_WORDS * c : C_WORDS * (c + 1)])
        rows_rest = placed("rows_rest", [P, LAST * G_WORDS], I32, 12 * KIB)
        deal_scales(nc.gpsimd.tensor_copy, rows_rest[0:32, :], w1s_rest[0:32, :])
        for n in range(4 * PASSES):
            a, quad = divmod(n, 4)
            nc.sync.dma_start(out=planes_rest[32 * quad : 32 * quad + 4, a, :], in_=rows_rest[4 * n : 4 * n + 4, :])
        w2_raw = {}
        for c in (LAST, 0, 1):
            w2_raw[c] = (placed("w2_raw%d" % c, [P, 4, N], F32, (20, 24, 8)[c] * KIB))
            w2_rows = w2[512 * c : 512 * (c + 1), :].rearrange("(b t u) n -> t b u n", t=4, u=8)
            for t in range(4):
                nc.sync.dma_start(out=w2_raw[c][:, t, :], in_=w2_rows[t])
        rew_sb = placed("rew_sb", [P, 2, PAIRS], F32, 31 * KIB + 512)
        nc.sync.dma_start(out=rew_sb[:], in_=rew.rearrange("(m p) j -> p m j", p=P))

        def dealt_tile(c):
            return placed("dealt%d" % c, [P, PASSES * C_WORDS], U32, 44 * KIB)

        def deal(copy, dst, src):
            copy(
                out=dst.rearrange("p (a t b w) -> p a t b w", t=4, b=16, w=4),
                in_=src.rearrange("p a (b t w) -> p a t b w", t=4, w=4),
            )

        dealt = [dealt_tile(0)]
        dealt00 = placed("dealt00", [P, C_WORDS], I32, 14 * KIB)
        deal(nc.vector.tensor_copy, dealt00[:], raw00[:])
        deal(nc.scalar.copy, dealt[0][:, C_WORDS:], raw01[:].bitcast(U32))
        v0 = keep.tile([P, S], U32, name="v0", align_bytes=64)
        nc.vector.tensor_copy(v0[:], table[0][:].bitcast(U32).indirect(idx[:]))
        v1 = keep.tile([P, S], U32, name="v1", align_bytes=64)
        for j0, j1 in PIECES:
            nc.vector.tensor_copy(v1[:, j0:j1], table[1][:].bitcast(U32).indirect(idx[:, j0 // 16 : j1 // 16]))
        v_words = [v0, v1]

        def bank(name, n):
            return psum.tile([P, BANK], F32, name=name, offset=n * BANK_BYTES)

        hs = [keep.tile([P, 2 * S], F32, name="h%d" % i, tag="h%d" % i, align_bytes=64) for i in range(4 * GROUPS)]

        def hidden_pass(acc, i, a, j0, j1, start, stop):
            c, t = divmod(i, 4)
            if c == 0:
                w1_plane = planes[a][:, V_WORDS + 32 * i : V_WORDS + 32 * (i + 1)]
            else:
                w1_plane = planes_rest[:, a, 32 * (i - 4) : 32 * (i - 3)]
            w0 = C_WORDS * a + T_WORDS * t
            nc.tensor.matmul_mx(
                out=acc[:, 0 : j1 - j0],
                lhsT=(dealt00 if (c, a) == (0, 0) else dealt[c])[:, w0 : w0 + T_WORDS].bitcast(U8).bitcast(FP4X4),
                lhsT_scale=w1_plane.bitcast(U8),
                rhs=v_words[a][:, j0:j1].bitcast(FP8X4),
                rhs_scale=planes[a][:, 0:V_WORDS].bitcast(U8)[:, j0:j1],
                start=start,
                stop=stop,
            )

        def relu(acc, i, j0, j1):
            nc.scalar.activation(out=hs[i][:, j0:j1], in_=acc[:, 0 : j1 - j0], func=ACT.Relu)

        def half_passes(i, half, n):
            acc = bank("acc%d_%d" % (i, half), n)
            for a in (1, 0):
                hidden_pass(acc, i, a, BANK * half, BANK * (half + 1), a == 1, a == 0)
            return acc

        def first_tile():
            parts = ((0, 512), (512, 768), (768, 896), (896, 1024))
            accs = [bank("acc0_%d" % n, (0, 1, 3, 4)[n]) for n in range(4)]
            early = bank("acc1_0", 2)
            late = bank("acc1_1", 5)
            for n in range(4):
                hidden_pass(accs[n], 0, 0, *parts[n], True, False)
            hidden_pass(early, 1, 0, 0, BANK, True, False)
            hidden_pass(accs[0], 0, 1, *parts[0], False, True)
            relu(accs[0], 0, *parts[0])
            hidden_pass(early, 1, 1, 0, BANK, False, True)
            nc.vector.tensor_scalar_max(hs[1][:, 0:BANK], early[:], 0.0)
            hidden_pass(accs[1], 0, 1, *parts[1], False, True)
            relu(accs[1], 0, *parts[1])
            hidden_pass(late, 1, 0, BANK, S, True, False)
            for n in (2, 3):
                hidden_pass(accs[n], 0, 1, *parts[n], False, True)
            relu(accs[2], 0, *parts[2])
            nc.vector.tensor_scalar_max(hs[0][:, 896:1024], accs[3][:, 0:P], 0.0)
            hidden_pass(late, 1, 1, BANK, S, False, True)
            relu(late, 1, BANK, S)

        def hidden_half(i, half, n):
            relu(half_passes(i, half, n), i, BANK * half, BANK * (half + 1))

        def hidden_tile(i):
            for half in () if i == 1 else (1, 0):
                if i < 4:
                    hidden_half(i, half, 2 * i - 3 - half)
                else:
                    hidden_half(i, half, (2 * i + 5 - half) % 8)

        w2_codes = {}
        w2_scales = keep.tile([P, GROUPS * N], U8, name="w2_scales", align_bytes=64)
        z_codes = {}
        z_scales = keep.tile([P, GROUPS * PAIRS], U8, name="z_scales", align_bytes=64)
        succ = [keep.tile([P, 4, PAIRS], F32, name="succ", bufs=2) for c in range(GROUPS)]
        w2_bf = {}
        z_bf = {}
        z = {}

        def pick_succ(i):
            nc.vector.tensor_scalar(
                out=succ[i // 4][:, i % 4, :],
                in0=hs[i][:].indirect(p2[:]),
                scalar1=-DISCOUNT,
                scalar2=0.0,
                op0=ALU.mult,
                op1=ALU.add,
            )

        def pick_state(i, j0, j1):
            c, t = divmod(i, 4)
            first = HALF if (c, j0 // HALF) == (LAST, 1) else 0
            nc.vector.tensor_tensor(
                z[c, first][:, t, j0 - first : j1 - first],
                hs[i][:].indirect(p1[:, j0 // 16 : j1 // 16]),
                succ[c][:, t, j0:j1],
                ALU.add,
            )

        def round_z(c, j0, j1, t0=0, t1=4):
            first = HALF if (c, j0 // HALF) == (LAST, 1) else 0
            if (c, first) not in z_bf:
                width = HALF if c == LAST else PAIRS
                z_bf[c, first] = placed("z_bf%d_%d" % (c, first), [P, width, 4], BF16, (16, 41, 49)[c] * KIB + 8 * first)
            js = slice(j0 - first, j1 - first)
            dst, src = z_bf[c, first][:, js, t0:t1], z[c, first][:, t0:t1, js]
            if t1 - t0 == 4:
                dst, src = interleaved(dst, src)
            else:
                src = src.rearrange("p t j -> p j t")
            nc.scalar.activation(out=dst, in_=src, func=ACT.Copy)

        def quantize_z(c, halves, offset):
            x0, x1 = PAIRS * c + HALF * halves[0], PAIRS * c + HALF * (halves[-1] + 1)
            first = HALF if (c, halves[0]) == (LAST, 1) else 0
            codes = placed("z_codes%d_%d" % (c, halves[0]), [P, x1 - x0], U32, offset)
            nc.vector.quantize_mx(
                out=codes[:].bitcast(FP8X4),
                scales=z_scales[:, x0:x1],
                in_=z_bf[c, first][:, x0 - PAIRS * c - first : x1 - PAIRS * c - first, :].rearrange("p j t -> p (j t)"),
            )
            for n, half in enumerate(halves):
                z_codes[c, half] = codes[:, HALF * n : HALF * (n + 1)]

        def round_w2(c):
            if c // 2 not in w2_bf:
                w2_bf[c // 2] = placed("w2_bf%d" % c, [P, 2 - c // 2, N, 4], BF16, (45, 53)[c // 2] * KIB)
            dst, src = interleaved(w2_bf[c // 2][:, c % 2, :, :], w2_raw[c][:])
            nc.scalar.activation(out=dst, in_=src, func=ACT.Copy)

        def quantize_w2(c0, c1, tag):
            codes = keep.tile([P, (c1 - c0) * N], U32, name="w2_codes", tag=tag, align_bytes=64)
            nc.vector.quantize_mx(
                out=codes[:].bitcast(FP8X4),
                scales=w2_scales[:, N * c0 : N * c1],
                in_=w2_bf[c0 // 2][:].rearrange("p c n t -> p (c n t)"),
            )
            for c in range(c0, c1):
                w2_codes[c] = codes[:, N * (c - c0) : N * (c - c0 + 1)]

        z_offsets = (0, 8 * KIB, 21 * KIB)
        for c in range(GROUPS):
            for t in range(4):
                if c == 0 and t == 0:
                    first_tile()
                else:
                    hidden_tile(4 * c + t)
                pick_succ(4 * c + t)
            if c < LAST:
                dealt.append(dealt_tile(c + 1))
                deal(nc.scalar.copy, dealt[c + 1][:], raw[c + 1][:].bitcast(U32))
            if c == 1:
                round_z(0, 0, PAIRS)
            elif c == 0:
                round_w2(LAST)
            else:
                round_w2(0)
                round_w2(1)
            if c < LAST:
                z[c, 0] = placed("z%d" % c, [P, 4, PAIRS], F32, z_offsets[c])
                for t in range(4):
                    pick_state(4 * c + t, 0, PAIRS)
        round_z(1, 0, PAIRS)
        for half in range(2):
            z[LAST, HALF * half] = placed("z%d_%d" % (LAST, half), [P, 4, HALF], F32, z_offsets[LAST] + 6 * KIB * half)
            for t in range(4):
                if (half, t) == (1, 0):
                    quantize_w2(0, LAST, "w2_first")
                if (half, t) == (1, 1):
                    quantize_z(0, (0,), 25 * KIB)
                if (half, t) == (1, 2):
                    quantize_z(1, (0,), 38 * KIB)
                if (half, t) == (1, 3):
                    pick_state(4 * LAST + t, HALF, HALF + P)
                    pick_state(4 * LAST + t, HALF + P, PAIRS)
                else:
                    pick_state(4 * LAST + t, HALF * half, HALF * (half + 1))
        round_z(LAST, 0, HALF)
        round_z(LAST, HALF, PAIRS, 0, 2)
        round_z(LAST, HALF, HALF + P, 2, 4)
        round_z(LAST, HALF + P, PAIRS, 2, 4)
        quantize_z(LAST, (0,), 39 * KIB)
        quantize_w2(LAST, GROUPS, "h%d" % (4 * LAST + 3))
        quantize_z(0, (1,), 26 * KIB)
        quantize_z(1, (1,), z_offsets[LAST])
        quantize_z(LAST, (1,), 40 * KIB)

        out_v = out.rearrange("(m p) j -> p m j", p=P)
        for half in range(2):
            err = placed("err%d" % half, [P, 2, HALF], F32, (27 + 2 * half) * KIB)
            res = ring.tile([P, 2, HALF], F32, name="res")
            d = [bank("d%d_%d" % (half, m), 4 + 2 * half + m) for m in range(2)]
            for c in range(GROUPS):
                pairs = slice(PAIRS * c + HALF * half, PAIRS * c + HALF * (half + 1))
                for m in range(2):
                    heads = slice(N * c + P * m, N * c + P * (m + 1))
                    nc.tensor.matmul_mx(
                        out=d[m][:, 0:HALF],
                        lhsT=w2_codes[c][:, P * m : P * (m + 1)].bitcast(FP8X4),
                        lhsT_scale=w2_scales[:, heads],
                        rhs=z_codes[c, half].bitcast(FP8X4),
                        rhs_scale=z_scales[:, pairs],
                        start=(c == 0),
                        stop=(c == LAST),
                    )
            for m in range(2):
                last = (half, m) == (1, 1)
                for j0, j1 in ((0, P), (P, HALF)) if last else ((0, HALF),):
                    js = slice(HALF * half + j0, HALF * half + j1)
                    nc.vector.tensor_tensor(
                        out=err[:, m, j0:j1], in0=rew_sb[:, m, js], in1=d[m][:, j0:j1], op=ALU.subtract
                    )
                    nc.scalar.activation(out=res[:, m, j0:j1], in_=err[:, m, j0:j1], func=ACT.Tanh)
                    queue = nc.scalar if last and j1 == HALF else nc.sync
                    queue.dma_start(out=out_v[:, m, js], in_=res[:, m, j0:j1])
